import numpy as np
import ml_dtypes


def mxq(x, axis, fmt="e4m3"):
    dtype, down = {"e4m3": (ml_dtypes.float8_e4m3fn, 7), "e5m2": (ml_dtypes.float8_e5m2, 14)}[fmt]
    v = np.moveaxis(np.asarray(x, np.float32).astype(ml_dtypes.bfloat16).astype(np.float64), axis, -1)
    blocks = v.reshape(v.shape[:-1] + (-1, 32))
    amax = np.abs(blocks).max(-1, keepdims=True)
    byte = np.maximum(np.where(amax > 0, np.frexp(amax)[1] - 1 + 127, 0) - down, 1)
    scale = np.exp2(byte - 127.0)
    codes = (blocks / scale).astype(np.float32).astype(dtype).astype(np.float64)
    return np.moveaxis((codes * scale).reshape(v.shape), -1, axis)


WIDE = False


def mx_kscale(k):
    if not WIDE:
        return np.ones(k)
    levels = np.array([10, -10, 5, -5, 0])
    if k % 512:
        return np.exp2(np.random.permutation(np.resize(levels, k // 32))).repeat(32)
    a = np.empty((k // 512, 16))
    for p in range(k // 512):
        a[p, :8] = np.random.permutation(np.resize(levels, 8))
        for g in range(8):
            far = levels[np.abs(levels - a[p, g]) >= 10]
            a[p, g + 8] = far[np.random.randint(len(far))]
    return np.exp2(a.ravel()).repeat(32)


def f64(x):
    return np.asarray(x).astype(np.float64)


def striped(idx):
    return np.tile(idx.reshape(-1, 16).T, (8, 1)).astype(np.uint16)


def unstriped(offs):
    return offs[:16].T.reshape(-1).astype(np.int64)


E2M1 = np.array([0.0, 0.5, 1.0, 1.5, 2.0, 3.0, 4.0, 6.0, -0.0, -0.5, -1.0, -1.5, -2.0, -3.0, -4.0, -6.0])


def pack_weight(w, fmt):
    k, n = w.shape
    w = f64(np.asarray(w, np.float32).astype(ml_dtypes.bfloat16)).reshape(k // 32, 32, n)
    amax = np.abs(w).max(1)
    if fmt == "e4m3":
        byte = np.frexp(amax)[1] - 1 + 127 - 7
    else:
        mant, ex = np.frexp(amax / 6.0)
        byte = np.where(mant > 0.5, ex, ex - 1) + 127
    byte = np.clip(np.where(amax > 0, byte, 1), 1, 254)
    scaled = (w * np.exp2(127.0 - byte)[:, None, :]).reshape(k, n).astype(np.float32)
    by_word = np.ascontiguousarray(scaled.reshape(k // 512, 128, 4, n).transpose(0, 1, 3, 2))
    if fmt == "e4m3":
        words = by_word.astype(ml_dtypes.float8_e4m3fn).view(np.uint8)
    else:
        c = by_word.astype(ml_dtypes.float4_e2m1fn).view(np.uint8) & 0xF
        words = (c[..., 0::2] | (c[..., 1::2] << 4)).reshape(k // 512, 128, 2 * n)
    return np.ascontiguousarray(words), np.ascontiguousarray(byte.astype(np.uint8).reshape(k // 512, 16, n))


def unpack_weight(words, scales, fmt):
    g, _, n = scales.shape
    words = np.ascontiguousarray(words).reshape(g, 128, n, -1)
    if fmt == "e4m3":
        vals = words.view(ml_dtypes.float8_e4m3fn).astype(np.float64)
    else:
        nib = np.empty((g, 128, n, 4), np.uint8)
        nib[..., 0::2] = words & 0xF
        nib[..., 1::2] = words >> 4
        vals = E2M1[nib]
    vals = vals * np.repeat(np.exp2(scales.astype(np.float64) - 127.0), 8, axis=1)[..., None]
    return vals.transpose(0, 1, 3, 2).reshape(g * 512, n)


def gelu(v):
    return 0.5 * v * (1.0 + np.tanh(np.sqrt(2.0 / np.pi) * (v + 0.044715 * v**3)))


K, T, S, T2, H, P, N = 1024, 2048, 1024, 2048, 1024, 1024, 512

def setup_inputs():
    n = np.random.standard_normal
    s = mx_kscale(K)[:, None]
    u = mx_kscale(H)[:, None]
    tab_words, tab_scales = pack_weight(n((K, T)) * s, "e4m3")
    w2_words, w2_scales = pack_weight(n((H, H)) / np.sqrt(H) / u, "e2m1")
    return {
        "tab_words": tab_words, "tab_scales": tab_scales,
        "offs": striped(np.random.permutation(T)[:S]),
        "offs2": striped(np.random.permutation(T2)[:S]),
        "offs3": striped(np.random.permutation(T2)[:P]),
        "w1": (n((K, H)) / np.sqrt(K) / s * u.T).astype(np.float32),
        "b1": (0.5 * n(H) * u[:, 0]).astype(np.float32),
        "wgs": np.exp(0.3 * n((128, S))).astype(np.float32),
        "page0": (n((H, T2)) * u).astype(np.float32),
        "w2_words": w2_words, "w2_scales": w2_scales,
        "b2": (0.5 * n(H)).astype(np.float32),
        "w3": (1.5 * n((H, N)) / np.sqrt(H) / u).astype(np.float32),
    }

def reference(tab_words, tab_scales, offs, offs2, offs3, w1, b1, wgs, page0, w2_words, w2_scales, b2, w3):
    v = unpack_weight(tab_words, tab_scales, "e4m3")[:, unstriped(offs)]
    h = (mxq(f64(w1), 0, "e4m3").T @ v) + f64(b1)[:, None]
    page = f64(page0).copy()
    page[:, unstriped(offs2)] = np.tile(f64(wgs), (H // 128, 1)) * h
    x = page[:, unstriped(offs3)]
    w2 = unpack_weight(w2_words, w2_scales, "e2m1")
    g = (w2.T @ mxq(x, 0, "e4m3")) + f64(b2)[:, None]
    z = x * (1.0 / (1.0 + np.exp(-g)))
    return mxq(f64(w3), 0, "e4m3").T @ mxq(z, 0, "e4m3")

@@ -1,0 +1,320 @@
+from contextlib import ExitStack
+
+import concourse.mybir as mybir
+
+K, T, S, T2, H, M, N = 1024, 2048, 1024, 2048, 1024, 1024, 512
+FLOPS = 2 * K * H * S + 2 * H * H * M + 2 * H * N * M
+
+F32 = mybir.dt.float32
+BF16 = mybir.dt.bfloat16
+I32 = mybir.dt.int32
+U32 = mybir.dt.uint32
+U16 = mybir.dt.uint16
+U8 = mybir.dt.uint8
+FP8X4 = mybir.dt.float8_e4m3fn_x4
+FP4X4 = mybir.dt.float4_e2m1fn_x4
+MULT = mybir.AluOpType.mult
+ACT = mybir.ActivationFunctionType
+
+P = 128
+PACK = 4
+PASS = P * PACK
+BANK = 512
+HALF = BANK // 2
+QUAD = 32
+LIST_COLS = BANK // 16
+
+
+def tile_list_playlist_slot_refresh_kernel(
+    tc, tab_words, tab_scales, offs, offs2, offs3, w1, b1, wgs, page0, w2_words, w2_scales, b2, w3, out
+):
+    nc = tc.nc
+    with ExitStack() as ctx:
+        lists = ctx.enter_context(tc.tile_pool(name="lists", bufs=1))
+        sb = ctx.enter_context(tc.tile_pool(name="sb", bufs=1))
+        psum = ctx.enter_context(tc.psum_pool(name="psum", bufs=4))
+
+        def tile(shape, dtype, slot, name):
+            return sb.tile(shape, dtype, tag=slot, name=name, align_bytes=64)
+
+        def woven(ap):
+            return ap.rearrange("p (c e t) -> p c t e", e=2, t=PACK)
+
+        def planes(ap):
+            return ap.rearrange("p t (c e) -> p c t e", e=2)
+
+        idx = lists.tile([P, S // 16], U16, name="idx")
+        idx2 = lists.tile([P, S // 16], U16, name="idx2")
+        idx3 = lists.tile([P, M // 16], U16, name="idx3")
+
+        tab_sc = tile([P, T], U8, "tab_sc", "tab_sc")
+        nc.vector.memset(tab_sc[:].bitcast(I32), 0)
+        w2_sc_raw = tile([P, 2, H], U8, "w2_sc_raw", "w2_sc_raw")
+        nc.vector.memset(w2_sc_raw[:].bitcast(I32), 0)
+        b1_sb = tile([P, 2, PACK], F32, "b1", "b1_sb")
+        b2_sb = tile([P, 2, PACK], F32, "b2", "b2_sb")
+
+        w2_raw = tile([P, 2, 2 * H], U8, "w2_raw", "w2_raw")
+        nc.sync.dma_start(out=w2_raw[:].bitcast(I32), in_=w2_words.rearrange("a p c -> p a c").bitcast(I32))
+        nc.sync.dma_start(idx[:], offs)
+        for q in range(4):
+            nc.sync.dma_start(
+                out=tab_sc[QUAD * q : QUAD * q + 8, :].bitcast(I32),
+                in_=tab_scales[:, 4 * q : 4 * q + 4, :].bitcast(I32),
+            )
+        w2_codes = tile([P, 2, 2 * H], U8, "w2_codes", "w2_codes")
+        w2_sc = tile([P, 2, H], U8, "w2_sc", "w2_sc")
+        nc.vector.tensor_copy(
+            out=w2_codes[:].rearrange("p a c -> p (a c)").bitcast(U16).rearrange("p (g t m) -> p g t m", t=PACK, m=P),
+            in_=w2_raw[:].rearrange("p a c -> p (a c)").bitcast(U16).rearrange("p (g m t) -> p g t m", t=PACK, m=P),
+        )
+
+        tab_w = [tile([P, T], I32, "A%d" % a, "tab_w%d" % a) for a in range(2)]
+        v_codes = [tile([P, S], U32, "v%d" % a, "v_codes%d" % a) for a in range(2)]
+        v_sc = tile([P, S], U8, "v_sc", "v_sc")
+        w1_codes = {}
+        w1_sc = {}
+
+        def load_tab(a):
+            nc.sync.dma_start(out=tab_w[a][:], in_=tab_words[a].rearrange("p t i -> p (t i)").bitcast(I32))
+
+        def prep_w1(a, b):
+            raw = tile([P, PACK, PASS], F32, "B%d" % (2 * b + a), "w1_raw%d%d" % (a, b))
+            rows = w1[PASS * a : PASS * (a + 1), PASS * b : PASS * (b + 1)]
+            nc.sync.dma_start(out=raw[:], in_=rows.rearrange("(p j) c -> p j c", j=PACK))
+            grouped = tile([P, PASS * PACK], BF16, "wb%d" % a, "w1_b%d%d" % (a, b))
+            nc.scalar.copy(
+                out=grouped[:].rearrange("p (t m j) -> p m j t", t=PACK, j=PACK),
+                in_=raw[:].rearrange("p j (m t) -> p m j t", t=PACK),
+            )
+            codes = tile([P, PASS], U32, "wc%d%d" % (a, b), "w1_codes%d%d" % (a, b))
+            scales = tile([P, PASS], U8, "ws%d%d" % (a, b), "w1_sc%d%d" % (a, b))
+            nc.vector.quantize_mx(out=codes[:].bitcast(FP8X4), scales=scales[:], in_=grouped[:])
+            w1_codes[a, b] = codes
+            w1_sc[a, b] = scales
+
+        prep_w1(0, 0)
+        load_tab(0)
+        for q in range(4):
+            nc.sync.dma_start(
+                out=w2_sc_raw[QUAD * q : QUAD * q + 4, :, :].bitcast(I32),
+                in_=w2_scales[:, 4 * q : 4 * q + 4, :].rearrange("a r c -> r a c").bitcast(I32),
+            )
+        nc.vector.tensor_copy(v_sc[:], tab_sc[:].indirect(idx[:]))
+        nc.vector.tensor_copy(
+            out=w2_sc[:].rearrange("p a (b t m) -> p (a b) t m", t=PACK, m=P),
+            in_=w2_sc_raw[:].rearrange("p a (b m t) -> p (a b) t m", t=PACK, m=P),
+        )
+        nc.vector.tensor_copy(v_codes[0][:], tab_w[0][:].bitcast(U32).indirect(idx[:]))
+        prep_w1(1, 0)
+        load_tab(1)
+        for c in range(2):
+            nc.vector.tensor_copy(
+                v_codes[1][:, BANK * c : BANK * (c + 1)],
+                tab_w[1][:].bitcast(U32).indirect(idx[:, LIST_COLS * c : LIST_COLS * (c + 1)]),
+            )
+        nc.sync.dma_start(out=b1_sb[:], in_=b1.rearrange("(a p i) -> p a i", a=2, i=PACK))
+        nc.sync.dma_start(idx2[:], offs2)
+
+        gains = [tile([P, 2, S], F32, "G%d" % u, "gains%d" % u) for u in range(2)]
+        wgs_rows = wgs.rearrange("(r i) j -> r i j", i=PACK)
+
+        def load_gains(i0, i1):
+            for q in range(4):
+                nc.sync.dma_start(
+                    out=gains[i0 // 2][QUAD * q : QUAD * (q + 1), i0 % 2 : i0 % 2 + i1 - i0, :],
+                    in_=wgs_rows[:, i0:i1, :],
+                )
+
+        pages = {}
+
+        def load_page(b, i):
+            page = tile([P, T2], F32, "P%d%d" % (b, i), "page%d%d" % (b, i))
+            rows = page0[PASS * b : PASS * (b + 1), :].rearrange("(p i) t -> p i t", i=PACK)
+            nc.sync.dma_start(out=page[:], in_=rows[:, i, :])
+            pages[b, i] = page
+
+        def refresh(b, i):
+            h = tile([P, S], F32, "h%d%d" % (b, i), "h%d%d" % (b, i))
+            for c in range(2):
+                acc = psum.tile([P, BANK], F32, tag="acc", name="acc_h")
+                for a in range(2):
+                    nc.tensor.matmul_mx(
+                        out=acc[:],
+                        lhsT=w1_codes[a, b][:, P * i : P * (i + 1)].bitcast(FP8X4),
+                        lhsT_scale=w1_sc[a, b][:, P * i : P * (i + 1)],
+                        rhs=v_codes[a][:, BANK * c : BANK * (c + 1)].bitcast(FP8X4),
+                        rhs_scale=v_sc[4 * a : P, BANK * c : BANK * (c + 1)],
+                        start=(a == 0),
+                        stop=(a == 1),
+                    )
+                nc.scalar.activation(
+                    out=h[:, BANK * c : BANK * (c + 1)], in_=acc[:], func=ACT.Identity, bias=b1_sb[:, b, i : i + 1]
+                )
+            nc.vector.tensor_tensor(pages[b, i][:].indirect(idx2[:]), h[:], gains[i // 2][:, i % 2, :], MULT)
+
+        x_slot = {(0, 0): "B0", (0, 1): "B1", (1, 0): "B2", (1, 1): "G1"}
+        xs = {}
+
+        def x_planes(b, c):
+            return xs[b, c][:].rearrange("p (t m) -> p t m", t=PACK)
+
+        def fetch(b, i, c):
+            nc.vector.tensor_copy(
+                xs[b, c][:, BANK * i : BANK * (i + 1)],
+                pages[b, i][:].indirect(idx3[:, LIST_COLS * c : LIST_COLS * (c + 1)]),
+            )
+
+        x_codes = {}
+        x_sc = {}
+
+        def quant_x(b, c, xb):
+            codes = tile([P, BANK], U32, "xc%d%d" % (b, c), "x_codes%d%d" % (b, c))
+            scales = tile([P, BANK], U8, "xs%d%d" % (b, c), "x_sc%d%d" % (b, c))
+            nc.vector.quantize_mx(out=codes[:].bitcast(FP8X4), scales=scales[:], in_=xb)
+            x_codes[b, c] = codes
+            x_sc[b, c] = scales
+
+        w3_codes = {}
+        w3_sc = {}
+
+        def prep_w3(b):
+            raw = tile([P, PACK, N], F32, "A%d" % b, "w3_raw%d" % b)
+            nc.sync.dma_start(out=raw[:], in_=w3[PASS * b : PASS * (b + 1), :].rearrange("(p j) n -> p j n", j=PACK))
+            grouped = tile([P, N * PACK], BF16, "zb%d" % b, "w3_b%d" % b)
+            nc.scalar.copy(out=woven(grouped[:]), in_=planes(raw[:]))
+            codes = tile([P, N], U32, "w3c%d" % b, "w3_codes%d" % b)
+            scales = tile([P, N], U8, "w3s%d" % b, "w3_sc%d" % b)
+            nc.vector.quantize_mx(out=codes[:].bitcast(FP8X4), scales=scales[:], in_=grouped[:])
+            w3_codes[b] = codes
+            w3_sc[b] = scales
+
+        for key in x_slot:
+            xs[key] = tile([P, PACK * BANK], F32, x_slot[key], "x%d%d" % key)
+
+        load_page(0, 0)
+        load_gains(0, 1)
+        refresh(0, 0)
+        nc.sync.dma_start(idx3[:], offs3)
+        load_page(0, 1)
+        load_gains(1, 2)
+        fetch(0, 0, 0)
+        fetch(0, 0, 1)
+        refresh(0, 1)
+        prep_w1(0, 1)
+        load_page(0, 2)
+        load_gains(2, 4)
+        fetch(0, 1, 0)
+        fetch(0, 1, 1)
+        refresh(0, 2)
+        prep_w1(1, 1)
+        nc.sync.dma_start(out=b2_sb[:], in_=b2.rearrange("(a p i) -> p a i", a=2, i=PACK))
+        prep_w3(0)
+        prep_w3(1)
+        load_page(0, 3)
+        fetch(0, 2, 0)
+        fetch(0, 2, 1)
+        refresh(0, 3)
+        fetch(0, 3, 0)
+        fetch(0, 3, 1)
+
+        for i in range(PACK):
+            load_page(1, i)
+            refresh(1, i)
+            if i < 2:
+                xb = tile([P, BANK * PACK], BF16, "wb%d" % i, "xb0%d" % i)
+                nc.scalar.copy(out=woven(xb[:]), in_=planes(x_planes(0, i)))
+                quant_x(0, i, xb[:])
+            fetch(1, i, 0)
+        xb10 = xs[1, 1][:, 2 * BANK : 4 * BANK].bitcast(BF16)
+        nc.scalar.copy(out=woven(xb10), in_=planes(x_planes(1, 0)))
+        fetch(1, 0, 1)
+        fetch(1, 1, 1)
+        quant_x(1, 0, xb10)
+        fetch(1, 2, 1)
+        fetch(1, 3, 1)
+        xb11 = tile([P, BANK * PACK], BF16, "wb0", "xb11")
+        nc.vector.tensor_copy(out=woven(xb11[:]), in_=planes(x_planes(1, 1)))
+        quant_x(1, 1, xb11[:])
+
+        gates = {}
+        zbs = {}
+        z_codes = {}
+        z_sc = {}
+
+        def gate(b, c):
+            g = tile([P, PACK, BANK], F32, "P0%d" % (2 * c + b), "gate%d%d" % (b, c))
+            for i in range(PACK):
+                acc = psum.tile([P, BANK], F32, tag="acc", name="acc_g")
+                col = PASS * b + P * i
+                for a in range(2):
+                    nc.tensor.matmul_mx(
+                        out=acc[:],
+                        lhsT=w2_codes[:, a, 2 * col : 2 * (col + P)].bitcast(FP4X4),
+                        lhsT_scale=w2_sc[:, a, col : col + P],
+                        rhs=x_codes[a, c][:].bitcast(FP8X4),
+                        rhs_scale=x_sc[a, c][:],
+                        start=(a == 0),
+                        stop=(a == 1),
+                    )
+                nc.scalar.activation(out=g[:, i, :], in_=acc[:], func=ACT.Sigmoid, bias=b2_sb[:, b, i : i + 1])
+            gates[b, c] = g
+            zbs[b, c] = tile([P, BANK * PACK], BF16, "zb%d" % b, "zb%d%d" % (b, c))
+            z_codes[b, c] = tile([P, BANK], U32, "wc%d%d" % (b, c), "z_codes%d%d" % (b, c))
+            z_sc[b, c] = tile([P, BANK], U8, "ws%d%d" % (b, c), "z_sc%d%d" % (b, c))
+
+        def gated(b, c, lo, hi):
+            nc.vector.tensor_tensor(
+                woven(zbs[b, c][:, PACK * lo : PACK * hi]),
+                planes(x_planes(b, c)[:, :, lo:hi]),
+                planes(gates[b, c][:, :, lo:hi]),
+                MULT,
+            )
+
+        def quant_z(b, c, lo, hi):
+            nc.vector.quantize_mx(
+                out=z_codes[b, c][:, lo:hi].bitcast(FP8X4),
+                scales=z_sc[b, c][:, lo:hi],
+                in_=zbs[b, c][:, PACK * lo : PACK * hi],
+            )
+
+        staged = [tile([P, N // P, BANK], F32, "A%d" % c, "staged%d" % c) for c in range(2)]
+
+        def scores(c, lo, hi, banks, shared):
+            for n in range(N // P):
+                acc = psum.tile([P, hi - lo], F32, tag=banks, name="acc_o")
+                for b in range(2):
+                    nc.tensor.matmul_mx(
+                        out=acc[:],
+                        lhsT=w3_codes[b][:, P * n : P * (n + 1)].bitcast(FP8X4),
+                        lhsT_scale=w3_sc[b][:, P * n : P * (n + 1)],
+                        rhs=z_codes[b, c][:, lo:hi].bitcast(FP8X4),
+                        rhs_scale=z_sc[b, c][:, lo:hi],
+                        start=(b == 0),
+                        stop=(b == 1),
+                    )
+                if shared and n % 2 == 1:
+                    nc.vector.tensor_copy(out=staged[c][:, n, lo:hi], in_=acc[:])
+                else:
+                    nc.scalar.copy(out=staged[c][:, n, lo:hi], in_=acc[:])
+                nc.sync.dma_start(
+                    out=out[P * n : P * (n + 1), BANK * c + lo : BANK * c + hi], in_=staged[c][:, n, lo:hi]
+                )
+
+        gate(0, 0)
+        gate(1, 0)
+        gated(0, 0, 0, BANK)
+        gated(1, 0, 0, BANK)
+        quant_z(0, 0, 0, BANK)
+        gate(0, 1)
+        gated(0, 1, 0, BANK)
+        quant_z(1, 0, 0, BANK)
+        gate(1, 1)
+        gated(1, 1, 0, HALF)
+        quant_z(0, 1, 0, BANK)
+        gated(1, 1, HALF, BANK)
+        quant_z(1, 1, 0, HALF)
+        quant_z(1, 1, HALF, BANK)
+        scores(0, 0, BANK, "out", False)
+        scores(1, 0, HALF, "out", False)
+        scores(1, HALF, BANK, "acc", True)

@@ -54,11 +54,25 @@ def tile_list_playlist_slot_refresh_kernel(
         b1_sb = tile([P, 2, PACK], F32, "b1", "b1_sb")
         b2_sb = tile([P, 2, PACK], F32, "b2", "b2_sb")
 
+        gains = [tile([P, 2, S], F32, "G%d" % u, "gains%d" % u) for u in range(2)]
+        wgs_rows = wgs.rearrange("(r i) j -> r i j", i=PACK)
+
+        def load_gains(i0, i1, queue):
+            for q in (0, 2, 1, 3):
+                queue.dma_start(
+                    out=gains[i0 // 2][QUAD * q : QUAD * (q + 1), i0 % 2 : i0 % 2 + i1 - i0, :],
+                    in_=wgs_rows[:, i0:i1, :],
+                )
+
+        load_gains(0, 1, nc.scalar)
+        nc.scalar.dma_start(out=b1_sb[:], in_=b1.rearrange("(a p i) -> p a i", a=2, i=PACK))
+        nc.scalar.dma_start(out=b2_sb[:], in_=b2.rearrange("(a p i) -> p a i", a=2, i=PACK))
+
         w2_raw = tile([P, 2, 2 * H], U8, "w2_raw", "w2_raw")
         nc.sync.dma_start(out=w2_raw[:].bitcast(I32), in_=w2_words.rearrange("a p c -> p a c").bitcast(I32))
         nc.sync.dma_start(idx[:], offs)
         for q in range(4):
-            nc.sync.dma_start(
+            nc.gpsimd.dma_start(
                 out=tab_sc[QUAD * q : QUAD * q + 8, :].bitcast(I32),
                 in_=tab_scales[:, 4 * q : 4 * q + 4, :].bitcast(I32),
             )
@@ -78,53 +92,38 @@ def tile_list_playlist_slot_refresh_kernel(
         def load_tab(a):
             nc.sync.dma_start(out=tab_w[a][:], in_=tab_words[a].rearrange("p t i -> p (t i)").bitcast(I32))
 
-        def prep_w1(a, b):
+        def prep_w1(a, b, cuts):
             raw = tile([P, PACK, PASS], F32, "B%d" % (2 * b + a), "w1_raw%d%d" % (a, b))
             rows = w1[PASS * a : PASS * (a + 1), PASS * b : PASS * (b + 1)]
             nc.sync.dma_start(out=raw[:], in_=rows.rearrange("(p j) c -> p j c", j=PACK))
             grouped = tile([P, PASS * PACK], BF16, "wb%d" % a, "w1_b%d%d" % (a, b))
-            nc.scalar.copy(
-                out=grouped[:].rearrange("p (t m j) -> p m j t", t=PACK, j=PACK),
-                in_=raw[:].rearrange("p j (m t) -> p m j t", t=PACK),
-            )
             codes = tile([P, PASS], U32, "wc%d%d" % (a, b), "w1_codes%d%d" % (a, b))
             scales = tile([P, PASS], U8, "ws%d%d" % (a, b), "w1_sc%d%d" % (a, b))
-            nc.vector.quantize_mx(out=codes[:].bitcast(FP8X4), scales=scales[:], in_=grouped[:])
+            for t0, t1 in zip(cuts, cuts[1:]):
+                nc.scalar.copy(
+                    out=grouped[:].rearrange("p (t m j) -> p t m j", t=PACK, j=PACK)[:, t0:t1],
+                    in_=raw[:].rearrange("p j (m t) -> p t m j", t=PACK)[:, t0:t1],
+                )
+                nc.vector.quantize_mx(
+                    out=codes[:, P * t0 : P * t1].bitcast(FP8X4),
+                    scales=scales[:, P * t0 : P * t1],
+                    in_=grouped[:, PASS * t0 : PASS * t1],
+                )
             w1_codes[a, b] = codes
             w1_sc[a, b] = scales
 
-        prep_w1(0, 0)
+        prep_w1(0, 0, (0, 4))
         load_tab(0)
-        for q in range(4):
-            nc.sync.dma_start(
-                out=w2_sc_raw[QUAD * q : QUAD * q + 4, :, :].bitcast(I32),
-                in_=w2_scales[:, 4 * q : 4 * q + 4, :].rearrange("a r c -> r a c").bitcast(I32),
-            )
         nc.vector.tensor_copy(v_sc[:], tab_sc[:].indirect(idx[:]))
-        nc.vector.tensor_copy(
-            out=w2_sc[:].rearrange("p a (b t m) -> p (a b) t m", t=PACK, m=P),
-            in_=w2_sc_raw[:].rearrange("p a (b m t) -> p (a b) t m", t=PACK, m=P),
-        )
         nc.vector.tensor_copy(v_codes[0][:], tab_w[0][:].bitcast(U32).indirect(idx[:]))
-        prep_w1(1, 0)
+        prep_w1(1, 0, (0, 1, 2, 4))
         load_tab(1)
         for c in range(2):
             nc.vector.tensor_copy(
                 v_codes[1][:, BANK * c : BANK * (c + 1)],
                 tab_w[1][:].bitcast(U32).indirect(idx[:, LIST_COLS * c : LIST_COLS * (c + 1)]),
             )
-        nc.sync.dma_start(out=b1_sb[:], in_=b1.rearrange("(a p i) -> p a i", a=2, i=PACK))
         nc.sync.dma_start(idx2[:], offs2)
-
-        gains = [tile([P, 2, S], F32, "G%d" % u, "gains%d" % u) for u in range(2)]
-        wgs_rows = wgs.rearrange("(r i) j -> r i j", i=PACK)
-
-        def load_gains(i0, i1):
-            for q in range(4):
-                nc.sync.dma_start(
-                    out=gains[i0 // 2][QUAD * q : QUAD * (q + 1), i0 % 2 : i0 % 2 + i1 - i0, :],
-                    in_=wgs_rows[:, i0:i1, :],
-                )
 
         pages = {}
 
@@ -193,22 +192,29 @@ def tile_list_playlist_slot_refresh_kernel(
             xs[key] = tile([P, PACK * BANK], F32, x_slot[key], "x%d%d" % key)
 
         load_page(0, 0)
-        load_gains(0, 1)
         refresh(0, 0)
         nc.sync.dma_start(idx3[:], offs3)
         load_page(0, 1)
-        load_gains(1, 2)
+        load_gains(1, 2, nc.sync)
+        for q in range(4):
+            nc.sync.dma_start(
+                out=w2_sc_raw[QUAD * q : QUAD * q + 4, :, :].bitcast(I32),
+                in_=w2_scales[:, 4 * q : 4 * q + 4, :].rearrange("a r c -> r a c").bitcast(I32),
+            )
+        nc.vector.tensor_copy(
+            out=w2_sc[:].rearrange("p a (b t m) -> p (a b) t m", t=PACK, m=P),
+            in_=w2_sc_raw[:].rearrange("p a (b m t) -> p (a b) t m", t=PACK, m=P),
+        )
         fetch(0, 0, 0)
         fetch(0, 0, 1)
         refresh(0, 1)
-        prep_w1(0, 1)
+        prep_w1(0, 1, (0, 4))
         load_page(0, 2)
-        load_gains(2, 4)
+        load_gains(2, 4, nc.sync)
         fetch(0, 1, 0)
         fetch(0, 1, 1)
         refresh(0, 2)
-        prep_w1(1, 1)
-        nc.sync.dma_start(out=b2_sb[:], in_=b2.rearrange("(a p i) -> p a i", a=2, i=PACK))
+        prep_w1(1, 1, (0, 4))
         prep_w3(0)
         prep_w3(1)
         load_page(0, 3)

@@ -38,10 +38,10 @@ def tile_list_playlist_slot_refresh_kernel(
             return sb.tile(shape, dtype, tag=slot, name=name, align_bytes=64)
 
         def woven(ap):
-            return ap.rearrange("p (c e t) -> p c t e", e=2, t=PACK)
+            return ap.rearrange("p (c t) -> p c t", t=PACK)
 
         def planes(ap):
-            return ap.rearrange("p t (c e) -> p c t e", e=2)
+            return ap.rearrange("p t c -> p c t")
 
         idx = lists.tile([P, S // 16], U16, name="idx")
         idx2 = lists.tile([P, S // 16], U16, name="idx2")
@@ -57,31 +57,12 @@ def tile_list_playlist_slot_refresh_kernel(
         gains = [tile([P, 2, S], F32, "G%d" % u, "gains%d" % u) for u in range(2)]
         wgs_rows = wgs.rearrange("(r i) j -> r i j", i=PACK)
 
-        def load_gains(i0, i1, queue):
+        def load_gains(i0, i1, lo, hi):
             for q in (0, 2, 1, 3):
-                queue.dma_start(
-                    out=gains[i0 // 2][QUAD * q : QUAD * (q + 1), i0 % 2 : i0 % 2 + i1 - i0, :],
-                    in_=wgs_rows[:, i0:i1, :],
+                nc.sync.dma_start(
+                    out=gains[i0 // 2][QUAD * q : QUAD * (q + 1), i0 % 2 : i0 % 2 + i1 - i0, lo:hi],
+                    in_=wgs_rows[:, i0:i1, lo:hi],
                 )
-
-        load_gains(0, 1, nc.scalar)
-        nc.scalar.dma_start(out=b1_sb[:], in_=b1.rearrange("(a p i) -> p a i", a=2, i=PACK))
-        nc.scalar.dma_start(out=b2_sb[:], in_=b2.rearrange("(a p i) -> p a i", a=2, i=PACK))
-
-        w2_raw = tile([P, 2, 2 * H], U8, "w2_raw", "w2_raw")
-        nc.sync.dma_start(out=w2_raw[:].bitcast(I32), in_=w2_words.rearrange("a p c -> p a c").bitcast(I32))
-        nc.sync.dma_start(idx[:], offs)
-        for q in range(4):
-            nc.gpsimd.dma_start(
-                out=tab_sc[QUAD * q : QUAD * q + 8, :].bitcast(I32),
-                in_=tab_scales[:, 4 * q : 4 * q + 4, :].bitcast(I32),
-            )
-        w2_codes = tile([P, 2, 2 * H], U8, "w2_codes", "w2_codes")
-        w2_sc = tile([P, 2, H], U8, "w2_sc", "w2_sc")
-        nc.vector.tensor_copy(
-            out=w2_codes[:].rearrange("p a c -> p (a c)").bitcast(U16).rearrange("p (g t m) -> p g t m", t=PACK, m=P),
-            in_=w2_raw[:].rearrange("p a c -> p (a c)").bitcast(U16).rearrange("p (g m t) -> p g t m", t=PACK, m=P),
-        )
 
         tab_w = [tile([P, T], I32, "A%d" % a, "tab_w%d" % a) for a in range(2)]
         v_codes = [tile([P, S], U32, "v%d" % a, "v_codes%d" % a) for a in range(2)]
@@ -92,18 +73,21 @@ def tile_list_playlist_slot_refresh_kernel(
         def load_tab(a):
             nc.sync.dma_start(out=tab_w[a][:], in_=tab_words[a].rearrange("p t i -> p (t i)").bitcast(I32))
 
-        def prep_w1(a, b, cuts):
+        def prep_w1(a, b, cuts, shared=False):
             raw = tile([P, PACK, PASS], F32, "B%d" % (2 * b + a), "w1_raw%d%d" % (a, b))
             rows = w1[PASS * a : PASS * (a + 1), PASS * b : PASS * (b + 1)]
             nc.sync.dma_start(out=raw[:], in_=rows.rearrange("(p j) c -> p j c", j=PACK))
             grouped = tile([P, PASS * PACK], BF16, "wb%d" % a, "w1_b%d%d" % (a, b))
             codes = tile([P, PASS], U32, "wc%d%d" % (a, b), "w1_codes%d%d" % (a, b))
             scales = tile([P, PASS], U8, "ws%d%d" % (a, b), "w1_sc%d%d" % (a, b))
+            dst = grouped[:].rearrange("p (t m j) -> p t m j", t=PACK, j=PACK)
+            src = raw[:].rearrange("p j (m t) -> p t m j", t=PACK)
             for t0, t1 in zip(cuts, cuts[1:]):
-                nc.scalar.copy(
-                    out=grouped[:].rearrange("p (t m j) -> p t m j", t=PACK, j=PACK)[:, t0:t1],
-                    in_=raw[:].rearrange("p j (m t) -> p t m j", t=PACK)[:, t0:t1],
-                )
+                if shared:
+                    nc.scalar.copy(out=dst[:, 0:2], in_=src[:, 0:2])
+                    nc.vector.tensor_copy(out=dst[:, 2:4], in_=src[:, 2:4])
+                else:
+                    nc.scalar.copy(out=dst[:, t0:t1], in_=src[:, t0:t1])
                 nc.vector.quantize_mx(
                     out=codes[:, P * t0 : P * t1].bitcast(FP8X4),
                     scales=scales[:, P * t0 : P * t1],
@@ -112,18 +96,25 @@ def tile_list_playlist_slot_refresh_kernel(
             w1_codes[a, b] = codes
             w1_sc[a, b] = scales
 
-        prep_w1(0, 0, (0, 4))
         load_tab(0)
-        nc.vector.tensor_copy(v_sc[:], tab_sc[:].indirect(idx[:]))
+        nc.sync.dma_start(idx[:], offs)
+        for q in range(4):
+            nc.sync.dma_start(
+                out=tab_sc[QUAD * q : QUAD * q + 8, :].bitcast(I32),
+                in_=tab_scales[:, 4 * q : 4 * q + 4, :].bitcast(I32),
+            )
+        nc.sync.dma_start(out=b1_sb[:], in_=b1.rearrange("(a p i) -> p a i", a=2, i=PACK))
+        nc.sync.dma_start(idx2[:], offs2)
         nc.vector.tensor_copy(v_codes[0][:], tab_w[0][:].bitcast(U32).indirect(idx[:]))
-        prep_w1(1, 0, (0, 1, 2, 4))
+        nc.vector.tensor_copy(v_sc[:], tab_sc[:].indirect(idx[:]))
+        prep_w1(0, 0, (0, 4), shared=True)
+        prep_w1(1, 0, (0, 4), shared=True)
         load_tab(1)
         for c in range(2):
             nc.vector.tensor_copy(
                 v_codes[1][:, BANK * c : BANK * (c + 1)],
                 tab_w[1][:].bitcast(U32).indirect(idx[:, LIST_COLS * c : LIST_COLS * (c + 1)]),
             )
-        nc.sync.dma_start(idx2[:], offs2)
 
         pages = {}
 
@@ -133,7 +124,7 @@ def tile_list_playlist_slot_refresh_kernel(
             nc.sync.dma_start(out=page[:], in_=rows[:, i, :])
             pages[b, i] = page
 
-        def refresh(b, i):
+        def refresh(b, i, pieces=1):
             h = tile([P, S], F32, "h%d%d" % (b, i), "h%d%d" % (b, i))
             for c in range(2):
                 acc = psum.tile([P, BANK], F32, tag="acc", name="acc_h")
@@ -150,7 +141,14 @@ def tile_list_playlist_slot_refresh_kernel(
                 nc.scalar.activation(
                     out=h[:, BANK * c : BANK * (c + 1)], in_=acc[:], func=ACT.Identity, bias=b1_sb[:, b, i : i + 1]
                 )
-            nc.vector.tensor_tensor(pages[b, i][:].indirect(idx2[:]), h[:], gains[i // 2][:, i % 2, :], MULT)
+            width = S // pieces
+            for u in range(pieces):
+                nc.vector.tensor_tensor(
+                    pages[b, i][:].indirect(idx2[:, width // 16 * u : width // 16 * (u + 1)]),
+                    h[:, width * u : width * (u + 1)],
+                    gains[i // 2][:, i % 2, width * u : width * (u + 1)],
+                    MULT,
+                )
 
         x_slot = {(0, 0): "B0", (0, 1): "B1", (1, 0): "B2", (1, 1): "G1"}
         xs = {}
@@ -192,10 +190,22 @@ def tile_list_playlist_slot_refresh_kernel(
             xs[key] = tile([P, PACK * BANK], F32, x_slot[key], "x%d%d" % key)
 
         load_page(0, 0)
-        refresh(0, 0)
+        load_gains(0, 1, 0, BANK)
+        load_gains(0, 1, BANK, S)
+        refresh(0, 0, 2)
         nc.sync.dma_start(idx3[:], offs3)
         load_page(0, 1)
-        load_gains(1, 2, nc.sync)
+        load_gains(1, 2, 0, S)
+        nc.sync.dma_start(out=b2_sb[:], in_=b2.rearrange("(a p i) -> p a i", a=2, i=PACK))
+        w2_raw = tile([P, 2, 2 * H], U8, "w2_raw", "w2_raw")
+        nc.sync.dma_start(out=w2_raw[:].bitcast(I32), in_=w2_words.rearrange("a p c -> p a c").bitcast(I32))
+        w2_codes = tile([P, 2, 2 * H], U8, "w2_codes", "w2_codes")
+        w2_sc = tile([P, 2, H], U8, "w2_sc", "w2_sc")
+        nc.vector.tensor_copy(
+            out=w2_codes[:].rearrange("p a c -> p (a c)").bitcast(U16).rearrange("p (g t m) -> p g t m", t=PACK, m=P),
+            in_=w2_raw[:].rearrange("p a c -> p (a c)").bitcast(U16).rearrange("p (g m t) -> p g t m", t=PACK, m=P),
+        )
+
         for q in range(4):
             nc.sync.dma_start(
                 out=w2_sc_raw[QUAD * q : QUAD * q + 4, :, :].bitcast(I32),
@@ -210,7 +220,7 @@ def tile_list_playlist_slot_refresh_kernel(
         refresh(0, 1)
         prep_w1(0, 1, (0, 4))
         load_page(0, 2)
-        load_gains(2, 4, nc.sync)
+        load_gains(2, 4, 0, S)
         fetch(0, 1, 0)
         fetch(0, 1, 1)
         refresh(0, 2)
@@ -245,6 +255,7 @@ def tile_list_playlist_slot_refresh_kernel(
 
         gates = {}
         zbs = {}
+        zps = {}
         z_codes = {}
         z_sc = {}
 
@@ -269,15 +280,22 @@ def tile_list_playlist_slot_refresh_kernel(
             z_codes[b, c] = tile([P, BANK], U32, "wc%d%d" % (b, c), "z_codes%d%d" % (b, c))
             z_sc[b, c] = tile([P, BANK], U8, "ws%d%d" % (b, c), "z_sc%d%d" % (b, c))
 
-        def gated(b, c, lo, hi):
+        def gated(b, c, lo, hi, slot):
+            zps[b, c, lo] = tile([P, 2, hi - lo, 2], BF16, slot, "zp%d%d%d" % (b, c, lo))
             nc.vector.tensor_tensor(
-                woven(zbs[b, c][:, PACK * lo : PACK * hi]),
-                planes(x_planes(b, c)[:, :, lo:hi]),
-                planes(gates[b, c][:, :, lo:hi]),
+                zps[b, c, lo][:],
+                x_planes(b, c)[:, :, lo:hi].rearrange("p (u e) m -> p u m e", e=2),
+                gates[b, c][:, :, lo:hi].rearrange("p (u e) m -> p u m e", e=2),
                 MULT,
             )
 
-        def quant_z(b, c, lo, hi):
+        def quant_z(b, c, lo, hi, last=False):
+            pairs = zps[b, c, lo][:].rearrange("p u m e -> p (u m e)").bitcast(F32).rearrange("p (u m) -> p m u", u=2)
+            words = zbs[b, c][:].bitcast(F32).rearrange("p (m u) -> p m u", u=2)
+            if last:
+                nc.vector.tensor_copy(out=words[:, lo:hi, :], in_=pairs)
+            else:
+                nc.scalar.copy(out=words[:, lo:hi, :], in_=pairs)
             nc.vector.quantize_mx(
                 out=z_codes[b, c][:, lo:hi].bitcast(FP8X4),
                 scales=z_sc[b, c][:, lo:hi],
@@ -309,18 +327,18 @@ def tile_list_playlist_slot_refresh_kernel(
 
         gate(0, 0)
         gate(1, 0)
-        gated(0, 0, 0, BANK)
-        gated(1, 0, 0, BANK)
+        gated(0, 0, 0, BANK, "wb1")
+        gated(1, 0, 0, BANK, "wb0")
         quant_z(0, 0, 0, BANK)
         gate(0, 1)
-        gated(0, 1, 0, BANK)
+        gated(0, 1, 0, BANK, "wb1")
         quant_z(1, 0, 0, BANK)
         gate(1, 1)
-        gated(1, 1, 0, HALF)
+        gated(1, 1, 0, HALF, "wb0")
         quant_z(0, 1, 0, BANK)
-        gated(1, 1, HALF, BANK)
+        gated(1, 1, HALF, BANK, "wb1")
         quant_z(1, 1, 0, HALF)
-        quant_z(1, 1, HALF, BANK)
+        quant_z(1, 1, HALF, BANK, last=True)
         scores(0, 0, BANK, "out", False)
         scores(1, 0, HALF, "out", False)
         scores(1, HALF, BANK, "acc", True)

@@ -57,9 +57,9 @@ def tile_list_playlist_slot_refresh_kernel(
         gains = [tile([P, 2, S], F32, "G%d" % u, "gains%d" % u) for u in range(2)]
         wgs_rows = wgs.rearrange("(r i) j -> r i j", i=PACK)
 
-        def load_gains(i0, i1, lo, hi):
+        def load_gains(i0, i1, lo, hi, queue=nc.sync):
             for q in (0, 2, 1, 3):
-                nc.sync.dma_start(
+                queue.dma_start(
                     out=gains[i0 // 2][QUAD * q : QUAD * (q + 1), i0 % 2 : i0 % 2 + i1 - i0, lo:hi],
                     in_=wgs_rows[:, i0:i1, lo:hi],
                 )
@@ -99,7 +99,7 @@ def tile_list_playlist_slot_refresh_kernel(
         load_tab(0)
         nc.sync.dma_start(idx[:], offs)
         for q in range(4):
-            nc.sync.dma_start(
+            nc.gpsimd.dma_start(
                 out=tab_sc[QUAD * q : QUAD * q + 8, :].bitcast(I32),
                 in_=tab_scales[:, 4 * q : 4 * q + 4, :].bitcast(I32),
             )
@@ -107,6 +107,7 @@ def tile_list_playlist_slot_refresh_kernel(
         nc.sync.dma_start(idx2[:], offs2)
         nc.vector.tensor_copy(v_codes[0][:], tab_w[0][:].bitcast(U32).indirect(idx[:]))
         nc.vector.tensor_copy(v_sc[:], tab_sc[:].indirect(idx[:]))
+        load_gains(0, 1, 0, BANK, nc.gpsimd)
         prep_w1(0, 0, (0, 4), shared=True)
         prep_w1(1, 0, (0, 4), shared=True)
         load_tab(1)
@@ -117,6 +118,7 @@ def tile_list_playlist_slot_refresh_kernel(
             )
 
         pages = {}
+        hx = tile([P, (2 * PACK + 1) * S], F32, "hx", "hx")
 
         def load_page(b, i):
             page = tile([P, T2], F32, "P%d%d" % (b, i), "page%d%d" % (b, i))
@@ -125,7 +127,7 @@ def tile_list_playlist_slot_refresh_kernel(
             pages[b, i] = page
 
         def refresh(b, i, pieces=1):
-            h = tile([P, S], F32, "h%d%d" % (b, i), "h%d%d" % (b, i))
+            h = hx[:, S * (PACK * b + i) : S * (PACK * b + i + 1)]
             for c in range(2):
                 acc = psum.tile([P, BANK], F32, tag="acc", name="acc_h")
                 for a in range(2):
@@ -150,15 +152,21 @@ def tile_list_playlist_slot_refresh_kernel(
                     MULT,
                 )
 
-        x_slot = {(0, 0): "B0", (0, 1): "B1", (1, 0): "B2", (1, 1): "G1"}
-        xs = {}
+        x_last = tile([P, PACK * BANK], F32, "G1", "x_last")
 
         def x_planes(b, c):
-            return xs[b, c][:].rearrange("p (t m) -> p t m", t=PACK)
+            if (b, c) == (1, 1):
+                return x_last[:].rearrange("p (t m) -> p t m", t=PACK)
+            first = S * (PACK * b + 1)
+            return hx[:, first : first + PACK * S].rearrange("p (t m) -> p t m", t=PACK)[:, :, BANK * c : BANK * (c + 1)]
+
+        def fetch_whole(i):
+            first = S * (i + 1)
+            nc.vector.tensor_copy(hx[:, first : first + M], pages[0, i][:].indirect(idx3[:]))
 
         def fetch(b, i, c):
             nc.vector.tensor_copy(
-                xs[b, c][:, BANK * i : BANK * (i + 1)],
+                x_planes(b, c)[:, i, :],
                 pages[b, i][:].indirect(idx3[:, LIST_COLS * c : LIST_COLS * (c + 1)]),
             )
 
@@ -186,16 +194,23 @@ def tile_list_playlist_slot_refresh_kernel(
             w3_codes[b] = codes
             w3_sc[b] = scales
 
-        for key in x_slot:
-            xs[key] = tile([P, PACK * BANK], F32, x_slot[key], "x%d%d" % key)
-
         load_page(0, 0)
-        load_gains(0, 1, 0, BANK)
         load_gains(0, 1, BANK, S)
         refresh(0, 0, 2)
         nc.sync.dma_start(idx3[:], offs3)
         load_page(0, 1)
         load_gains(1, 2, 0, S)
+        refresh(0, 1)
+        fetch_whole(0)
+        load_page(0, 2)
+        load_gains(2, 4, 0, S)
+        refresh(0, 2)
+        fetch_whole(1)
+        prep_w1(0, 1, (0, 4))
+        prep_w1(1, 1, (0, 4))
+        load_page(0, 3)
+        refresh(0, 3)
+        fetch_whole(2)
         nc.sync.dma_start(out=b2_sb[:], in_=b2.rearrange("(a p i) -> p a i", a=2, i=PACK))
         w2_raw = tile([P, 2, 2 * H], U8, "w2_raw", "w2_raw")
         nc.sync.dma_start(out=w2_raw[:].bitcast(I32), in_=w2_words.rearrange("a p c -> p a c").bitcast(I32))
@@ -215,34 +230,21 @@ def tile_list_playlist_slot_refresh_kernel(
             out=w2_sc[:].rearrange("p a (b t m) -> p (a b) t m", t=PACK, m=P),
             in_=w2_sc_raw[:].rearrange("p a (b m t) -> p (a b) t m", t=PACK, m=P),
         )
-        fetch(0, 0, 0)
-        fetch(0, 0, 1)
-        refresh(0, 1)
-        prep_w1(0, 1, (0, 4))
-        load_page(0, 2)
-        load_gains(2, 4, 0, S)
-        fetch(0, 1, 0)
-        fetch(0, 1, 1)
-        refresh(0, 2)
-        prep_w1(1, 1, (0, 4))
         prep_w3(0)
         prep_w3(1)
-        load_page(0, 3)
-        fetch(0, 2, 0)
-        fetch(0, 2, 1)
-        refresh(0, 3)
-        fetch(0, 3, 0)
-        fetch(0, 3, 1)
-
-        for i in range(PACK):
+        load_page(1, 0)
+        refresh(1, 0)
+        fetch_whole(3)
+        for i in range(1, PACK):
             load_page(1, i)
             refresh(1, i)
-            if i < 2:
-                xb = tile([P, BANK * PACK], BF16, "wb%d" % i, "xb0%d" % i)
-                nc.scalar.copy(out=woven(xb[:]), in_=planes(x_planes(0, i)))
-                quant_x(0, i, xb[:])
-            fetch(1, i, 0)
-        xb10 = xs[1, 1][:, 2 * BANK : 4 * BANK].bitcast(BF16)
+            if i < 3:
+                xb = tile([P, BANK * PACK], BF16, "wb%d" % (i - 1), "xb0%d" % (i - 1))
+                nc.scalar.copy(out=woven(xb[:]), in_=planes(x_planes(0, i - 1)))
+                quant_x(0, i - 1, xb[:])
+            fetch(1, i - 1, 0)
+        fetch(1, PACK - 1, 0)
+        xb10 = x_last[:, 2 * BANK : 4 * BANK].bitcast(BF16)
         nc.scalar.copy(out=woven(xb10), in_=planes(x_planes(1, 0)))
         fetch(1, 0, 1)
         fetch(1, 1, 1)

@@ -57,9 +57,9 @@ def tile_list_playlist_slot_refresh_kernel(
         gains = [tile([P, 2, S], F32, "G%d" % u, "gains%d" % u) for u in range(2)]
         wgs_rows = wgs.rearrange("(r i) j -> r i j", i=PACK)
 
-        def load_gains(i0, i1, lo, hi, queue=nc.sync):
+        def load_gains(i0, i1, lo, hi):
             for q in (0, 2, 1, 3):
-                queue.dma_start(
+                nc.sync.dma_start(
                     out=gains[i0 // 2][QUAD * q : QUAD * (q + 1), i0 % 2 : i0 % 2 + i1 - i0, lo:hi],
                     in_=wgs_rows[:, i0:i1, lo:hi],
                 )
@@ -99,7 +99,7 @@ def tile_list_playlist_slot_refresh_kernel(
         load_tab(0)
         nc.sync.dma_start(idx[:], offs)
         for q in range(4):
-            nc.gpsimd.dma_start(
+            nc.sync.dma_start(
                 out=tab_sc[QUAD * q : QUAD * q + 8, :].bitcast(I32),
                 in_=tab_scales[:, 4 * q : 4 * q + 4, :].bitcast(I32),
             )
@@ -107,7 +107,6 @@ def tile_list_playlist_slot_refresh_kernel(
         nc.sync.dma_start(idx2[:], offs2)
         nc.vector.tensor_copy(v_codes[0][:], tab_w[0][:].bitcast(U32).indirect(idx[:]))
         nc.vector.tensor_copy(v_sc[:], tab_sc[:].indirect(idx[:]))
-        load_gains(0, 1, 0, BANK, nc.gpsimd)
         prep_w1(0, 0, (0, 4), shared=True)
         prep_w1(1, 0, (0, 4), shared=True)
         load_tab(1)
@@ -195,6 +194,7 @@ def tile_list_playlist_slot_refresh_kernel(
             w3_sc[b] = scales
 
         load_page(0, 0)
+        load_gains(0, 1, 0, BANK)
         load_gains(0, 1, BANK, S)
         refresh(0, 0, 2)
         nc.sync.dma_start(idx3[:], offs3)

@@ -47,126 +47,140 @@ def tile_list_playlist_slot_refresh_kernel(
         idx2 = lists.tile([P, S // 16], U16, name="idx2")
         idx3 = lists.tile([P, M // 16], U16, name="idx3")
 
+        def weave(dst, src):
+            nc.scalar.copy(
+                out=dst.rearrange("p (c i t) -> p c t i", i=PACK, t=PACK),
+                in_=src.rearrange("p t (c i) -> p c t i", i=PACK),
+            )
+
         tab_sc = tile([P, T], U8, "tab_sc", "tab_sc")
         nc.vector.memset(tab_sc[:].bitcast(I32), 0)
         w2_sc_raw = tile([P, 2, H], U8, "w2_sc_raw", "w2_sc_raw")
         nc.vector.memset(w2_sc_raw[:].bitcast(I32), 0)
-        b1_sb = tile([P, 2, PACK], F32, "b1", "b1_sb")
+        warm = tile([P, 1], F32, "warm", "warm")
+        nc.gpsimd.memset(warm[:], 0.0)
+        warmed = tile([P, 1], F32, "warmed", "warmed")
+        nc.scalar.activation(out=warmed[:], in_=warm[:], func=ACT.Sigmoid)
+        b1_rows = tile([P, PACK], F32, "b1r", "b1_rows")
+        b1_planes = tile([P, PACK], F32, "b1p", "b1_planes")
         b2_sb = tile([P, 2, PACK], F32, "b2", "b2_sb")
 
+        gains_rows = tile([P, S], F32, "GR", "gains_rows")
         gains = [tile([P, 2, S], F32, "G%d" % u, "gains%d" % u) for u in range(2)]
         wgs_rows = wgs.rearrange("(r i) j -> r i j", i=PACK)
 
-        def load_gains(i0, i1, lo, hi):
+        def load_gains(i):
             for q in (0, 2, 1, 3):
-                nc.sync.dma_start(
-                    out=gains[i0 // 2][QUAD * q : QUAD * (q + 1), i0 % 2 : i0 % 2 + i1 - i0, lo:hi],
-                    in_=wgs_rows[:, i0:i1, lo:hi],
-                )
+                nc.sync.dma_start(out=gains[i // 2][QUAD * q : QUAD * (q + 1), i % 2, :], in_=wgs_rows[:, i, :])
 
-        tab_w = [tile([P, T], I32, "A%d" % a, "tab_w%d" % a) for a in range(2)]
+        tab_w = tile([P, 2 * T], I32, "A", "tab_w")
         v_codes = [tile([P, S], U32, "v%d" % a, "v_codes%d" % a) for a in range(2)]
         v_sc = tile([P, S], U8, "v_sc", "v_sc")
         w1_codes = {}
         w1_sc = {}
 
         def load_tab(a):
-            nc.sync.dma_start(out=tab_w[a][:], in_=tab_words[a].rearrange("p t i -> p (t i)").bitcast(I32))
-
-        def prep_w1(a, b, cuts, shared=False):
-            raw = tile([P, PACK, PASS], F32, "B%d" % (2 * b + a), "w1_raw%d%d" % (a, b))
-            rows = w1[PASS * a : PASS * (a + 1), PASS * b : PASS * (b + 1)]
-            nc.sync.dma_start(out=raw[:], in_=rows.rearrange("(p j) c -> p j c", j=PACK))
-            grouped = tile([P, PASS * PACK], BF16, "wb%d" % a, "w1_b%d%d" % (a, b))
-            codes = tile([P, PASS], U32, "wc%d%d" % (a, b), "w1_codes%d%d" % (a, b))
-            scales = tile([P, PASS], U8, "ws%d%d" % (a, b), "w1_sc%d%d" % (a, b))
-            dst = grouped[:].rearrange("p (t m j) -> p t m j", t=PACK, j=PACK)
-            src = raw[:].rearrange("p j (m t) -> p t m j", t=PACK)
-            for t0, t1 in zip(cuts, cuts[1:]):
-                if shared:
-                    nc.scalar.copy(out=dst[:, 0:2], in_=src[:, 0:2])
-                    nc.vector.tensor_copy(out=dst[:, 2:4], in_=src[:, 2:4])
-                else:
-                    nc.scalar.copy(out=dst[:, t0:t1], in_=src[:, t0:t1])
-                nc.vector.quantize_mx(
-                    out=codes[:, P * t0 : P * t1].bitcast(FP8X4),
-                    scales=scales[:, P * t0 : P * t1],
-                    in_=grouped[:, PASS * t0 : PASS * t1],
-                )
-            w1_codes[a, b] = codes
-            w1_sc[a, b] = scales
-
-        load_tab(0)
-        nc.sync.dma_start(idx[:], offs)
-        for q in range(4):
             nc.sync.dma_start(
-                out=tab_sc[QUAD * q : QUAD * q + 8, :].bitcast(I32),
-                in_=tab_scales[:, 4 * q : 4 * q + 4, :].bitcast(I32),
+                out=tab_w[:, T * a : T * (a + 1)], in_=tab_words[a].rearrange("p t i -> p (t i)").bitcast(I32)
             )
-        nc.sync.dma_start(out=b1_sb[:], in_=b1.rearrange("(a p i) -> p a i", a=2, i=PACK))
-        nc.sync.dma_start(idx2[:], offs2)
-        nc.vector.tensor_copy(v_codes[0][:], tab_w[0][:].bitcast(U32).indirect(idx[:]))
-        nc.vector.tensor_copy(v_sc[:], tab_sc[:].indirect(idx[:]))
-        prep_w1(0, 0, (0, 4), shared=True)
-        prep_w1(1, 0, (0, 4), shared=True)
-        load_tab(1)
-        for c in range(2):
-            nc.vector.tensor_copy(
-                v_codes[1][:, BANK * c : BANK * (c + 1)],
-                tab_w[1][:].bitcast(U32).indirect(idx[:, LIST_COLS * c : LIST_COLS * (c + 1)]),
+
+        def tab_window(a):
+            return tab_w[:, T * a : T * (a + 1)].bitcast(U32)
+
+        def prep_w1_rows(t):
+            raw = tile([P, 2 * PACK * P], F32, "R%d" % t, "w1_raw0%d" % t)
+            grouped = tile([P, 2 * PACK * P], BF16, "sb%d" % (t % 2), "w1_b0%d" % t)
+            codes = tile([P, 2 * P], U32, "wc0%d" % t, "w1_codes0%d" % t)
+            scales = tile([P, 2 * P], U8, "ws0%d" % t, "w1_sc0%d" % t)
+            for a in range(2):
+                part = raw[:, PASS * a : PASS * (a + 1)].rearrange("p (j c) -> p j c", j=PACK)
+                rows = w1[PASS * a : PASS * (a + 1), P * t : P * (t + 1)]
+                nc.sync.dma_start(out=part, in_=rows.rearrange("(p j) c -> p j c", j=PACK))
+                weave(grouped[:, PASS * a : PASS * (a + 1)], part)
+                w1_codes[a, 0, t] = codes[:, P * a : P * (a + 1)]
+                w1_sc[a, 0, t] = scales[:, P * a : P * (a + 1)]
+            nc.vector.quantize_mx(out=codes[:].bitcast(FP8X4), scales=scales[:], in_=grouped[:])
+
+        def prep_w1_planes(a):
+            raw = tile([P, PACK, PASS], F32, "B%d" % a, "w1_raw1%d" % a)
+            rows = w1[PASS * a : PASS * (a + 1), PASS : 2 * PASS]
+            nc.sync.dma_start(out=raw[:], in_=rows.rearrange("(p j) c -> p j c", j=PACK))
+            grouped = tile([P, PASS * PACK], BF16, "wb%d" % a, "w1_b1%d" % a)
+            codes = tile([P, PASS], U32, "wc1%d" % a, "w1_codes1%d" % a)
+            scales = tile([P, PASS], U8, "ws1%d" % a, "w1_sc1%d" % a)
+            nc.scalar.copy(
+                out=grouped[:].rearrange("p (t m j) -> p t m j", t=PACK, j=PACK),
+                in_=raw[:].rearrange("p j (m t) -> p t m j", t=PACK),
             )
+            nc.vector.quantize_mx(out=codes[:].bitcast(FP8X4), scales=scales[:], in_=grouped[:])
+            for i in range(PACK):
+                w1_codes[a, 1, i] = codes[:, P * i : P * (i + 1)]
+                w1_sc[a, 1, i] = scales[:, P * i : P * (i + 1)]
 
         pages = {}
-        hx = tile([P, (2 * PACK + 1) * S], F32, "hx", "hx")
 
         def load_page(b, i):
             page = tile([P, T2], F32, "P%d%d" % (b, i), "page%d%d" % (b, i))
-            rows = page0[PASS * b : PASS * (b + 1), :].rearrange("(p i) t -> p i t", i=PACK)
-            nc.sync.dma_start(out=page[:], in_=rows[:, i, :])
+            if b == 0:
+                rows = page0[P * i : P * (i + 1), :]
+            else:
+                rows = page0[PASS : 2 * PASS, :].rearrange("(p i) t -> p i t", i=PACK)[:, i, :]
+            nc.sync.dma_start(out=page[:], in_=rows)
             pages[b, i] = page
 
-        def refresh(b, i, pieces=1):
-            h = hx[:, S * (PACK * b + i) : S * (PACK * b + i + 1)]
+        hs = {}
+
+        def features(b, i):
+            h = tile([P, S], F32, "h%d" % ((PACK * b + i) % 3), "h%d%d" % (b, i))
+            bias = b1_rows if b == 0 else b1_planes
             for c in range(2):
                 acc = psum.tile([P, BANK], F32, tag="acc", name="acc_h")
                 for a in range(2):
                     nc.tensor.matmul_mx(
                         out=acc[:],
-                        lhsT=w1_codes[a, b][:, P * i : P * (i + 1)].bitcast(FP8X4),
-                        lhsT_scale=w1_sc[a, b][:, P * i : P * (i + 1)],
+                        lhsT=w1_codes[a, b, i].bitcast(FP8X4),
+                        lhsT_scale=w1_sc[a, b, i],
                         rhs=v_codes[a][:, BANK * c : BANK * (c + 1)].bitcast(FP8X4),
                         rhs_scale=v_sc[4 * a : P, BANK * c : BANK * (c + 1)],
                         start=(a == 0),
                         stop=(a == 1),
                     )
                 nc.scalar.activation(
-                    out=h[:, BANK * c : BANK * (c + 1)], in_=acc[:], func=ACT.Identity, bias=b1_sb[:, b, i : i + 1]
+                    out=h[:, BANK * c : BANK * (c + 1)], in_=acc[:], func=ACT.Identity, bias=bias[:, i : i + 1]
                 )
-            width = S // pieces
-            for u in range(pieces):
-                nc.vector.tensor_tensor(
-                    pages[b, i][:].indirect(idx2[:, width // 16 * u : width // 16 * (u + 1)]),
-                    h[:, width * u : width * (u + 1)],
-                    gains[i // 2][:, i % 2, width * u : width * (u + 1)],
-                    MULT,
-                )
+            hs[b, i] = h
 
-        x_last = tile([P, PACK * BANK], F32, "G1", "x_last")
+        def put(b, i, lo, hi):
+            gain = gains_rows[:] if b == 0 else gains[i // 2][:, i % 2, :]
+            nc.vector.tensor_tensor(
+                pages[b, i][:].indirect(idx2[:, lo // 16 : hi // 16]), hs[b, i][:, lo:hi], gain[:, lo:hi], MULT
+            )
+
+        x_near = tile([P, (PACK + 1) * BANK], F32, "XN", "x_near")
+        xt = {}
+        x_rows = {}
 
         def x_planes(b, c):
-            if (b, c) == (1, 1):
-                return x_last[:].rearrange("p (t m) -> p t m", t=PACK)
-            first = S * (PACK * b + 1)
-            return hx[:, first : first + PACK * S].rearrange("p (t m) -> p t m", t=PACK)[:, :, BANK * c : BANK * (c + 1)]
+            if b == 0:
+                return xt["first"][:, :, BANK * c : BANK * (c + 1)]
+            if c == 0:
+                return x_near[:, BANK:].rearrange("p (t m) -> p t m", t=PACK)
+            return xt["last"][:, 0 : PACK * BANK].rearrange("p (t m) -> p t m", t=PACK)
 
-        def fetch_whole(i):
-            first = S * (i + 1)
-            nc.vector.tensor_copy(hx[:, first : first + M], pages[0, i][:].indirect(idx3[:]))
+        def fetch_rows(t, slot):
+            rows = tile([P, M], F32, slot, "x_rows%d" % t)
+            nc.vector.tensor_copy(rows[:], pages[0, t][:].indirect(idx3[:]))
+            x_rows[t] = rows
 
-        def fetch(b, i, c):
+        def deal_rows(t):
+            nc.sync.dma_start(
+                out=xt["first"][QUAD * t : QUAD * (t + 1)].rearrange("p i m -> p (i m)"), in_=x_rows[t][:]
+            )
+
+        def fetch(i, c):
             nc.vector.tensor_copy(
-                x_planes(b, c)[:, i, :],
-                pages[b, i][:].indirect(idx3[:, LIST_COLS * c : LIST_COLS * (c + 1)]),
+                x_planes(1, c)[:, i, :],
+                pages[1, i][:].indirect(idx3[:, LIST_COLS * c : LIST_COLS * (c + 1)]),
             )
 
         x_codes = {}
@@ -179,39 +193,27 @@ def tile_list_playlist_slot_refresh_kernel(
             x_codes[b, c] = codes
             x_sc[b, c] = scales
 
-        w3_codes = {}
-        w3_sc = {}
+        w3_codes = [tile([P, N], U32, "w3c%d" % b, "w3_codes%d" % b) for b in range(2)]
+        w3_sc = [tile([P, N], U8, "w3s%d" % b, "w3_sc%d" % b) for b in range(2)]
 
-        def prep_w3(b):
-            raw = tile([P, PACK, N], F32, "A%d" % b, "w3_raw%d" % b)
-            nc.sync.dma_start(out=raw[:], in_=w3[PASS * b : PASS * (b + 1), :].rearrange("(p j) n -> p j n", j=PACK))
-            grouped = tile([P, N * PACK], BF16, "zb%d" % b, "w3_b%d" % b)
-            nc.scalar.copy(out=woven(grouped[:]), in_=planes(raw[:]))
-            codes = tile([P, N], U32, "w3c%d" % b, "w3_codes%d" % b)
-            scales = tile([P, N], U8, "w3s%d" % b, "w3_sc%d" % b)
-            nc.vector.quantize_mx(out=codes[:].bitcast(FP8X4), scales=scales[:], in_=grouped[:])
-            w3_codes[b] = codes
-            w3_sc[b] = scales
+        w3_raw = {}
 
-        load_page(0, 0)
-        load_gains(0, 1, 0, BANK)
-        load_gains(0, 1, BANK, S)
-        refresh(0, 0, 2)
-        nc.sync.dma_start(idx3[:], offs3)
-        load_page(0, 1)
-        load_gains(1, 2, 0, S)
-        refresh(0, 1)
-        fetch_whole(0)
-        load_page(0, 2)
-        load_gains(2, 4, 0, S)
-        refresh(0, 2)
-        fetch_whole(1)
-        prep_w1(0, 1, (0, 4))
-        prep_w1(1, 1, (0, 4))
-        load_page(0, 3)
-        refresh(0, 3)
-        fetch_whole(2)
-        nc.sync.dma_start(out=b2_sb[:], in_=b2.rearrange("(a p i) -> p a i", a=2, i=PACK))
+        def load_w3(b, u, raw):
+            part = raw.rearrange("p (j n) -> p j n", j=PACK)
+            rows = w3[PASS * b : PASS * (b + 1), HALF * u : HALF * (u + 1)]
+            nc.sync.dma_start(out=part, in_=rows.rearrange("(p j) n -> p j n", j=PACK))
+            w3_raw[b, u] = part
+
+        def prep_w3(b, u):
+            part = w3_raw[b, u]
+            grouped = tile([P, HALF * PACK], BF16, "sb%d" % u, "w3_b%d%d" % (b, u))
+            weave(grouped[:], part)
+            nc.vector.quantize_mx(
+                out=w3_codes[b][:, HALF * u : HALF * (u + 1)].bitcast(FP8X4),
+                scales=w3_sc[b][:, HALF * u : HALF * (u + 1)],
+                in_=grouped[:],
+            )
+
         w2_raw = tile([P, 2, 2 * H], U8, "w2_raw", "w2_raw")
         nc.sync.dma_start(out=w2_raw[:].bitcast(I32), in_=w2_words.rearrange("a p c -> p a c").bitcast(I32))
         w2_codes = tile([P, 2, 2 * H], U8, "w2_codes", "w2_codes")
@@ -220,7 +222,24 @@ def tile_list_playlist_slot_refresh_kernel(
             out=w2_codes[:].rearrange("p a c -> p (a c)").bitcast(U16).rearrange("p (g t m) -> p g t m", t=PACK, m=P),
             in_=w2_raw[:].rearrange("p a c -> p (a c)").bitcast(U16).rearrange("p (g m t) -> p g t m", t=PACK, m=P),
         )
-
+        load_tab(0)
+        nc.sync.dma_start(idx[:], offs)
+        for q in range(4):
+            nc.sync.dma_start(
+                out=tab_sc[QUAD * q : QUAD * q + 8, :].bitcast(I32),
+                in_=tab_scales[:, 4 * q : 4 * q + 4, :].bitcast(I32),
+            )
+        nc.vector.tensor_copy(v_codes[0][:], tab_window(0).indirect(idx[:]))
+        nc.vector.tensor_copy(v_sc[:], tab_sc[:].indirect(idx[:]))
+        prep_w1_rows(0)
+        with nc.allow_non_contiguous_dma(reason="one bias value for each partition and block of 128 channels"):
+            nc.sync.dma_start(out=b1_rows[:], in_=b1[0:PASS].rearrange("(t p) -> p t", p=P))
+        load_tab(1)
+        for c in range(2):
+            nc.vector.tensor_copy(
+                v_codes[1][:, BANK * c : BANK * (c + 1)],
+                tab_window(1).indirect(idx[:, LIST_COLS * c : LIST_COLS * (c + 1)]),
+            )
         for q in range(4):
             nc.sync.dma_start(
                 out=w2_sc_raw[QUAD * q : QUAD * q + 4, :, :].bitcast(I32),
@@ -230,45 +249,99 @@ def tile_list_playlist_slot_refresh_kernel(
             out=w2_sc[:].rearrange("p a (b t m) -> p (a b) t m", t=PACK, m=P),
             in_=w2_sc_raw[:].rearrange("p a (b m t) -> p (a b) t m", t=PACK, m=P),
         )
-        prep_w3(0)
-        prep_w3(1)
+        xt["first"] = tile([P, PACK, M], F32, "A", "x_first")
+        nc.sync.dma_start(idx2[:], offs2)
+        load_page(0, 0)
+        nc.sync.dma_start(out=gains_rows[:, 0:BANK], in_=wgs[:, 0:BANK])
+        features(0, 0)
+        put(0, 0, 0, BANK)
+        prep_w1_rows(1)
+        features(0, 1)
+        prep_w1_rows(2)
+        nc.sync.dma_start(out=gains_rows[:, BANK:S], in_=wgs[:, BANK:S])
+        put(0, 0, BANK, S)
+        features(0, 2)
+        prep_w1_rows(3)
+        features(0, 3)
+        nc.sync.dma_start(idx3[:], offs3)
+        load_page(0, 1)
+        put(0, 1, 0, S)
+        prep_w1_planes(0)
+        fetch_rows(0, "B0")
+        load_page(0, 2)
+        put(0, 2, 0, S)
+        nc.sync.dma_start(out=b1_planes[:], in_=b1[PASS : 2 * PASS].rearrange("(p i) -> p i", i=PACK))
+        nc.sync.dma_start(out=b2_sb[:], in_=b2.rearrange("(a p i) -> p a i", a=2, i=PACK))
+        prep_w1_planes(1)
+        fetch_rows(1, "B1")
+        features(1, 0)
+        load_page(0, 3)
+        put(0, 3, 0, S)
+        w3_raw0 = tile([P, PACK * HALF], F32, "R0", "w3_raw0")
+        load_w3(0, 0, w3_raw0[:])
+        prep_w3(0, 0)
+        fetch_rows(2, "R0")
+        features(1, 1)
+        load_gains(0)
         load_page(1, 0)
-        refresh(1, 0)
-        fetch_whole(3)
-        for i in range(1, PACK):
-            load_page(1, i)
-            refresh(1, i)
-            if i < 3:
-                xb = tile([P, BANK * PACK], BF16, "wb%d" % (i - 1), "xb0%d" % (i - 1))
-                nc.scalar.copy(out=woven(xb[:]), in_=planes(x_planes(0, i - 1)))
-                quant_x(0, i - 1, xb[:])
-            fetch(1, i - 1, 0)
-        fetch(1, PACK - 1, 0)
-        xb10 = x_last[:, 2 * BANK : 4 * BANK].bitcast(BF16)
-        nc.scalar.copy(out=woven(xb10), in_=planes(x_planes(1, 0)))
-        fetch(1, 0, 1)
-        fetch(1, 1, 1)
+        put(1, 0, 0, S)
+        w3_raw3 = tile([P, PACK * HALF], F32, "R1", "w3_raw3")
+        load_w3(1, 1, w3_raw3[:])
+        prep_w3(1, 1)
+        fetch_rows(3, "R1")
+        load_gains(1)
+        load_page(1, 1)
+        deal_rows(0)
+        deal_rows(1)
+        load_w3(0, 1, x_near[:, 0 : 2 * BANK])
+        load_gains(2)
+        load_page(1, 2)
+        deal_rows(2)
+        deal_rows(3)
+        load_w3(1, 0, x_near[:, 2 * BANK : 4 * BANK])
+        load_gains(3)
+        load_page(1, 3)
+        put(1, 1, 0, S)
+        prep_w3(0, 1)
+        features(1, 2)
+        fetch(0, 0)
+        put(1, 2, 0, S)
+        prep_w3(1, 0)
+        features(1, 3)
+        fetch(1, 0)
+        fetch(2, 0)
+        for c in range(2):
+            xb = tile([P, BANK * PACK], BF16, "wb%d" % c, "xb0%d" % c)
+            weave(xb[:], x_planes(0, c))
+            quant_x(0, c, xb[:])
+        put(1, 3, 0, S)
+        xt["last"] = tile([P, (PACK + 1) * BANK], F32, "G1", "x_last")
+        fetch(0, 1)
+        fetch(3, 0)
+        xb10 = xt["last"][:, 3 * BANK : 5 * BANK].bitcast(BF16)
+        weave(xb10, x_planes(1, 0))
+        fetch(1, 1)
+        fetch(2, 1)
         quant_x(1, 0, xb10)
-        fetch(1, 2, 1)
-        fetch(1, 3, 1)
+        fetch(3, 1)
         xb11 = tile([P, BANK * PACK], BF16, "wb0", "xb11")
         nc.vector.tensor_copy(out=woven(xb11[:]), in_=planes(x_planes(1, 1)))
         quant_x(1, 1, xb11[:])
 
         gates = {}
         zbs = {}
-        zps = {}
         z_codes = {}
         z_sc = {}
 
         def gate(b, c):
             g = tile([P, PACK, BANK], F32, "P0%d" % (2 * c + b), "gate%d%d" % (b, c))
-            for i in range(PACK):
-                acc = psum.tile([P, BANK], F32, tag="acc", name="acc_g")
-                col = PASS * b + P * i
-                for a in range(2):
+            banks = "acc" if b == 0 else "out"
+            accs = [psum.tile([P, BANK], F32, tag=banks, name="acc_g%d" % i) for i in range(PACK)]
+            for a in range(2):
+                for i in range(PACK):
+                    col = PASS * b + P * i
                     nc.tensor.matmul_mx(
-                        out=acc[:],
+                        out=accs[i][:],
                         lhsT=w2_codes[:, a, 2 * col : 2 * (col + P)].bitcast(FP4X4),
                         lhsT_scale=w2_sc[:, a, col : col + P],
                         rhs=x_codes[a, c][:].bitcast(FP8X4),
@@ -276,42 +349,36 @@ def tile_list_playlist_slot_refresh_kernel(
                         start=(a == 0),
                         stop=(a == 1),
                     )
-                nc.scalar.activation(out=g[:, i, :], in_=acc[:], func=ACT.Sigmoid, bias=b2_sb[:, b, i : i + 1])
+            for i in range(PACK):
+                nc.scalar.activation(out=g[:, i, :], in_=accs[i][:], func=ACT.Sigmoid, bias=b2_sb[:, b, i : i + 1])
             gates[b, c] = g
-            zbs[b, c] = tile([P, BANK * PACK], BF16, "zb%d" % b, "zb%d%d" % (b, c))
-            z_codes[b, c] = tile([P, BANK], U32, "wc%d%d" % (b, c), "z_codes%d%d" % (b, c))
-            z_sc[b, c] = tile([P, BANK], U8, "ws%d%d" % (b, c), "z_sc%d%d" % (b, c))
+            zbs[b, c] = tile([P, BANK * PACK], BF16, ("zb%d" % b if c == 0 else "wb%d" % (1 - b)), "zb%d%d" % (b, c))
+            z_codes[b, c] = tile([P, BANK], U32, ("wc1%d" if c == 0 else "v%d") % b, "z_codes%d%d" % (b, c))
+            z_sc[b, c] = tile([P, BANK], U8, "zs%d%d" % (b, c), "z_sc%d%d" % (b, c))
 
-        def gated(b, c, lo, hi, slot):
-            zps[b, c, lo] = tile([P, 2, hi - lo, 2], BF16, slot, "zp%d%d%d" % (b, c, lo))
+        def gated(b, c, lo, hi):
             nc.vector.tensor_tensor(
-                zps[b, c, lo][:],
-                x_planes(b, c)[:, :, lo:hi].rearrange("p (u e) m -> p u m e", e=2),
-                gates[b, c][:, :, lo:hi].rearrange("p (u e) m -> p u m e", e=2),
+                zbs[b, c][:, PACK * lo : PACK * hi].rearrange("p (m e t) -> p m t e", e=2, t=PACK),
+                x_planes(b, c)[:, :, lo:hi].rearrange("p t (m e) -> p m t e", e=2),
+                gates[b, c][:, :, lo:hi].rearrange("p t (m e) -> p m t e", e=2),
                 MULT,
             )
 
-        def quant_z(b, c, lo, hi, last=False):
-            pairs = zps[b, c, lo][:].rearrange("p u m e -> p (u m e)").bitcast(F32).rearrange("p (u m) -> p m u", u=2)
-            words = zbs[b, c][:].bitcast(F32).rearrange("p (m u) -> p m u", u=2)
-            if last:
-                nc.vector.tensor_copy(out=words[:, lo:hi, :], in_=pairs)
-            else:
-                nc.scalar.copy(out=words[:, lo:hi, :], in_=pairs)
+        def quant_z(b, c, lo, hi):
             nc.vector.quantize_mx(
                 out=z_codes[b, c][:, lo:hi].bitcast(FP8X4),
                 scales=z_sc[b, c][:, lo:hi],
                 in_=zbs[b, c][:, PACK * lo : PACK * hi],
             )
 
-        staged = [tile([P, N // P, BANK], F32, "A%d" % c, "staged%d" % c) for c in range(2)]
+        staged = [tile([P, N // P, BANK], F32, "P1%d" % c, "staged%d" % c) for c in range(2)]
 
         def scores(c, lo, hi, banks, shared):
-            for n in range(N // P):
-                acc = psum.tile([P, hi - lo], F32, tag=banks, name="acc_o")
-                for b in range(2):
+            accs = [psum.tile([P, hi - lo], F32, tag=banks, name="acc_o%d" % n) for n in range(N // P)]
+            for b in range(2):
+                for n in range(N // P):
                     nc.tensor.matmul_mx(
-                        out=acc[:],
+                        out=accs[n][:],
                         lhsT=w3_codes[b][:, P * n : P * (n + 1)].bitcast(FP8X4),
                         lhsT_scale=w3_sc[b][:, P * n : P * (n + 1)],
                         rhs=z_codes[b, c][:, lo:hi].bitcast(FP8X4),
@@ -319,28 +386,29 @@ def tile_list_playlist_slot_refresh_kernel(
                         start=(b == 0),
                         stop=(b == 1),
                     )
+            for n in range(N // P):
                 if shared and n % 2 == 1:
-                    nc.vector.tensor_copy(out=staged[c][:, n, lo:hi], in_=acc[:])
+                    nc.vector.tensor_copy(out=staged[c][:, n, lo:hi], in_=accs[n][:])
                 else:
-                    nc.scalar.copy(out=staged[c][:, n, lo:hi], in_=acc[:])
+                    nc.scalar.copy(out=staged[c][:, n, lo:hi], in_=accs[n][:])
                 nc.sync.dma_start(
                     out=out[P * n : P * (n + 1), BANK * c + lo : BANK * c + hi], in_=staged[c][:, n, lo:hi]
                 )
 
         gate(0, 0)
         gate(1, 0)
-        gated(0, 0, 0, BANK, "wb1")
-        gated(1, 0, 0, BANK, "wb0")
+        gated(0, 0, 0, BANK)
+        gated(1, 0, 0, BANK)
         quant_z(0, 0, 0, BANK)
         gate(0, 1)
-        gated(0, 1, 0, BANK, "wb1")
+        gated(0, 1, 0, BANK)
         quant_z(1, 0, 0, BANK)
         gate(1, 1)
-        gated(1, 1, 0, HALF, "wb0")
+        gated(1, 1, 0, HALF)
         quant_z(0, 1, 0, BANK)
-        gated(1, 1, HALF, BANK, "wb1")
+        gated(1, 1, HALF, BANK)
         quant_z(1, 1, 0, HALF)
-        quant_z(1, 1, HALF, BANK, last=True)
-        scores(0, 0, BANK, "out", False)
+        quant_z(1, 1, HALF, BANK)
+        scores(0, 0, BANK, "acc", False)
         scores(1, 0, HALF, "out", False)
         scores(1, HALF, BANK, "acc", True)

@@ -87,19 +87,34 @@ def tile_list_playlist_slot_refresh_kernel(
         def tab_window(a):
             return tab_w[:, T * a : T * (a + 1)].bitcast(U32)
 
-        def prep_w1_rows(t):
-            raw = tile([P, 2 * PACK * P], F32, "R%d" % t, "w1_raw0%d" % t)
-            grouped = tile([P, 2 * PACK * P], BF16, "sb%d" % (t % 2), "w1_b0%d" % t)
-            codes = tile([P, 2 * P], U32, "wc0%d" % t, "w1_codes0%d" % t)
-            scales = tile([P, 2 * P], U8, "ws0%d" % t, "w1_sc0%d" % t)
+        w1_raw = {}
+
+        def load_w1_rows(t0, t1, a):
+            if a == 0:
+                w1_raw[t0] = tile([P, 2, PACK * P * (t1 - t0)], F32, "R%d" % t0, "w1_raw0%d" % t0)
+            rows = w1[PASS * a : PASS * (a + 1), P * t0 : P * t1]
+            nc.sync.dma_start(
+                out=w1_raw[t0][:, a, :].rearrange("p (j c) -> p j c", j=PACK),
+                in_=rows.rearrange("(p j) c -> p j c", j=PACK),
+            )
+
+        def prep_w1_rows(t0, t1, slot):
+            blocks = t1 - t0
+            grouped = tile([P, blocks, 2, PASS], BF16, slot, "w1_b0%d" % t0)
+            codes = tile([P, blocks * 2 * P], U32, "wc0%d" % t0, "w1_codes0%d" % t0)
+            scales = tile([P, blocks * 2 * P], U8, "ws0%d" % t0, "w1_sc0%d" % t0)
             for a in range(2):
-                part = raw[:, PASS * a : PASS * (a + 1)].rearrange("p (j c) -> p j c", j=PACK)
-                rows = w1[PASS * a : PASS * (a + 1), P * t : P * (t + 1)]
-                nc.sync.dma_start(out=part, in_=rows.rearrange("(p j) c -> p j c", j=PACK))
-                weave(grouped[:, PASS * a : PASS * (a + 1)], part)
-                w1_codes[a, 0, t] = codes[:, P * a : P * (a + 1)]
-                w1_sc[a, 0, t] = scales[:, P * a : P * (a + 1)]
-            nc.vector.quantize_mx(out=codes[:].bitcast(FP8X4), scales=scales[:], in_=grouped[:])
+                nc.scalar.copy(
+                    out=grouped[:, :, a, :].rearrange("p t (c i j) -> p t c j i", i=PACK, j=PACK),
+                    in_=w1_raw[t0][:, a, :].rearrange("p (j t c i) -> p t c j i", j=PACK, t=blocks, i=PACK),
+                )
+                for t in range(t0, t1):
+                    first = P * (2 * (t - t0) + a)
+                    w1_codes[a, 0, t] = codes[:, first : first + P]
+                    w1_sc[a, 0, t] = scales[:, first : first + P]
+            nc.vector.quantize_mx(
+                out=codes[:].bitcast(FP8X4), scales=scales[:], in_=grouped[:].rearrange("p t a k -> p (t a k)")
+            )
 
         def prep_w1_planes(a):
             raw = tile([P, PACK, PASS], F32, "B%d" % a, "w1_raw1%d" % a)
@@ -108,10 +123,11 @@ def tile_list_playlist_slot_refresh_kernel(
             grouped = tile([P, PASS * PACK], BF16, "wb%d" % a, "w1_b1%d" % a)
             codes = tile([P, PASS], U32, "wc1%d" % a, "w1_codes1%d" % a)
             scales = tile([P, PASS], U8, "ws1%d" % a, "w1_sc1%d" % a)
-            nc.scalar.copy(
-                out=grouped[:].rearrange("p (t m j) -> p t m j", t=PACK, j=PACK),
-                in_=raw[:].rearrange("p j (m t) -> p t m j", t=PACK),
-            )
+            for u in range(2):
+                nc.scalar.copy(
+                    out=grouped[:].rearrange("p (u e m j) -> p u m j e", u=2, e=2, j=PACK)[:, u],
+                    in_=raw[:].rearrange("p j (m u e) -> p u m j e", u=2, e=2)[:, u],
+                )
             nc.vector.quantize_mx(out=codes[:].bitcast(FP8X4), scales=scales[:], in_=grouped[:])
             for i in range(PACK):
                 w1_codes[a, 1, i] = codes[:, P * i : P * (i + 1)]
@@ -198,21 +214,20 @@ def tile_list_playlist_slot_refresh_kernel(
 
         w3_raw = {}
 
-        def load_w3(b, u, raw):
+        def load_w3(b, lo, hi, raw):
             part = raw.rearrange("p (j n) -> p j n", j=PACK)
-            rows = w3[PASS * b : PASS * (b + 1), HALF * u : HALF * (u + 1)]
+            rows = w3[PASS * b : PASS * (b + 1), lo:hi]
             nc.sync.dma_start(out=part, in_=rows.rearrange("(p j) n -> p j n", j=PACK))
-            w3_raw[b, u] = part
+            w3_raw[b, lo] = part
 
-        def prep_w3(b, u):
-            part = w3_raw[b, u]
-            grouped = tile([P, HALF * PACK], BF16, "sb%d" % u, "w3_b%d%d" % (b, u))
-            weave(grouped[:], part)
-            nc.vector.quantize_mx(
-                out=w3_codes[b][:, HALF * u : HALF * (u + 1)].bitcast(FP8X4),
-                scales=w3_sc[b][:, HALF * u : HALF * (u + 1)],
-                in_=grouped[:],
-            )
+        def stage_w3(b, lo, hi, slot):
+            raw = tile([P, PACK * (hi - lo)], F32, slot, "w3_raw%d%d" % (b, lo))
+            load_w3(b, lo, hi, raw[:])
+
+        def prep_w3(b, lo, hi, slot):
+            grouped = tile([P, (hi - lo) * PACK], BF16, slot, "w3_b%d%d" % (b, lo))
+            weave(grouped[:], w3_raw[b, lo])
+            nc.vector.quantize_mx(out=w3_codes[b][:, lo:hi].bitcast(FP8X4), scales=w3_sc[b][:, lo:hi], in_=grouped[:])
 
         w2_raw = tile([P, 2, 2 * H], U8, "w2_raw", "w2_raw")
         nc.sync.dma_start(out=w2_raw[:].bitcast(I32), in_=w2_words.rearrange("a p c -> p a c").bitcast(I32))
@@ -231,7 +246,9 @@ def tile_list_playlist_slot_refresh_kernel(
             )
         nc.vector.tensor_copy(v_codes[0][:], tab_window(0).indirect(idx[:]))
         nc.vector.tensor_copy(v_sc[:], tab_sc[:].indirect(idx[:]))
-        prep_w1_rows(0)
+        load_w1_rows(0, 1, 0)
+        load_w1_rows(0, 1, 1)
+        prep_w1_rows(0, 1, "sb0")
         with nc.allow_non_contiguous_dma(reason="one bias value for each partition and block of 128 channels"):
             nc.sync.dma_start(out=b1_rows[:], in_=b1[0:PASS].rearrange("(t p) -> p t", p=P))
         load_tab(1)
@@ -255,58 +272,62 @@ def tile_list_playlist_slot_refresh_kernel(
         nc.sync.dma_start(out=gains_rows[:, 0:BANK], in_=wgs[:, 0:BANK])
         features(0, 0)
         put(0, 0, 0, BANK)
-        prep_w1_rows(1)
+        load_w1_rows(1, 2, 0)
+        load_w1_rows(1, 2, 1)
+        prep_w1_rows(1, 2, "sb1")
         features(0, 1)
-        prep_w1_rows(2)
+        load_w1_rows(2, 3, 0)
+        load_w1_rows(2, 3, 1)
         nc.sync.dma_start(out=gains_rows[:, BANK:S], in_=wgs[:, BANK:S])
         put(0, 0, BANK, S)
+        prep_w1_rows(2, 3, "sb0")
         features(0, 2)
-        prep_w1_rows(3)
-        features(0, 3)
-        nc.sync.dma_start(idx3[:], offs3)
         load_page(0, 1)
         put(0, 1, 0, S)
-        prep_w1_planes(0)
-        fetch_rows(0, "B0")
+        nc.sync.dma_start(idx3[:], offs3)
+        load_w1_rows(3, 4, 0)
+        load_w1_rows(3, 4, 1)
+        prep_w1_rows(3, 4, "sb1")
+        fetch_rows(0, "R3")
+        features(0, 3)
         load_page(0, 2)
         put(0, 2, 0, S)
         nc.sync.dma_start(out=b1_planes[:], in_=b1[PASS : 2 * PASS].rearrange("(p i) -> p i", i=PACK))
         nc.sync.dma_start(out=b2_sb[:], in_=b2.rearrange("(a p i) -> p a i", a=2, i=PACK))
+        prep_w1_planes(0)
         prep_w1_planes(1)
         fetch_rows(1, "B1")
         features(1, 0)
         load_page(0, 3)
         put(0, 3, 0, S)
-        w3_raw0 = tile([P, PACK * HALF], F32, "R0", "w3_raw0")
-        load_w3(0, 0, w3_raw0[:])
-        prep_w3(0, 0)
+        stage_w3(0, 0, HALF, "R0")
+        prep_w3(0, 0, HALF, "sb0")
         fetch_rows(2, "R0")
         features(1, 1)
         load_gains(0)
         load_page(1, 0)
         put(1, 0, 0, S)
-        w3_raw3 = tile([P, PACK * HALF], F32, "R1", "w3_raw3")
-        load_w3(1, 1, w3_raw3[:])
-        prep_w3(1, 1)
+        stage_w3(0, HALF, N, "R1")
+        prep_w3(0, HALF, N, "sb1")
         fetch_rows(3, "R1")
         load_gains(1)
         load_page(1, 1)
         deal_rows(0)
         deal_rows(1)
-        load_w3(0, 1, x_near[:, 0 : 2 * BANK])
+        load_w3(1, HALF, N, x_near[:, 0 : 2 * BANK])
         load_gains(2)
         load_page(1, 2)
         deal_rows(2)
         deal_rows(3)
-        load_w3(1, 0, x_near[:, 2 * BANK : 4 * BANK])
+        load_w3(1, 0, HALF, x_near[:, 2 * BANK : 4 * BANK])
         load_gains(3)
         load_page(1, 3)
         put(1, 1, 0, S)
-        prep_w3(0, 1)
+        prep_w3(1, HALF, N, "sb0")
         features(1, 2)
         fetch(0, 0)
         put(1, 2, 0, S)
-        prep_w3(1, 0)
+        prep_w3(1, 0, HALF, "sb1")
         features(1, 3)
         fetch(1, 0)
         fetch(2, 0)
@@ -395,6 +416,26 @@ def tile_list_playlist_slot_refresh_kernel(
                     out=out[P * n : P * (n + 1), BANK * c + lo : BANK * c + hi], in_=staged[c][:, n, lo:hi]
                 )
 
+        def last_scores(lo, engines):
+            accs = [psum.tile([P, 2, P], F32, tag="acc", name="acc_l%d" % u) for u in range(2)]
+            for n, b in ((0, 0), (2, 0), (0, 1), (2, 1), (1, 0), (1, 1), (3, 0), (3, 1)):
+                nc.tensor.matmul_mx(
+                    out=accs[n // 2][:, n % 2, :],
+                    lhsT=w3_codes[b][:, P * n : P * (n + 1)].bitcast(FP8X4),
+                    lhsT_scale=w3_sc[b][:, P * n : P * (n + 1)],
+                    rhs=z_codes[b, 1][:, lo : lo + P].bitcast(FP8X4),
+                    rhs_scale=z_sc[b, 1][:, lo : lo + P],
+                    start=(b == 0),
+                    stop=(b == 1),
+                )
+            for u in range(2):
+                engines[u](out=staged[1][:, 2 * u : 2 * u + 2, lo : lo + P], in_=accs[u][:])
+                rows = out[2 * P * u : 2 * P * (u + 1), BANK + lo : BANK + lo + P]
+                nc.sync.dma_start(
+                    out=rows.rearrange("(n p) m -> p n m", p=P), in_=staged[1][:, 2 * u : 2 * u + 2, lo : lo + P]
+                )
+
+        last = BANK - P
         gate(0, 0)
         gate(1, 0)
         gated(0, 0, 0, BANK)
@@ -406,9 +447,12 @@ def tile_list_playlist_slot_refresh_kernel(
         gate(1, 1)
         gated(1, 1, 0, HALF)
         quant_z(0, 1, 0, BANK)
-        gated(1, 1, HALF, BANK)
+        gated(1, 1, HALF, last)
         quant_z(1, 1, 0, HALF)
-        quant_z(1, 1, HALF, BANK)
+        gated(1, 1, last, BANK)
+        quant_z(1, 1, HALF, last)
+        quant_z(1, 1, last, BANK)
         scores(0, 0, BANK, "acc", False)
         scores(1, 0, HALF, "out", False)
-        scores(1, HALF, BANK, "acc", True)
+        last_scores(HALF, (nc.scalar.copy, nc.scalar.copy))
+        last_scores(last, (nc.scalar.copy, nc.vector.tensor_copy))

@@ -61,7 +61,8 @@ def tile_list_playlist_slot_refresh_kernel(
         nc.gpsimd.memset(warm[:], 0.0)
         warmed = tile([P, 1], F32, "warmed", "warmed")
         nc.scalar.activation(out=warmed[:], in_=warm[:], func=ACT.Sigmoid)
-        b1_rows = tile([P, PACK], F32, "b1r", "b1_rows")
+        b1_first = tile([P, 1], F32, "b1f", "b1_first")
+        b1_rows = tile([P, PACK - 1], F32, "b1r", "b1_rows")
         b1_planes = tile([P, PACK], F32, "b1p", "b1_planes")
         b2_sb = tile([P, 2, PACK], F32, "b2", "b2_sb")
 
@@ -123,11 +124,10 @@ def tile_list_playlist_slot_refresh_kernel(
             grouped = tile([P, PASS * PACK], BF16, "wb%d" % a, "w1_b1%d" % a)
             codes = tile([P, PASS], U32, "wc1%d" % a, "w1_codes1%d" % a)
             scales = tile([P, PASS], U8, "ws1%d" % a, "w1_sc1%d" % a)
-            for u in range(2):
-                nc.scalar.copy(
-                    out=grouped[:].rearrange("p (u e m j) -> p u m j e", u=2, e=2, j=PACK)[:, u],
-                    in_=raw[:].rearrange("p j (m u e) -> p u m j e", u=2, e=2)[:, u],
-                )
+            nc.scalar.copy(
+                out=grouped[:].rearrange("p (t m j) -> p t m j", t=PACK, j=PACK),
+                in_=raw[:].rearrange("p j (m t) -> p t m j", t=PACK),
+            )
             nc.vector.quantize_mx(out=codes[:].bitcast(FP8X4), scales=scales[:], in_=grouped[:])
             for i in range(PACK):
                 w1_codes[a, 1, i] = codes[:, P * i : P * (i + 1)]
@@ -146,14 +146,14 @@ def tile_list_playlist_slot_refresh_kernel(
 
         hs = {}
 
-        def features(b, i):
-            h = tile([P, S], F32, "h%d" % ((PACK * b + i) % 3), "h%d%d" % (b, i))
-            bias = b1_rows if b == 0 else b1_planes
-            for c in range(2):
-                acc = psum.tile([P, BANK], F32, tag="acc", name="acc_h")
-                for a in range(2):
+        def features(b, i, slot):
+            h = tile([P, S], F32, slot, "h%d%d" % (b, i))
+            bias = b1_planes[:, i : i + 1] if b == 1 else b1_rows[:, i - 1 : i] if i > 0 else b1_first[:]
+            accs = [psum.tile([P, BANK], F32, tag="acc", name="acc_h%d" % c) for c in range(2)]
+            for a in range(2):
+                for c in range(2):
                     nc.tensor.matmul_mx(
-                        out=acc[:],
+                        out=accs[c][:],
                         lhsT=w1_codes[a, b, i].bitcast(FP8X4),
                         lhsT_scale=w1_sc[a, b, i],
                         rhs=v_codes[a][:, BANK * c : BANK * (c + 1)].bitcast(FP8X4),
@@ -161,8 +161,9 @@ def tile_list_playlist_slot_refresh_kernel(
                         start=(a == 0),
                         stop=(a == 1),
                     )
+            for c in range(2):
                 nc.scalar.activation(
-                    out=h[:, BANK * c : BANK * (c + 1)], in_=acc[:], func=ACT.Identity, bias=bias[:, i : i + 1]
+                    out=h[:, BANK * c : BANK * (c + 1)], in_=accs[c][:], func=ACT.Identity, bias=bias
                 )
             hs[b, i] = h
 
@@ -246,11 +247,10 @@ def tile_list_playlist_slot_refresh_kernel(
             )
         nc.vector.tensor_copy(v_codes[0][:], tab_window(0).indirect(idx[:]))
         nc.vector.tensor_copy(v_sc[:], tab_sc[:].indirect(idx[:]))
-        load_w1_rows(0, 1, 0)
-        load_w1_rows(0, 1, 1)
-        prep_w1_rows(0, 1, "sb0")
-        with nc.allow_non_contiguous_dma(reason="one bias value for each partition and block of 128 channels"):
-            nc.sync.dma_start(out=b1_rows[:], in_=b1[0:PASS].rearrange("(t p) -> p t", p=P))
+        load_w1_rows(0, 2, 0)
+        load_w1_rows(0, 2, 1)
+        prep_w1_rows(0, 2, "wb0")
+        nc.sync.dma_start(out=b1_first[:], in_=b1[0:P].rearrange("(p t) -> p t", t=1))
         load_tab(1)
         for c in range(2):
             nc.vector.tensor_copy(
@@ -270,40 +270,36 @@ def tile_list_playlist_slot_refresh_kernel(
         nc.sync.dma_start(idx2[:], offs2)
         load_page(0, 0)
         nc.sync.dma_start(out=gains_rows[:, 0:BANK], in_=wgs[:, 0:BANK])
-        features(0, 0)
+        features(0, 0, "h0")
         put(0, 0, 0, BANK)
-        load_w1_rows(1, 2, 0)
-        load_w1_rows(1, 2, 1)
-        prep_w1_rows(1, 2, "sb1")
-        features(0, 1)
-        load_w1_rows(2, 3, 0)
-        load_w1_rows(2, 3, 1)
         nc.sync.dma_start(out=gains_rows[:, BANK:S], in_=wgs[:, BANK:S])
         put(0, 0, BANK, S)
-        prep_w1_rows(2, 3, "sb0")
-        features(0, 2)
+        with nc.allow_non_contiguous_dma(reason="one bias value for each partition and block of 128 channels"):
+            nc.sync.dma_start(out=b1_rows[:], in_=b1[P:PASS].rearrange("(t p) -> p t", p=P))
+        features(0, 1, "h1")
+        load_w1_rows(2, 4, 0)
+        load_w1_rows(2, 4, 1)
+        prep_w1_rows(2, 4, "wb1")
+        features(0, 2, "h2")
+        features(0, 3, "h0")
         load_page(0, 1)
         put(0, 1, 0, S)
         nc.sync.dma_start(idx3[:], offs3)
-        load_w1_rows(3, 4, 0)
-        load_w1_rows(3, 4, 1)
-        prep_w1_rows(3, 4, "sb1")
-        fetch_rows(0, "R3")
-        features(0, 3)
-        load_page(0, 2)
-        put(0, 2, 0, S)
-        nc.sync.dma_start(out=b1_planes[:], in_=b1[PASS : 2 * PASS].rearrange("(p i) -> p i", i=PACK))
-        nc.sync.dma_start(out=b2_sb[:], in_=b2.rearrange("(a p i) -> p a i", a=2, i=PACK))
-        prep_w1_planes(0)
-        prep_w1_planes(1)
-        fetch_rows(1, "B1")
-        features(1, 0)
-        load_page(0, 3)
-        put(0, 3, 0, S)
         stage_w3(0, 0, HALF, "R0")
         prep_w3(0, 0, HALF, "sb0")
-        fetch_rows(2, "R0")
-        features(1, 1)
+        fetch_rows(0, "R0")
+        load_page(0, 2)
+        put(0, 2, 0, S)
+        prep_w1_planes(0)
+        fetch_rows(1, "B0")
+        nc.sync.dma_start(out=b1_planes[:], in_=b1[PASS : 2 * PASS].rearrange("(p i) -> p i", i=PACK))
+        nc.sync.dma_start(out=b2_sb[:], in_=b2.rearrange("(a p i) -> p a i", a=2, i=PACK))
+        load_page(0, 3)
+        put(0, 3, 0, S)
+        prep_w1_planes(1)
+        fetch_rows(2, "B1")
+        features(1, 0, "R2")
+        features(1, 1, "h1")
         load_gains(0)
         load_page(1, 0)
         put(1, 0, 0, S)
@@ -324,11 +320,11 @@ def tile_list_playlist_slot_refresh_kernel(
         load_page(1, 3)
         put(1, 1, 0, S)
         prep_w3(1, HALF, N, "sb0")
-        features(1, 2)
+        features(1, 2, "h0")
         fetch(0, 0)
         put(1, 2, 0, S)
         prep_w3(1, 0, HALF, "sb1")
-        features(1, 3)
+        features(1, 3, "R2")
         fetch(1, 0)
         fetch(2, 0)
         for c in range(2):
@@ -346,7 +342,10 @@ def tile_list_playlist_slot_refresh_kernel(
         quant_x(1, 0, xb10)
         fetch(3, 1)
         xb11 = tile([P, BANK * PACK], BF16, "wb0", "xb11")
-        nc.vector.tensor_copy(out=woven(xb11[:]), in_=planes(x_planes(1, 1)))
+        nc.vector.tensor_copy(
+            out=xb11[:].rearrange("p (m e t) -> p m t e", e=2, t=PACK),
+            in_=x_planes(1, 1).rearrange("p t (m e) -> p m t e", e=2),
+        )
         quant_x(1, 1, xb11[:])
 
         gates = {}
@@ -416,26 +415,6 @@ def tile_list_playlist_slot_refresh_kernel(
                     out=out[P * n : P * (n + 1), BANK * c + lo : BANK * c + hi], in_=staged[c][:, n, lo:hi]
                 )
 
-        def last_scores(lo, engines):
-            accs = [psum.tile([P, 2, P], F32, tag="acc", name="acc_l%d" % u) for u in range(2)]
-            for n, b in ((0, 0), (2, 0), (0, 1), (2, 1), (1, 0), (1, 1), (3, 0), (3, 1)):
-                nc.tensor.matmul_mx(
-                    out=accs[n // 2][:, n % 2, :],
-                    lhsT=w3_codes[b][:, P * n : P * (n + 1)].bitcast(FP8X4),
-                    lhsT_scale=w3_sc[b][:, P * n : P * (n + 1)],
-                    rhs=z_codes[b, 1][:, lo : lo + P].bitcast(FP8X4),
-                    rhs_scale=z_sc[b, 1][:, lo : lo + P],
-                    start=(b == 0),
-                    stop=(b == 1),
-                )
-            for u in range(2):
-                engines[u](out=staged[1][:, 2 * u : 2 * u + 2, lo : lo + P], in_=accs[u][:])
-                rows = out[2 * P * u : 2 * P * (u + 1), BANK + lo : BANK + lo + P]
-                nc.sync.dma_start(
-                    out=rows.rearrange("(n p) m -> p n m", p=P), in_=staged[1][:, 2 * u : 2 * u + 2, lo : lo + P]
-                )
-
-        last = BANK - P
         gate(0, 0)
         gate(1, 0)
         gated(0, 0, 0, BANK)
@@ -447,12 +426,9 @@ def tile_list_playlist_slot_refresh_kernel(
         gate(1, 1)
         gated(1, 1, 0, HALF)
         quant_z(0, 1, 0, BANK)
-        gated(1, 1, HALF, last)
+        gated(1, 1, HALF, BANK)
         quant_z(1, 1, 0, HALF)
-        gated(1, 1, last, BANK)
-        quant_z(1, 1, HALF, last)
-        quant_z(1, 1, last, BANK)
+        quant_z(1, 1, HALF, BANK)
         scores(0, 0, BANK, "acc", False)
         scores(1, 0, HALF, "out", False)
-        last_scores(HALF, (nc.scalar.copy, nc.scalar.copy))
-        last_scores(last, (nc.scalar.copy, nc.vector.tensor_copy))
+        scores(1, HALF, BANK, "acc", True)

@@ -55,10 +55,12 @@ def tile_list_playlist_slot_refresh_kernel(
 
         tab_sc = tile([P, T], U8, "tab_sc", "tab_sc")
         nc.vector.memset(tab_sc[:].bitcast(I32), 0)
-        w2_sc_raw = tile([P, 2, H], U8, "w2_sc_raw", "w2_sc_raw")
-        nc.vector.memset(w2_sc_raw[:].bitcast(I32), 0)
         warm = tile([P, 1], F32, "warm", "warm")
-        nc.gpsimd.memset(warm[:], 0.0)
+        nc.vector.memset(warm[:], 0.0)
+        w2_sc_raw = tile([P, H], U8, "w2_sc_raw", "w2_sc_raw")
+        nc.vector.memset(w2_sc_raw[:].bitcast(I32), 0)
+        w2_sc_moved = tile([P, H], U8, "w2_sc_moved", "w2_sc_moved")
+        nc.vector.memset(w2_sc_moved[:].bitcast(I32), 0)
         warmed = tile([P, 1], F32, "warmed", "warmed")
         nc.scalar.activation(out=warmed[:], in_=warm[:], func=ACT.Sigmoid)
         b1_first = tile([P, 1], F32, "b1f", "b1_first")
@@ -231,13 +233,39 @@ def tile_list_playlist_slot_refresh_kernel(
             nc.vector.quantize_mx(out=w3_codes[b][:, lo:hi].bitcast(FP8X4), scales=w3_sc[b][:, lo:hi], in_=grouped[:])
 
         w2_raw = tile([P, 2, 2 * H], U8, "w2_raw", "w2_raw")
-        nc.sync.dma_start(out=w2_raw[:].bitcast(I32), in_=w2_words.rearrange("a p c -> p a c").bitcast(I32))
-        w2_codes = tile([P, 2, 2 * H], U8, "w2_codes", "w2_codes")
-        w2_sc = tile([P, 2, H], U8, "w2_sc", "w2_sc")
-        nc.vector.tensor_copy(
-            out=w2_codes[:].rearrange("p a c -> p (a c)").bitcast(U16).rearrange("p (g t m) -> p g t m", t=PACK, m=P),
-            in_=w2_raw[:].rearrange("p a c -> p (a c)").bitcast(U16).rearrange("p (g m t) -> p g t m", t=PACK, m=P),
-        )
+        w2_codes = {}
+        w2_sc = {}
+
+        def load_w2():
+            nc.sync.dma_start(out=w2_raw[:].bitcast(I32), in_=w2_words.rearrange("a p c -> p a c").bitcast(I32))
+            for q in range(4):
+                nc.sync.dma_start(
+                    out=w2_sc_raw[QUAD * q : QUAD * q + 8, :].bitcast(I32),
+                    in_=w2_scales[:, 4 * q : 4 * q + 4, :].bitcast(I32),
+                )
+
+        def order_w2_words(a, b, slot):
+            codes = tile([P, 2 * PASS], U8, slot, "w2_codes%d%d" % (a, b))
+            nc.gpsimd.tensor_copy(
+                out=codes[:].bitcast(U16).rearrange("p (t m) -> p t m", t=PACK),
+                in_=w2_raw[:, a, 2 * PASS * b : 2 * PASS * (b + 1)].bitcast(U16).rearrange("p (m t) -> p t m", t=PACK),
+            )
+            w2_codes[a, b] = codes
+
+        def order_w2_scales(b, slot):
+            both = tile([P, PASS], U8, slot, "w2_sc%d" % b)
+            nc.gpsimd.tensor_copy(
+                out=both[:].rearrange("p (t m) -> p t m", t=PACK),
+                in_=w2_sc_raw[:, PASS * b : PASS * (b + 1)].rearrange("p (m t) -> p t m", t=PACK),
+            )
+            w2_sc[0, b] = both[:]
+            w2_sc[1, b] = w2_sc_moved[:, PASS * b : PASS * (b + 1)]
+            for q in range(4):
+                nc.sync.dma_start(
+                    out=w2_sc[1, b][QUAD * q : QUAD * q + 4, :].bitcast(I32),
+                    in_=both[QUAD * q + 4 : QUAD * q + 8, :].bitcast(I32),
+                )
+
         load_tab(0)
         nc.sync.dma_start(idx[:], offs)
         for q in range(4):
@@ -257,15 +285,6 @@ def tile_list_playlist_slot_refresh_kernel(
                 v_codes[1][:, BANK * c : BANK * (c + 1)],
                 tab_window(1).indirect(idx[:, LIST_COLS * c : LIST_COLS * (c + 1)]),
             )
-        for q in range(4):
-            nc.sync.dma_start(
-                out=w2_sc_raw[QUAD * q : QUAD * q + 4, :, :].bitcast(I32),
-                in_=w2_scales[:, 4 * q : 4 * q + 4, :].rearrange("a r c -> r a c").bitcast(I32),
-            )
-        nc.vector.tensor_copy(
-            out=w2_sc[:].rearrange("p a (b t m) -> p (a b) t m", t=PACK, m=P),
-            in_=w2_sc_raw[:].rearrange("p a (b m t) -> p (a b) t m", t=PACK, m=P),
-        )
         xt["first"] = tile([P, PACK, M], F32, "A", "x_first")
         nc.sync.dma_start(idx2[:], offs2)
         load_page(0, 0)
@@ -284,25 +303,30 @@ def tile_list_playlist_slot_refresh_kernel(
         features(0, 3, "h0")
         load_page(0, 1)
         put(0, 1, 0, S)
+        load_w2()
+        order_w2_words(0, 0, "h1")
         nc.sync.dma_start(idx3[:], offs3)
         stage_w3(0, 0, HALF, "R0")
         prep_w3(0, 0, HALF, "sb0")
         fetch_rows(0, "R0")
         load_page(0, 2)
         put(0, 2, 0, S)
+        order_w2_words(0, 1, "h2")
         prep_w1_planes(0)
         fetch_rows(1, "B0")
         nc.sync.dma_start(out=b1_planes[:], in_=b1[PASS : 2 * PASS].rearrange("(p i) -> p i", i=PACK))
         nc.sync.dma_start(out=b2_sb[:], in_=b2.rearrange("(a p i) -> p a i", a=2, i=PACK))
         load_page(0, 3)
         put(0, 3, 0, S)
+        order_w2_words(1, 0, "h0")
         prep_w1_planes(1)
         fetch_rows(2, "B1")
         features(1, 0, "R2")
-        features(1, 1, "h1")
+        features(1, 1, "h3")
         load_gains(0)
         load_page(1, 0)
         put(1, 0, 0, S)
+        order_w2_words(1, 1, "R2")
         stage_w3(0, HALF, N, "R1")
         prep_w3(0, HALF, N, "sb1")
         fetch_rows(3, "R1")
@@ -319,12 +343,14 @@ def tile_list_playlist_slot_refresh_kernel(
         load_gains(3)
         load_page(1, 3)
         put(1, 1, 0, S)
+        order_w2_scales(0, "h3")
         prep_w3(1, HALF, N, "sb0")
-        features(1, 2, "h0")
+        features(1, 2, "R0")
         fetch(0, 0)
         put(1, 2, 0, S)
+        order_w2_scales(1, "R0")
         prep_w3(1, 0, HALF, "sb1")
-        features(1, 3, "R2")
+        features(1, 3, "B0")
         fetch(1, 0)
         fetch(2, 0)
         for c in range(2):
@@ -359,11 +385,10 @@ def tile_list_playlist_slot_refresh_kernel(
             accs = [psum.tile([P, BANK], F32, tag=banks, name="acc_g%d" % i) for i in range(PACK)]
             for a in range(2):
                 for i in range(PACK):
-                    col = PASS * b + P * i
                     nc.tensor.matmul_mx(
                         out=accs[i][:],
-                        lhsT=w2_codes[:, a, 2 * col : 2 * (col + P)].bitcast(FP4X4),
-                        lhsT_scale=w2_sc[:, a, col : col + P],
+                        lhsT=w2_codes[a, b][:, 2 * P * i : 2 * P * (i + 1)].bitcast(FP4X4),
+                        lhsT_scale=w2_sc[a, b][:, P * i : P * (i + 1)],
                         rhs=x_codes[a, c][:].bitcast(FP8X4),
                         rhs_scale=x_sc[a, c][:],
                         start=(a == 0),

@@ -23,6 +23,7 @@ BANK = 512
 HALF = BANK // 2
 QUAD = 32
 LIST_COLS = BANK // 16
+CHUNK = HALF
 
 
 def tile_list_playlist_slot_refresh_kernel(
@@ -32,16 +33,16 @@ def tile_list_playlist_slot_refresh_kernel(
     with ExitStack() as ctx:
         lists = ctx.enter_context(tc.tile_pool(name="lists", bufs=1))
         sb = ctx.enter_context(tc.tile_pool(name="sb", bufs=1))
-        psum = ctx.enter_context(tc.psum_pool(name="psum", bufs=4))
+        psum = ctx.enter_context(tc.psum_pool(name="psum", bufs=1))
 
         def tile(shape, dtype, slot, name):
             return sb.tile(shape, dtype, tag=slot, name=name, align_bytes=64)
 
-        def woven(ap):
-            return ap.rearrange("p (c t) -> p c t", t=PACK)
+        def bank(k, name):
+            return psum.tile([P, BANK], F32, tag="bank%d" % k, name=name)
 
-        def planes(ap):
-            return ap.rearrange("p t c -> p c t")
+        def as_planes(ap):
+            return ap.rearrange("p (t m) -> p t m", t=PACK)
 
         idx = lists.tile([P, S // 16], U16, name="idx")
         idx2 = lists.tile([P, S // 16], U16, name="idx2")
@@ -151,7 +152,7 @@ def tile_list_playlist_slot_refresh_kernel(
         def features(b, i, slot):
             h = tile([P, S], F32, slot, "h%d%d" % (b, i))
             bias = b1_planes[:, i : i + 1] if b == 1 else b1_rows[:, i - 1 : i] if i > 0 else b1_first[:]
-            accs = [psum.tile([P, BANK], F32, tag="acc", name="acc_h%d" % c) for c in range(2)]
+            accs = [bank(2 * i + c, "acc_h%d" % c) for c in range(2)]
             for a in range(2):
                 for c in range(2):
                     nc.tensor.matmul_mx(
@@ -176,41 +177,41 @@ def tile_list_playlist_slot_refresh_kernel(
             )
 
         x_near = tile([P, (PACK + 1) * BANK], F32, "XN", "x_near")
-        xt = {}
+        x_f32 = {}
         x_rows = {}
+        for c in range(2):
+            x_f32[1, c] = as_planes(x_near[:, BANK:])[:, :, CHUNK * c : CHUNK * (c + 1)]
 
-        def x_planes(b, c):
-            if b == 0:
-                return xt["first"][:, :, BANK * c : BANK * (c + 1)]
-            if c == 0:
-                return x_near[:, BANK:].rearrange("p (t m) -> p t m", t=PACK)
-            return xt["last"][:, 0 : PACK * BANK].rearrange("p (t m) -> p t m", t=PACK)
+        def gather(dst, page, lo, hi):
+            nc.vector.tensor_copy(dst, page[:].indirect(idx3[:, lo // 16 : hi // 16]))
 
         def fetch_rows(t, slot):
-            rows = tile([P, M], F32, slot, "x_rows%d" % t)
-            nc.vector.tensor_copy(rows[:], pages[0, t][:].indirect(idx3[:]))
+            rows = tile([P, BANK], F32, slot, "x_rows%d" % t)
+            gather(rows[:], pages[0, t], 0, BANK)
             x_rows[t] = rows
 
-        def deal_rows(t):
-            nc.sync.dma_start(
-                out=xt["first"][QUAD * t : QUAD * (t + 1)].rearrange("p i m -> p (i m)"), in_=x_rows[t][:]
-            )
+        def deal(dst, t, rows):
+            nc.sync.dma_start(out=dst[QUAD * t : QUAD * (t + 1), :], in_=rows)
 
-        def fetch(i, c):
-            nc.vector.tensor_copy(
-                x_planes(1, c)[:, i, :],
-                pages[1, i][:].indirect(idx3[:, LIST_COLS * c : LIST_COLS * (c + 1)]),
-            )
+        def fetch(i):
+            gather(x_near[:, BANK * (i + 1) : BANK * (i + 2)], pages[1, i], 0, BANK)
 
         x_codes = {}
         x_sc = {}
 
-        def quant_x(b, c, xb):
-            codes = tile([P, BANK], U32, "xc%d%d" % (b, c), "x_codes%d%d" % (b, c))
-            scales = tile([P, BANK], U8, "xs%d%d" % (b, c), "x_sc%d%d" % (b, c))
-            nc.vector.quantize_mx(out=codes[:].bitcast(FP8X4), scales=scales[:], in_=xb)
-            x_codes[b, c] = codes
-            x_sc[b, c] = scales
+        def quantise(name, slot, woven):
+            width = woven.shape[1] // PACK
+            codes = tile([P, width], U32, slot, name + "_codes")
+            scales = tile([P, width], U8, name + "s", name + "_sc")
+            nc.vector.quantize_mx(out=codes[:].bitcast(FP8X4), scales=scales[:], in_=woven)
+            return codes, scales
+
+        def quant_x(keys, woven):
+            name = "x%d%d" % keys[0]
+            codes, scales = quantise(name, name, woven)
+            for j, key in enumerate(keys):
+                x_codes[key] = codes[:, CHUNK * j : CHUNK * (j + 1)]
+                x_sc[key] = scales[:, CHUNK * j : CHUNK * (j + 1)]
 
         w3_codes = [tile([P, N], U32, "w3c%d" % b, "w3_codes%d" % b) for b in range(2)]
         w3_sc = [tile([P, N], U8, "w3s%d" % b, "w3_sc%d" % b) for b in range(2)]
@@ -285,7 +286,12 @@ def tile_list_playlist_slot_refresh_kernel(
                 v_codes[1][:, BANK * c : BANK * (c + 1)],
                 tab_window(1).indirect(idx[:, LIST_COLS * c : LIST_COLS * (c + 1)]),
             )
-        xt["first"] = tile([P, PACK, M], F32, "A", "x_first")
+        x_dealt = tile([P, PACK * M], F32, "A", "x_dealt")
+        dealt_near = x_dealt[:, 0 : PACK * BANK]
+        dealt_far = x_dealt[:, PACK * BANK :]
+        for c in range(4):
+            half = dealt_near if c < 2 else dealt_far
+            x_f32[0, c] = as_planes(half)[:, :, CHUNK * (c % 2) : CHUNK * (c % 2 + 1)]
         nc.sync.dma_start(idx2[:], offs2)
         load_page(0, 0)
         nc.sync.dma_start(out=gains_rows[:, 0:BANK], in_=wgs[:, 0:BANK])
@@ -332,13 +338,13 @@ def tile_list_playlist_slot_refresh_kernel(
         fetch_rows(3, "R1")
         load_gains(1)
         load_page(1, 1)
-        deal_rows(0)
-        deal_rows(1)
+        deal(dealt_near, 0, x_rows[0][:])
+        deal(dealt_near, 1, x_rows[1][:])
         load_w3(1, HALF, N, x_near[:, 0 : 2 * BANK])
         load_gains(2)
         load_page(1, 2)
-        deal_rows(2)
-        deal_rows(3)
+        deal(dealt_near, 2, x_rows[2][:])
+        deal(dealt_near, 3, x_rows[3][:])
         load_w3(1, 0, HALF, x_near[:, 2 * BANK : 4 * BANK])
         load_gains(3)
         load_page(1, 3)
@@ -346,114 +352,175 @@ def tile_list_playlist_slot_refresh_kernel(
         order_w2_scales(0, "h3")
         prep_w3(1, HALF, N, "sb0")
         features(1, 2, "R0")
-        fetch(0, 0)
+        fetch(0)
         put(1, 2, 0, S)
         order_w2_scales(1, "R0")
         prep_w3(1, 0, HALF, "sb1")
         features(1, 3, "B0")
-        fetch(1, 0)
-        fetch(2, 0)
-        for c in range(2):
-            xb = tile([P, BANK * PACK], BF16, "wb%d" % c, "xb0%d" % c)
-            weave(xb[:], x_planes(0, c))
-            quant_x(0, c, xb[:])
-        put(1, 3, 0, S)
-        xt["last"] = tile([P, (PACK + 1) * BANK], F32, "G1", "x_last")
-        fetch(0, 1)
-        fetch(3, 0)
-        xb10 = xt["last"][:, 3 * BANK : 5 * BANK].bitcast(BF16)
-        weave(xb10, x_planes(1, 0))
-        fetch(1, 1)
-        fetch(2, 1)
-        quant_x(1, 0, xb10)
-        fetch(3, 1)
-        xb11 = tile([P, BANK * PACK], BF16, "wb0", "xb11")
-        nc.vector.tensor_copy(
-            out=xb11[:].rearrange("p (m e t) -> p m t e", e=2, t=PACK),
-            in_=x_planes(1, 1).rearrange("p t (m e) -> p m t e", e=2),
-        )
-        quant_x(1, 1, xb11[:])
+        fetch(1)
+        fetch(2)
+        xb = tile([P, BANK * PACK], BF16, "wb0", "xb_near")
+        weave(xb[:], as_planes(dealt_near))
+        quant_x([(0, 0), (0, 1)], xb[:])
 
+        gate_banks = {}
         gates = {}
         zbs = {}
         z_codes = {}
         z_sc = {}
 
-        def gate(b, c):
-            g = tile([P, PACK, BANK], F32, "P0%d" % (2 * c + b), "gate%d%d" % (b, c))
-            banks = "acc" if b == 0 else "out"
-            accs = [psum.tile([P, BANK], F32, tag=banks, name="acc_g%d" % i) for i in range(PACK)]
-            for a in range(2):
-                for i in range(PACK):
+        def gate_passes(a, b, c):
+            for i in range(PACK):
+                acc = gate_banks[b, c][i // 2]
+                for u in range(2):
+                    col = CHUNK * (i % 2) + P * u
                     nc.tensor.matmul_mx(
-                        out=accs[i][:],
+                        out=acc[:, col : col + P],
                         lhsT=w2_codes[a, b][:, 2 * P * i : 2 * P * (i + 1)].bitcast(FP4X4),
                         lhsT_scale=w2_sc[a, b][:, P * i : P * (i + 1)],
-                        rhs=x_codes[a, c][:].bitcast(FP8X4),
-                        rhs_scale=x_sc[a, c][:],
-                        start=(a == 0),
-                        stop=(a == 1),
+                        rhs=x_codes[a, c][:, P * u : P * (u + 1)].bitcast(FP8X4),
+                        rhs_scale=x_sc[a, c][:, P * u : P * (u + 1)],
+                        start=(a == 0 and col == 0),
+                        stop=(a == 1 and col == BANK - P),
                     )
-            for i in range(PACK):
-                nc.scalar.activation(out=g[:, i, :], in_=accs[i][:], func=ACT.Sigmoid, bias=b2_sb[:, b, i : i + 1])
-            gates[b, c] = g
-            zbs[b, c] = tile([P, BANK * PACK], BF16, ("zb%d" % b if c == 0 else "wb%d" % (1 - b)), "zb%d%d" % (b, c))
-            z_codes[b, c] = tile([P, BANK], U32, ("wc1%d" if c == 0 else "v%d") % b, "z_codes%d%d" % (b, c))
-            z_sc[b, c] = tile([P, BANK], U8, "zs%d%d" % (b, c), "z_sc%d%d" % (b, c))
 
-        def gated(b, c, lo, hi):
-            nc.vector.tensor_tensor(
-                zbs[b, c][:, PACK * lo : PACK * hi].rearrange("p (m e t) -> p m t e", e=2, t=PACK),
-                x_planes(b, c)[:, :, lo:hi].rearrange("p t (m e) -> p m t e", e=2),
-                gates[b, c][:, :, lo:hi].rearrange("p t (m e) -> p m t e", e=2),
+        def open_gate(b, c, first):
+            gate_banks[b, c] = [bank(first + u, "acc_g%d%d%d" % (b, c, u)) for u in range(2)]
+            gate_passes(0, b, c)
+
+        def close_gate(b, c, g):
+            gate_passes(1, b, c)
+            gates[b, c] = g
+            for i in range(PACK):
+                nc.scalar.activation(
+                    out=g[:, i, :],
+                    in_=gate_banks[b, c][i // 2][:, CHUNK * (i % 2) : CHUNK * (i % 2 + 1)],
+                    func=ACT.Sigmoid,
+                    bias=b2_sb[:, b, i : i + 1],
+                )
+
+        def gate_tile(slot, name):
+            return as_planes(tile([P, PACK * CHUNK], F32, slot, name)[:])
+
+        def gated(engine, b, c, run):
+            engine.tensor_tensor(
+                zbs[c][:, PACK * CHUNK * b : PACK * CHUNK * (b + 1)].rearrange("p (m e t) -> p m t e", e=run, t=PACK),
+                x_f32[b, c].rearrange("p t (m e) -> p m t e", e=run),
+                gates[b, c].rearrange("p t (m e) -> p m t e", e=run),
                 MULT,
             )
 
-        def quant_z(b, c, lo, hi):
-            nc.vector.quantize_mx(
-                out=z_codes[b, c][:, lo:hi].bitcast(FP8X4),
-                scales=z_sc[b, c][:, lo:hi],
-                in_=zbs[b, c][:, PACK * lo : PACK * hi],
+        def quant_z(c, slot):
+            codes, scales = quantise("z%d" % c, slot, zbs[c])
+            for b in range(2):
+                z_codes[b, c] = codes[:, CHUNK * b : CHUNK * (b + 1)]
+                z_sc[b, c] = scales[:, CHUNK * b : CHUNK * (b + 1)]
+
+        def quant_z_part(b, c, slot):
+            codes, scales = quantise("z%d%d" % (c, b), slot, zbs[c][:, PACK * CHUNK * b : PACK * CHUNK * (b + 1)])
+            z_codes[b, c] = codes[:]
+            z_sc[b, c] = scales[:]
+
+        def score_pass(acc, n, b, c):
+            nc.tensor.matmul_mx(
+                out=acc,
+                lhsT=w3_codes[b][:, P * n : P * (n + 1)].bitcast(FP8X4),
+                lhsT_scale=w3_sc[b][:, P * n : P * (n + 1)],
+                rhs=z_codes[b, c].bitcast(FP8X4),
+                rhs_scale=z_sc[b, c],
+                start=(b == 0),
+                stop=(b == 1),
             )
 
-        staged = [tile([P, N // P, BANK], F32, "P1%d" % c, "staged%d" % c) for c in range(2)]
-
-        def scores(c, lo, hi, banks, shared):
-            accs = [psum.tile([P, hi - lo], F32, tag=banks, name="acc_o%d" % n) for n in range(N // P)]
-            for b in range(2):
-                for n in range(N // P):
-                    nc.tensor.matmul_mx(
-                        out=accs[n][:],
-                        lhsT=w3_codes[b][:, P * n : P * (n + 1)].bitcast(FP8X4),
-                        lhsT_scale=w3_sc[b][:, P * n : P * (n + 1)],
-                        rhs=z_codes[b, c][:, lo:hi].bitcast(FP8X4),
-                        rhs_scale=z_sc[b, c][:, lo:hi],
-                        start=(b == 0),
-                        stop=(b == 1),
-                    )
-            for n in range(N // P):
-                if shared and n % 2 == 1:
-                    nc.vector.tensor_copy(out=staged[c][:, n, lo:hi], in_=accs[n][:])
-                else:
-                    nc.scalar.copy(out=staged[c][:, n, lo:hi], in_=accs[n][:])
+        def scores(c, first, copy, staged):
+            for u in range(2):
+                acc = bank(first + u, "acc_o%d%d" % (c, u))
+                for j in range(2):
+                    for b in range(2):
+                        score_pass(acc[:, CHUNK * j : CHUNK * (j + 1)], 2 * u + j, b, c)
+                part = staged[:, BANK * u : BANK * (u + 1)]
+                copy(out=part, in_=acc[:])
                 nc.sync.dma_start(
-                    out=out[P * n : P * (n + 1), BANK * c + lo : BANK * c + hi], in_=staged[c][:, n, lo:hi]
+                    out=out[2 * P * u : 2 * P * (u + 1), CHUNK * c : CHUNK * (c + 1)].rearrange("(j p) m -> p j m", p=P),
+                    in_=part.rearrange("p (j m) -> p j m", j=2),
                 )
 
-        gate(0, 0)
-        gate(1, 0)
-        gated(0, 0, 0, BANK)
-        gated(1, 0, 0, BANK)
-        quant_z(0, 0, 0, BANK)
-        gate(0, 1)
-        gated(0, 1, 0, BANK)
-        quant_z(1, 0, 0, BANK)
-        gate(1, 1)
-        gated(1, 1, 0, HALF)
-        quant_z(0, 1, 0, BANK)
-        gated(1, 1, HALF, BANK)
-        quant_z(1, 1, 0, HALF)
-        quant_z(1, 1, HALF, BANK)
-        scores(0, 0, BANK, "acc", False)
-        scores(1, 0, HALF, "out", False)
-        scores(1, HALF, BANK, "acc", True)
+        def last_scores(c, banks, slot):
+            staged = tile([P, N // P, CHUNK], F32, slot, "staged%d" % c)
+            accs = [bank(k, "acc_o%d%d" % (c, k)) for k in banks]
+            for b in range(2):
+                for n in range(N // P):
+                    score_pass(accs[n][:, 0:CHUNK], n, b, c)
+            for n in range(N // P):
+                copy = nc.vector.tensor_copy if n % 2 == 1 else nc.scalar.copy
+                copy(out=staged[:, n, :], in_=accs[n][:, 0:CHUNK])
+                nc.sync.dma_start(out=out[P * n : P * (n + 1), CHUNK * c : CHUNK * (c + 1)], in_=staged[:, n, :])
+
+        def far_rows(t, dst):
+            gather(dst, pages[0, t], BANK, M)
+            deal(dealt_far, t, dst)
+
+        def far_planes(c, dst):
+            x_f32[1, c] = as_planes(dst)
+            for i in range(PACK):
+                gather(x_f32[1, c][:, i, :], pages[1, i], CHUNK * c, CHUNK * (c + 1))
+
+        for c in range(2):
+            for b in range(2):
+                open_gate(b, c, 4 * c + 2 * b)
+        put(1, 3, 0, S)
+        for c in range(2):
+            gather(x_f32[1, c][:, PACK - 1, :], pages[1, PACK - 1], CHUNK * c, CHUNK * (c + 1))
+        far_rows(0, tile([P, BANK], F32, "G1", "rows_a")[:])
+        xb = tile([P, PACK * CHUNK], BF16, "B0", "xb10")
+        weave(xb[:], x_f32[1, 0])
+        quant_x([(1, 0)], xb[:])
+        far_rows(1, tile([P, BANK], F32, "B0", "rows_b")[:])
+        xb = tile([P, PACK * CHUNK], BF16, "G0", "xb11")
+        weave(xb[:], x_f32[1, 1])
+        quant_x([(1, 1)], xb[:])
+        far = tile([P, 3 * PACK * CHUNK], F32, "G0", "far")
+        for t in range(2):
+            far_rows(2 + t, far[:, BANK * t : BANK * (t + 1)])
+        far_planes(2, far[:, PACK * CHUNK : 2 * PACK * CHUNK])
+        far_planes(3, far[:, 2 * PACK * CHUNK :])
+        close_gate(0, 0, gate_tile("B1", "gate00"))
+        close_gate(1, 0, gate_tile("wb1", "gate10"))
+        close_gate(0, 1, gate_tile("R1", "gate01"))
+        close_gate(1, 1, gate_tile("zb1", "gate11"))
+        zbs[0] = tile([P, 2 * PACK * CHUNK], BF16, "wb0", "zb0")[:]
+        gated(nc.gpsimd, 0, 0, 4)
+        gated(nc.gpsimd, 1, 0, 4)
+        xb = tile([P, 2 * PACK * CHUNK], BF16, "B1", "xb2")
+        weave(xb[:, PACK * CHUNK :], x_f32[1, 2])
+        weave(xb[:, 0 : PACK * CHUNK], x_f32[0, 2])
+        quant_x([(0, 2), (1, 2)], xb[:])
+        quant_z(0, "wc10")
+        held = tile([P, 4 * PACK * CHUNK], BF16, "B1", "held")
+        xb = held[:, 0 : 2 * PACK * CHUNK]
+        zbs[1] = held[:, 2 * PACK * CHUNK :]
+        weave(xb[:, 0 : PACK * CHUNK], x_f32[0, 3])
+        weave(xb[:, PACK * CHUNK :], x_f32[1, 3])
+        gated(nc.vector, 0, 1, 2)
+        gated(nc.vector, 1, 1, 2)
+        quant_x([(0, 3), (1, 3)], xb)
+        quant_z(1, "wc11")
+        open_gate(0, 2, 0)
+        close_gate(0, 2, gate_tile("P03", "gate02"))
+        open_gate(1, 2, 2)
+        close_gate(1, 2, gate_tile("P00", "gate12"))
+        for b in range(2):
+            open_gate(b, 3, 4 + 2 * b)
+            close_gate(b, 3, gate_tile("P0%d" % (1 + b), "gate%d3" % b))
+        zbs[2] = tile([P, 2 * PACK * CHUNK], BF16, "wb0", "zb2")[:]
+        zbs[3] = tile([P, 2 * PACK * CHUNK], BF16, "wb1", "zb3")[:]
+        gated(nc.vector, 0, 2, 2)
+        gated(nc.vector, 1, 2, 2)
+        gated(nc.vector, 0, 3, 2)
+        quant_z(2, "v0")
+        gated(nc.vector, 1, 3, 2)
+        quant_z_part(0, 3, "v1")
+        quant_z_part(1, 3, "z31")
+        for c in range(3):
+            scores(c, 2 * c, nc.scalar.copy, tile([P, PACK * CHUNK], F32, "P1%d" % c, "staged%d" % c)[:])
+        last_scores(3, (6, 7, 0, 1), "P13")

@@ -102,22 +102,17 @@ def tile_list_playlist_slot_refresh_kernel(
                 in_=rows.rearrange("(p j) c -> p j c", j=PACK),
             )
 
-        def prep_w1_rows(t0, t1, slot):
-            blocks = t1 - t0
-            grouped = tile([P, blocks, 2, PASS], BF16, slot, "w1_b0%d" % t0)
-            codes = tile([P, blocks * 2 * P], U32, "wc0%d" % t0, "w1_codes0%d" % t0)
-            scales = tile([P, blocks * 2 * P], U8, "ws0%d" % t0, "w1_sc0%d" % t0)
+        def prep_w1_rows(t, t0, slot):
+            grouped = tile([P, 2, PASS], BF16, slot, "w1_b0%d" % t)
+            codes = tile([P, 2 * P], U32, "wc0%d" % t, "w1_codes0%d" % t)
+            scales = tile([P, 2 * P], U8, "ws0%d" % t, "w1_sc0%d" % t)
             for a in range(2):
-                nc.scalar.copy(
-                    out=grouped[:, :, a, :].rearrange("p t (c i j) -> p t c j i", i=PACK, j=PACK),
-                    in_=w1_raw[t0][:, a, :].rearrange("p (j t c i) -> p t c j i", j=PACK, t=blocks, i=PACK),
-                )
-                for t in range(t0, t1):
-                    first = P * (2 * (t - t0) + a)
-                    w1_codes[a, 0, t] = codes[:, first : first + P]
-                    w1_sc[a, 0, t] = scales[:, first : first + P]
+                block = w1_raw[t0][:, a, :].rearrange("p (j c) -> p j c", j=PACK)[:, :, P * (t - t0) : P * (t - t0 + 1)]
+                weave(grouped[:, a, :], block)
+                w1_codes[a, 0, t] = codes[:, P * a : P * (a + 1)]
+                w1_sc[a, 0, t] = scales[:, P * a : P * (a + 1)]
             nc.vector.quantize_mx(
-                out=codes[:].bitcast(FP8X4), scales=scales[:], in_=grouped[:].rearrange("p t a k -> p (t a k)")
+                out=codes[:].bitcast(FP8X4), scales=scales[:], in_=grouped[:].rearrange("p a k -> p (a k)")
             )
 
         def prep_w1_planes(a):
@@ -128,8 +123,8 @@ def tile_list_playlist_slot_refresh_kernel(
             codes = tile([P, PASS], U32, "wc1%d" % a, "w1_codes1%d" % a)
             scales = tile([P, PASS], U8, "ws1%d" % a, "w1_sc1%d" % a)
             nc.scalar.copy(
-                out=grouped[:].rearrange("p (t m j) -> p t m j", t=PACK, j=PACK),
-                in_=raw[:].rearrange("p j (m t) -> p t m j", t=PACK),
+                out=grouped[:].rearrange("p (t m j) -> p m j t", t=PACK, j=PACK),
+                in_=raw[:].rearrange("p j (m t) -> p m j t", t=PACK),
             )
             nc.vector.quantize_mx(out=codes[:].bitcast(FP8X4), scales=scales[:], in_=grouped[:])
             for i in range(PACK):
@@ -176,11 +171,11 @@ def tile_list_playlist_slot_refresh_kernel(
                 pages[b, i][:].indirect(idx2[:, lo // 16 : hi // 16]), hs[b, i][:, lo:hi], gain[:, lo:hi], MULT
             )
 
-        x_near = tile([P, (PACK + 1) * BANK], F32, "XN", "x_near")
+        x_near = tile([P, PACK * BANK], F32, "XN", "x_near")
         x_f32 = {}
         x_rows = {}
         for c in range(2):
-            x_f32[1, c] = as_planes(x_near[:, BANK:])[:, :, CHUNK * c : CHUNK * (c + 1)]
+            x_f32[1, c] = as_planes(x_near[:])[:, :, CHUNK * c : CHUNK * (c + 1)]
 
         def gather(dst, page, lo, hi):
             nc.vector.tensor_copy(dst, page[:].indirect(idx3[:, lo // 16 : hi // 16]))
@@ -194,7 +189,7 @@ def tile_list_playlist_slot_refresh_kernel(
             nc.sync.dma_start(out=dst[QUAD * t : QUAD * (t + 1), :], in_=rows)
 
         def fetch(i):
-            gather(x_near[:, BANK * (i + 1) : BANK * (i + 2)], pages[1, i], 0, BANK)
+            gather(x_near[:, BANK * i : BANK * (i + 1)], pages[1, i], 0, BANK)
 
         x_codes = {}
         x_sc = {}
@@ -253,17 +248,18 @@ def tile_list_playlist_slot_refresh_kernel(
             )
             w2_codes[a, b] = codes
 
-        def order_w2_scales(b, slot):
-            both = tile([P, PASS], U8, slot, "w2_sc%d" % b)
+        def order_w2_scales(slot):
+            both = tile([P, H], U8, slot, "w2_sc_both")
             nc.gpsimd.tensor_copy(
-                out=both[:].rearrange("p (t m) -> p t m", t=PACK),
-                in_=w2_sc_raw[:, PASS * b : PASS * (b + 1)].rearrange("p (m t) -> p t m", t=PACK),
+                out=both[:].rearrange("p (b t m) -> p b t m", b=2, t=PACK),
+                in_=w2_sc_raw[:].rearrange("p (b m t) -> p b t m", b=2, t=PACK),
             )
-            w2_sc[0, b] = both[:]
-            w2_sc[1, b] = w2_sc_moved[:, PASS * b : PASS * (b + 1)]
+            for b in range(2):
+                w2_sc[0, b] = both[:, PASS * b : PASS * (b + 1)]
+                w2_sc[1, b] = w2_sc_moved[:, PASS * b : PASS * (b + 1)]
             for q in range(4):
                 nc.sync.dma_start(
-                    out=w2_sc[1, b][QUAD * q : QUAD * q + 4, :].bitcast(I32),
+                    out=w2_sc_moved[QUAD * q : QUAD * q + 4, :].bitcast(I32),
                     in_=both[QUAD * q + 4 : QUAD * q + 8, :].bitcast(I32),
                 )
 
@@ -276,11 +272,11 @@ def tile_list_playlist_slot_refresh_kernel(
             )
         nc.vector.tensor_copy(v_codes[0][:], tab_window(0).indirect(idx[:]))
         nc.vector.tensor_copy(v_sc[:], tab_sc[:].indirect(idx[:]))
-        load_w1_rows(0, 2, 0)
-        load_w1_rows(0, 2, 1)
-        prep_w1_rows(0, 2, "wb0")
-        nc.sync.dma_start(out=b1_first[:], in_=b1[0:P].rearrange("(p t) -> p t", t=1))
+        load_w1_rows(0, 1, 0)
+        load_w1_rows(0, 1, 1)
+        prep_w1_rows(0, 0, "wb0")
         load_tab(1)
+        nc.sync.dma_start(out=b1_first[:], in_=b1[0:P].rearrange("(p t) -> p t", t=1))
         for c in range(2):
             nc.vector.tensor_copy(
                 v_codes[1][:, BANK * c : BANK * (c + 1)],
@@ -297,66 +293,69 @@ def tile_list_playlist_slot_refresh_kernel(
         nc.sync.dma_start(out=gains_rows[:, 0:BANK], in_=wgs[:, 0:BANK])
         features(0, 0, "h0")
         put(0, 0, 0, BANK)
-        nc.sync.dma_start(out=gains_rows[:, BANK:S], in_=wgs[:, BANK:S])
-        put(0, 0, BANK, S)
+        load_w1_rows(1, 3, 0)
+        load_w1_rows(1, 3, 1)
+        prep_w1_rows(1, 1, "sb0")
         with nc.allow_non_contiguous_dma(reason="one bias value for each partition and block of 128 channels"):
             nc.sync.dma_start(out=b1_rows[:], in_=b1[P:PASS].rearrange("(t p) -> p t", p=P))
         features(0, 1, "h1")
-        load_w1_rows(2, 4, 0)
-        load_w1_rows(2, 4, 1)
-        prep_w1_rows(2, 4, "wb1")
+        nc.sync.dma_start(out=gains_rows[:, BANK:S], in_=wgs[:, BANK:S])
+        put(0, 0, BANK, S)
+        prep_w1_rows(2, 1, "sb1")
         features(0, 2, "h2")
-        features(0, 3, "h0")
         load_page(0, 1)
         put(0, 1, 0, S)
-        load_w2()
-        order_w2_words(0, 0, "h1")
         nc.sync.dma_start(idx3[:], offs3)
         stage_w3(0, 0, HALF, "R0")
         prep_w3(0, 0, HALF, "sb0")
         fetch_rows(0, "R0")
+        load_w1_rows(3, 4, 0)
+        load_w1_rows(3, 4, 1)
+        prep_w1_rows(3, 3, "wb1")
+        features(0, 3, "h0")
+        load_w2()
+        order_w2_words(0, 0, "h1")
         load_page(0, 2)
         put(0, 2, 0, S)
         order_w2_words(0, 1, "h2")
         prep_w1_planes(0)
         fetch_rows(1, "B0")
+        prep_w1_planes(1)
         nc.sync.dma_start(out=b1_planes[:], in_=b1[PASS : 2 * PASS].rearrange("(p i) -> p i", i=PACK))
         nc.sync.dma_start(out=b2_sb[:], in_=b2.rearrange("(a p i) -> p a i", a=2, i=PACK))
         load_page(0, 3)
         put(0, 3, 0, S)
         order_w2_words(1, 0, "h0")
-        prep_w1_planes(1)
-        fetch_rows(2, "B1")
-        features(1, 0, "R2")
+        stage_w3(0, HALF, N, "R1")
+        prep_w3(0, HALF, N, "sb1")
+        fetch_rows(2, "R1")
+        features(1, 0, "R3")
         features(1, 1, "h3")
         load_gains(0)
         load_page(1, 0)
         put(1, 0, 0, S)
-        order_w2_words(1, 1, "R2")
-        stage_w3(0, HALF, N, "R1")
-        prep_w3(0, HALF, N, "sb1")
-        fetch_rows(3, "R1")
+        order_w2_words(1, 1, "R3")
+        stage_w3(1, HALF, N, "B1")
+        prep_w3(1, HALF, N, "sb0")
+        fetch_rows(3, "B1")
         load_gains(1)
         load_page(1, 1)
         deal(dealt_near, 0, x_rows[0][:])
         deal(dealt_near, 1, x_rows[1][:])
-        load_w3(1, HALF, N, x_near[:, 0 : 2 * BANK])
         load_gains(2)
         load_page(1, 2)
         deal(dealt_near, 2, x_rows[2][:])
         deal(dealt_near, 3, x_rows[3][:])
-        load_w3(1, 0, HALF, x_near[:, 2 * BANK : 4 * BANK])
+        load_w3(1, 0, HALF, x_near[:, HALF : HALF + 2 * BANK])
         load_gains(3)
         load_page(1, 3)
         put(1, 1, 0, S)
-        order_w2_scales(0, "h3")
-        prep_w3(1, HALF, N, "sb0")
         features(1, 2, "R0")
-        fetch(0)
         put(1, 2, 0, S)
-        order_w2_scales(1, "R0")
+        order_w2_scales("R0")
         prep_w3(1, 0, HALF, "sb1")
         features(1, 3, "B0")
+        fetch(0)
         fetch(1)
         fetch(2)
         xb = tile([P, BANK * PACK], BF16, "wb0", "xb_near")

@@ -56,20 +56,16 @@ def tile_list_playlist_slot_refresh_kernel(
 
         tab_sc = tile([P, T], U8, "tab_sc", "tab_sc")
         nc.vector.memset(tab_sc[:].bitcast(I32), 0)
-        warm = tile([P, 1], F32, "warm", "warm")
-        nc.vector.memset(warm[:], 0.0)
         w2_sc_raw = tile([P, H], U8, "w2_sc_raw", "w2_sc_raw")
         nc.vector.memset(w2_sc_raw[:].bitcast(I32), 0)
         w2_sc_moved = tile([P, H], U8, "w2_sc_moved", "w2_sc_moved")
         nc.vector.memset(w2_sc_moved[:].bitcast(I32), 0)
-        warmed = tile([P, 1], F32, "warmed", "warmed")
-        nc.scalar.activation(out=warmed[:], in_=warm[:], func=ACT.Sigmoid)
         b1_first = tile([P, 1], F32, "b1f", "b1_first")
         b1_rows = tile([P, PACK - 1], F32, "b1r", "b1_rows")
         b1_planes = tile([P, PACK], F32, "b1p", "b1_planes")
         b2_sb = tile([P, 2, PACK], F32, "b2", "b2_sb")
 
-        gains_rows = tile([P, S], F32, "GR", "gains_rows")
+        gains_rows = sb.tile([P, S], F32, tag="GR", name="gains_rows", align_bytes=256)
         gains = [tile([P, 2, S], F32, "G%d" % u, "gains%d" % u) for u in range(2)]
         wgs_rows = wgs.rearrange("(r i) j -> r i j", i=PACK)
 

@@ -36,7 +36,8 @@ def tile_list_playlist_slot_refresh_kernel(
         psum = ctx.enter_context(tc.psum_pool(name="psum", bufs=1))
 
         def tile(shape, dtype, slot, name):
-            return sb.tile(shape, dtype, tag=slot, name=name, align_bytes=64)
+            align = 256 if slot[0] in "ABGPRX" or slot in ("tab_sc", "v_sc", "w2_raw") else 64
+            return sb.tile(shape, dtype, tag=slot, name=name, align_bytes=align)
 
         def bank(k, name):
             return psum.tile([P, BANK], F32, tag="bank%d" % k, name=name)
@@ -55,17 +56,20 @@ def tile_list_playlist_slot_refresh_kernel(
             )
 
         tab_sc = tile([P, T], U8, "tab_sc", "tab_sc")
-        nc.vector.memset(tab_sc[:].bitcast(I32), 0)
+        nc.vector.memset(tab_sc[QUAD : 2 * QUAD, :].bitcast(I32), 0)
+        nc.vector.memset(tab_sc[2 * QUAD : P, :].bitcast(I32), 0)
+        v_sc = tile([P, 2, S], U8, "v_sc", "v_sc")
+        nc.gpsimd.memset(v_sc[:].bitcast(I32), 0)
         w2_sc_raw = tile([P, H], U8, "w2_sc_raw", "w2_sc_raw")
-        nc.vector.memset(w2_sc_raw[:].bitcast(I32), 0)
+        nc.gpsimd.memset(w2_sc_raw[:].bitcast(I32), 0)
         w2_sc_moved = tile([P, H], U8, "w2_sc_moved", "w2_sc_moved")
-        nc.vector.memset(w2_sc_moved[:].bitcast(I32), 0)
+        nc.gpsimd.memset(w2_sc_moved[:].bitcast(I32), 0)
         b1_first = tile([P, 1], F32, "b1f", "b1_first")
         b1_rows = tile([P, PACK - 1], F32, "b1r", "b1_rows")
         b1_planes = tile([P, PACK], F32, "b1p", "b1_planes")
         b2_sb = tile([P, 2, PACK], F32, "b2", "b2_sb")
 
-        gains_rows = sb.tile([P, S], F32, tag="GR", name="gains_rows", align_bytes=256)
+        gains_rows = tile([P, S], F32, "GR", "gains_rows")
         gains = [tile([P, 2, S], F32, "G%d" % u, "gains%d" % u) for u in range(2)]
         wgs_rows = wgs.rearrange("(r i) j -> r i j", i=PACK)
 
@@ -75,7 +79,7 @@ def tile_list_playlist_slot_refresh_kernel(
 
         tab_w = tile([P, 2 * T], I32, "A", "tab_w")
         v_codes = [tile([P, S], U32, "v%d" % a, "v_codes%d" % a) for a in range(2)]
-        v_sc = tile([P, S], U8, "v_sc", "v_sc")
+        v_sc_packed = tile([P, S], U8, "v_scp", "v_sc_packed")
         w1_codes = {}
         w1_sc = {}
 
@@ -151,7 +155,7 @@ def tile_list_playlist_slot_refresh_kernel(
                         lhsT=w1_codes[a, b, i].bitcast(FP8X4),
                         lhsT_scale=w1_sc[a, b, i],
                         rhs=v_codes[a][:, BANK * c : BANK * (c + 1)].bitcast(FP8X4),
-                        rhs_scale=v_sc[4 * a : P, BANK * c : BANK * (c + 1)],
+                        rhs_scale=v_sc[:, a, BANK * c : BANK * (c + 1)],
                         start=(a == 0),
                         stop=(a == 1),
                     )
@@ -259,20 +263,26 @@ def tile_list_playlist_slot_refresh_kernel(
                     in_=both[QUAD * q + 4 : QUAD * q + 8, :].bitcast(I32),
                 )
 
-        load_tab(0)
         nc.sync.dma_start(idx[:], offs)
-        for q in range(4):
-            nc.sync.dma_start(
-                out=tab_sc[QUAD * q : QUAD * q + 8, :].bitcast(I32),
-                in_=tab_scales[:, 4 * q : 4 * q + 4, :].bitcast(I32),
-            )
+        for a in range(2):
+            nc.sync.dma_start(out=tab_sc[a:QUAD:2, :].bitcast(I32), in_=tab_scales[a].bitcast(I32))
+        load_tab(0)
+        nc.sync.dma_start(out=b1_first[:], in_=b1[0:P].rearrange("(p t) -> p t", t=1))
+        nc.sync.dma_start(idx2[:], offs2)
+        nc.sync.dma_start(idx3[:], offs3)
+        nc.sync.dma_start(out=b1_planes[:], in_=b1[PASS : 2 * PASS].rearrange("(p i) -> p i", i=PACK))
+        nc.vector.tensor_copy(v_sc_packed[:], tab_sc[:].indirect(idx[:]))
         nc.vector.tensor_copy(v_codes[0][:], tab_window(0).indirect(idx[:]))
-        nc.vector.tensor_copy(v_sc[:], tab_sc[:].indirect(idx[:]))
         load_w1_rows(0, 1, 0)
         load_w1_rows(0, 1, 1)
         prep_w1_rows(0, 0, "wb0")
         load_tab(1)
-        nc.sync.dma_start(out=b1_first[:], in_=b1[0:P].rearrange("(p t) -> p t", t=1))
+        nc.sync.dma_start(out=b2_sb[:], in_=b2.rearrange("(a p i) -> p a i", a=2, i=PACK))
+        for q in range(4):
+            nc.sync.dma_start(
+                out=v_sc[QUAD * q : QUAD * q + 4, :, :].bitcast(I32),
+                in_=v_sc_packed[8 * q : 8 * q + 8, :].bitcast(I32),
+            )
         for c in range(2):
             nc.vector.tensor_copy(
                 v_codes[1][:, BANK * c : BANK * (c + 1)],
@@ -284,7 +294,6 @@ def tile_list_playlist_slot_refresh_kernel(
         for c in range(4):
             half = dealt_near if c < 2 else dealt_far
             x_f32[0, c] = as_planes(half)[:, :, CHUNK * (c % 2) : CHUNK * (c % 2 + 1)]
-        nc.sync.dma_start(idx2[:], offs2)
         load_page(0, 0)
         nc.sync.dma_start(out=gains_rows[:, 0:BANK], in_=wgs[:, 0:BANK])
         features(0, 0, "h0")
@@ -301,7 +310,6 @@ def tile_list_playlist_slot_refresh_kernel(
         features(0, 2, "h2")
         load_page(0, 1)
         put(0, 1, 0, S)
-        nc.sync.dma_start(idx3[:], offs3)
         stage_w3(0, 0, HALF, "R0")
         prep_w3(0, 0, HALF, "sb0")
         fetch_rows(0, "R0")
@@ -317,8 +325,6 @@ def tile_list_playlist_slot_refresh_kernel(
         prep_w1_planes(0)
         fetch_rows(1, "B0")
         prep_w1_planes(1)
-        nc.sync.dma_start(out=b1_planes[:], in_=b1[PASS : 2 * PASS].rearrange("(p i) -> p i", i=PACK))
-        nc.sync.dma_start(out=b2_sb[:], in_=b2.rearrange("(a p i) -> p a i", a=2, i=PACK))
         load_page(0, 3)
         put(0, 3, 0, S)
         order_w2_words(1, 0, "h0")

@@ -148,8 +148,8 @@ def tile_list_playlist_slot_refresh_kernel(
             h = tile([P, S], F32, slot, "h%d%d" % (b, i))
             bias = b1_planes[:, i : i + 1] if b == 1 else b1_rows[:, i - 1 : i] if i > 0 else b1_first[:]
             accs = [bank(2 * i + c, "acc_h%d" % c) for c in range(2)]
-            for a in range(2):
-                for c in range(2):
+            for c in range(2):
+                for a in range(2):
                     nc.tensor.matmul_mx(
                         out=accs[c][:],
                         lhsT=w1_codes[a, b, i].bitcast(FP8X4),
@@ -234,6 +234,8 @@ def tile_list_playlist_slot_refresh_kernel(
 
         def load_w2():
             nc.sync.dma_start(out=w2_raw[:].bitcast(I32), in_=w2_words.rearrange("a p c -> p a c").bitcast(I32))
+
+        def load_w2_scales():
             for q in range(4):
                 nc.sync.dma_start(
                     out=w2_sc_raw[QUAD * q : QUAD * q + 8, :].bitcast(I32),
@@ -310,12 +312,10 @@ def tile_list_playlist_slot_refresh_kernel(
         features(0, 2, "h2")
         load_page(0, 1)
         put(0, 1, 0, S)
-        stage_w3(0, 0, HALF, "R0")
-        prep_w3(0, 0, HALF, "sb0")
-        fetch_rows(0, "R0")
         load_w1_rows(3, 4, 0)
         load_w1_rows(3, 4, 1)
         prep_w1_rows(3, 3, "wb1")
+        fetch_rows(0, "R3")
         features(0, 3, "h0")
         load_w2()
         order_w2_words(0, 0, "h1")
@@ -328,20 +328,23 @@ def tile_list_playlist_slot_refresh_kernel(
         load_page(0, 3)
         put(0, 3, 0, S)
         order_w2_words(1, 0, "h0")
+        stage_w3(0, 0, HALF, "R0")
+        prep_w3(0, 0, HALF, "sb0")
         stage_w3(0, HALF, N, "R1")
         prep_w3(0, HALF, N, "sb1")
         fetch_rows(2, "R1")
-        features(1, 0, "R3")
+        features(1, 0, "R0")
         features(1, 1, "h3")
         load_gains(0)
         load_page(1, 0)
         put(1, 0, 0, S)
-        order_w2_words(1, 1, "R3")
+        order_w2_words(1, 1, "R0")
         stage_w3(1, HALF, N, "B1")
         prep_w3(1, HALF, N, "sb0")
         fetch_rows(3, "B1")
         load_gains(1)
         load_page(1, 1)
+        load_w2_scales()
         deal(dealt_near, 0, x_rows[0][:])
         deal(dealt_near, 1, x_rows[1][:])
         load_gains(2)
@@ -352,9 +355,9 @@ def tile_list_playlist_slot_refresh_kernel(
         load_gains(3)
         load_page(1, 3)
         put(1, 1, 0, S)
-        features(1, 2, "R0")
+        features(1, 2, "R3")
         put(1, 2, 0, S)
-        order_w2_scales("R0")
+        order_w2_scales("R3")
         prep_w3(1, 0, HALF, "sb1")
         features(1, 3, "B0")
         fetch(0)
@@ -373,17 +376,15 @@ def tile_list_playlist_slot_refresh_kernel(
         def gate_passes(a, b, c):
             for i in range(PACK):
                 acc = gate_banks[b, c][i // 2]
-                for u in range(2):
-                    col = CHUNK * (i % 2) + P * u
-                    nc.tensor.matmul_mx(
-                        out=acc[:, col : col + P],
-                        lhsT=w2_codes[a, b][:, 2 * P * i : 2 * P * (i + 1)].bitcast(FP4X4),
-                        lhsT_scale=w2_sc[a, b][:, P * i : P * (i + 1)],
-                        rhs=x_codes[a, c][:, P * u : P * (u + 1)].bitcast(FP8X4),
-                        rhs_scale=x_sc[a, c][:, P * u : P * (u + 1)],
-                        start=(a == 0 and col == 0),
-                        stop=(a == 1 and col == BANK - P),
-                    )
+                nc.tensor.matmul_mx(
+                    out=acc[:, CHUNK * (i % 2) : CHUNK * (i % 2 + 1)],
+                    lhsT=w2_codes[a, b][:, 2 * P * i : 2 * P * (i + 1)].bitcast(FP4X4),
+                    lhsT_scale=w2_sc[a, b][:, P * i : P * (i + 1)],
+                    rhs=x_codes[a, c].bitcast(FP8X4),
+                    rhs_scale=x_sc[a, c],
+                    start=(a == 0 and i % 2 == 0),
+                    stop=(a == 1 and i % 2 == 1),
+                )
 
         def open_gate(b, c, first):
             gate_banks[b, c] = [bank(first + u, "acc_g%d%d%d" % (b, c, u)) for u in range(2)]
@@ -459,7 +460,10 @@ def tile_list_playlist_slot_refresh_kernel(
 
         def far_rows(t, dst):
             gather(dst, pages[0, t], BANK, M)
-            deal(dealt_far, t, dst)
+            for c in range(2):
+                nc.sync.dma_start(
+                    out=x_f32[0, 2 + c][QUAD * t : QUAD * (t + 1), :, :], in_=dst[:, CHUNK * c : CHUNK * (c + 1)]
+                )
 
         def far_planes(c, dst):
             x_f32[1, c] = as_planes(dst)
@@ -493,8 +497,8 @@ def tile_list_playlist_slot_refresh_kernel(
         gated(nc.gpsimd, 0, 0, 4)
         gated(nc.gpsimd, 1, 0, 4)
         xb = tile([P, 2 * PACK * CHUNK], BF16, "B1", "xb2")
-        weave(xb[:, PACK * CHUNK :], x_f32[1, 2])
         weave(xb[:, 0 : PACK * CHUNK], x_f32[0, 2])
+        weave(xb[:, PACK * CHUNK :], x_f32[1, 2])
         quant_x([(0, 2), (1, 2)], xb[:])
         quant_z(0, "wc10")
         held = tile([P, 4 * PACK * CHUNK], BF16, "B1", "held")

@@ -26,6 +26,38 @@ LIST_COLS = BANK // 16
 CHUNK = HALF
 
 
+AREA_SIZES = (
+    ("P00", 8192), ("P01", 8192), ("P02", 8192), ("P03", 8192),
+    ("P10", 8192), ("P11", 8192), ("P12", 8192), ("P13", 8192),
+    ("A", 16384), ("GR", 4096), ("G1", 8192),
+    ("R0", 4096), ("R1", 8192), ("R3", 4096), ("B0", 8192), ("B1", 8192), ("G0", 12288), ("XN", 8192),
+    ("tab_sc", 2048), ("v_sc", 2048), ("v_scp", 1024), ("v0", 4096), ("v1", 4096),
+    ("w2_raw", 4096), ("w2_sc_raw", 1024), ("w2_sc_moved", 1024),
+    ("wb0", 4096), ("wb1", 4096), ("sb0", 2048), ("sb1", 2048),
+    ("h3", 4096), ("h0", 4096), ("h1", 4096), ("h2", 4096),
+    ("wc00", 1024), ("wc01", 1024), ("wc02", 1024), ("wc03", 1024), ("wc10", 2048), ("wc11", 2048),
+    ("ws00", 256), ("ws01", 256), ("ws02", 256), ("ws03", 256), ("ws10", 512), ("ws11", 512),
+    ("w3c0", 2048), ("w3c1", 2048), ("w3s0", 512), ("w3s1", 512),
+    ("gate11", 4096), ("x11", 1024),
+    ("x00", 2048), ("x10", 1024), ("x02", 2048),
+    ("x00s", 512), ("x10s", 256), ("x11s", 256), ("x02s", 256), ("x12s", 256), ("x03s", 256), ("x13s", 256),
+    ("z0s", 512), ("z10s", 256), ("z11s", 256), ("z20s", 256), ("z21s", 256), ("z30s", 256), ("z31s", 256), ("z31", 1024),
+    ("b1f", 64), ("b1r", 64), ("b1p", 64), ("b2", 64),
+)
+
+
+def area_offsets():
+    starts = {}
+    at = 0
+    for area, size in AREA_SIZES:
+        starts[area] = at
+        at = at + size
+    return starts
+
+
+AREA = area_offsets()
+
+
 def tile_list_playlist_slot_refresh_kernel(
     tc, tab_words, tab_scales, offs, offs2, offs3, w1, b1, wgs, page0, w2_words, w2_scales, b2, w3, out
 ):
@@ -35,9 +67,9 @@ def tile_list_playlist_slot_refresh_kernel(
         sb = ctx.enter_context(tc.tile_pool(name="sb", bufs=1))
         psum = ctx.enter_context(tc.psum_pool(name="psum", bufs=1))
 
-        def tile(shape, dtype, slot, name):
-            align = 256 if slot[0] in "ABGPRX" or slot in ("tab_sc", "v_sc", "w2_raw") else 64
-            return sb.tile(shape, dtype, tag=slot, name=name, align_bytes=align)
+        def tile(shape, dtype, area, name, at=0):
+            start = AREA[area] + at
+            return sb.tile(shape, dtype, name=name, offset=start, align_bytes=256 if start % 256 == 0 else 64)
 
         def bank(k, name):
             return psum.tile([P, BANK], F32, tag="bank%d" % k, name=name)
@@ -194,16 +226,16 @@ def tile_list_playlist_slot_refresh_kernel(
         x_codes = {}
         x_sc = {}
 
-        def quantise(name, slot, woven):
+        def quantise(name, slot, woven, at=0):
             width = woven.shape[1] // PACK
-            codes = tile([P, width], U32, slot, name + "_codes")
+            codes = tile([P, width], U32, slot, name + "_codes", at)
             scales = tile([P, width], U8, name + "s", name + "_sc")
             nc.vector.quantize_mx(out=codes[:].bitcast(FP8X4), scales=scales[:], in_=woven)
             return codes, scales
 
-        def quant_x(keys, woven):
+        def quant_x(keys, woven, slot, at=0):
             name = "x%d%d" % keys[0]
-            codes, scales = quantise(name, name, woven)
+            codes, scales = quantise(name, slot, woven, at)
             for j, key in enumerate(keys):
                 x_codes[key] = codes[:, CHUNK * j : CHUNK * (j + 1)]
                 x_sc[key] = scales[:, CHUNK * j : CHUNK * (j + 1)]
@@ -290,12 +322,12 @@ def tile_list_playlist_slot_refresh_kernel(
                 v_codes[1][:, BANK * c : BANK * (c + 1)],
                 tab_window(1).indirect(idx[:, LIST_COLS * c : LIST_COLS * (c + 1)]),
             )
-        x_dealt = tile([P, PACK * M], F32, "A", "x_dealt")
-        dealt_near = x_dealt[:, 0 : PACK * BANK]
-        dealt_far = x_dealt[:, PACK * BANK :]
-        for c in range(4):
-            half = dealt_near if c < 2 else dealt_far
-            x_f32[0, c] = as_planes(half)[:, :, CHUNK * (c % 2) : CHUNK * (c % 2 + 1)]
+        dealt_near = tile([P, PACK * BANK], F32, "A", "dealt_near")[:]
+        dealt_far = {}
+        for c in range(2):
+            x_f32[0, c] = as_planes(dealt_near)[:, :, CHUNK * c : CHUNK * (c + 1)]
+            dealt_far[2 + c] = tile([P, PACK * CHUNK], F32, "A", "dealt%d" % (2 + c), 8192 + 4096 * c)
+            x_f32[0, 2 + c] = as_planes(dealt_far[2 + c][:])
         load_page(0, 0)
         nc.sync.dma_start(out=gains_rows[:, 0:BANK], in_=wgs[:, 0:BANK])
         features(0, 0, "h0")
@@ -365,7 +397,7 @@ def tile_list_playlist_slot_refresh_kernel(
         fetch(2)
         xb = tile([P, BANK * PACK], BF16, "wb0", "xb_near")
         weave(xb[:], as_planes(dealt_near))
-        quant_x([(0, 0), (0, 1)], xb[:])
+        quant_x([(0, 0), (0, 1)], xb[:], "x00")
 
         gate_banks = {}
         gates = {}
@@ -401,25 +433,28 @@ def tile_list_playlist_slot_refresh_kernel(
                     bias=b2_sb[:, b, i : i + 1],
                 )
 
-        def gate_tile(slot, name):
-            return as_planes(tile([P, PACK * CHUNK], F32, slot, name)[:])
+        def gate_tile(slot, name, at=0):
+            return as_planes(tile([P, PACK * CHUNK], F32, slot, name, at)[:])
 
         def gated(engine, b, c, run):
             engine.tensor_tensor(
-                zbs[c][:, PACK * CHUNK * b : PACK * CHUNK * (b + 1)].rearrange("p (m e t) -> p m t e", e=run, t=PACK),
+                zbs[b, c].rearrange("p (m e t) -> p m t e", e=run, t=PACK),
                 x_f32[b, c].rearrange("p t (m e) -> p m t e", e=run),
                 gates[b, c].rearrange("p t (m e) -> p m t e", e=run),
                 MULT,
             )
 
-        def quant_z(c, slot):
-            codes, scales = quantise("z%d" % c, slot, zbs[c])
+        def z_tile(b, c, slot, at=0):
+            zbs[b, c] = tile([P, PACK * CHUNK], BF16, slot, "zb%d%d" % (b, c), at)[:]
+
+        def quant_z(c, slot, both, at=0):
+            codes, scales = quantise("z%d" % c, slot, both, at)
             for b in range(2):
                 z_codes[b, c] = codes[:, CHUNK * b : CHUNK * (b + 1)]
                 z_sc[b, c] = scales[:, CHUNK * b : CHUNK * (b + 1)]
 
-        def quant_z_part(b, c, slot):
-            codes, scales = quantise("z%d%d" % (c, b), slot, zbs[c][:, PACK * CHUNK * b : PACK * CHUNK * (b + 1)])
+        def quant_z_part(b, c, slot, at=0):
+            codes, scales = quantise("z%d%d" % (c, b), slot, zbs[b, c], at)
             z_codes[b, c] = codes[:]
             z_sc[b, c] = scales[:]
 
@@ -458,12 +493,9 @@ def tile_list_playlist_slot_refresh_kernel(
                 copy(out=staged[:, n, :], in_=accs[n][:, 0:CHUNK])
                 nc.sync.dma_start(out=out[P * n : P * (n + 1), CHUNK * c : CHUNK * (c + 1)], in_=staged[:, n, :])
 
-        def far_rows(t, dst):
-            gather(dst, pages[0, t], BANK, M)
-            for c in range(2):
-                nc.sync.dma_start(
-                    out=x_f32[0, 2 + c][QUAD * t : QUAD * (t + 1), :, :], in_=dst[:, CHUNK * c : CHUNK * (c + 1)]
-                )
+        def far_rows(c, t, dst):
+            gather(dst, pages[0, t], CHUNK * c, CHUNK * (c + 1))
+            deal(dealt_far[c], t, dst)
 
         def far_planes(c, dst):
             x_f32[1, c] = as_planes(dst)
@@ -476,56 +508,71 @@ def tile_list_playlist_slot_refresh_kernel(
         put(1, 3, 0, S)
         for c in range(2):
             gather(x_f32[1, c][:, PACK - 1, :], pages[1, PACK - 1], CHUNK * c, CHUNK * (c + 1))
-        far_rows(0, tile([P, BANK], F32, "G1", "rows_a")[:])
-        xb = tile([P, PACK * CHUNK], BF16, "B0", "xb10")
-        weave(xb[:], x_f32[1, 0])
-        quant_x([(1, 0)], xb[:])
-        far_rows(1, tile([P, BANK], F32, "B0", "rows_b")[:])
-        xb = tile([P, PACK * CHUNK], BF16, "G0", "xb11")
-        weave(xb[:], x_f32[1, 1])
-        quant_x([(1, 1)], xb[:])
-        far = tile([P, 3 * PACK * CHUNK], F32, "G0", "far")
+        rows = tile([P, 2, CHUNK], F32, "G1", "rows_a")
         for t in range(2):
-            far_rows(2 + t, far[:, BANK * t : BANK * (t + 1)])
-        far_planes(2, far[:, PACK * CHUNK : 2 * PACK * CHUNK])
-        far_planes(3, far[:, 2 * PACK * CHUNK :])
-        close_gate(0, 0, gate_tile("B1", "gate00"))
+            far_rows(2, t, rows[:, t, :])
+        xb = tile([P, PACK * CHUNK], BF16, "B0", "xb10", 6144)
+        weave(xb[:], x_f32[1, 0])
+        quant_x([(1, 0)], xb[:], "x10")
+        rows = tile([P, 2, CHUNK], F32, "B1", "rows_b", -256)
+        for t in range(2):
+            far_rows(2, 2 + t, rows[:, t, :])
+        xb = tile([P, PACK * CHUNK], BF16, "G0", "xb11", 2048)
+        weave(xb[:], x_f32[1, 1])
+        quant_x([(1, 1)], xb[:], "x11")
+        rows = tile([P, PACK, CHUNK], F32, "G0", "rows_c", -1792)
+        for t in range(PACK):
+            far_rows(3, t, rows[:, t, :])
+        far = tile([P, 2 * PACK * CHUNK], F32, "G0", "far", 2304)
+        for c in (2, 3):
+            far_planes(c, far[:, PACK * CHUNK * (c - 2) : PACK * CHUNK * (c - 1)])
+        first_gate = tile([P, PACK * CHUNK + 128], F32, "B1", "gate00", 2048 - 256)
+        close_gate(0, 0, as_planes(first_gate[:, 0 : PACK * CHUNK]))
         close_gate(1, 0, gate_tile("wb1", "gate10"))
         close_gate(0, 1, gate_tile("R1", "gate01"))
-        close_gate(1, 1, gate_tile("zb1", "gate11"))
-        zbs[0] = tile([P, 2 * PACK * CHUNK], BF16, "wb0", "zb0")[:]
+        close_gate(1, 1, gate_tile("gate11", "gate11"))
+        zb0 = tile([P, 2 * PACK * CHUNK], BF16, "wb0", "zb0")
+        for b in range(2):
+            zbs[b, 0] = zb0[:, PACK * CHUNK * b : PACK * CHUNK * (b + 1)]
         gated(nc.gpsimd, 0, 0, 4)
         gated(nc.gpsimd, 1, 0, 4)
-        xb = tile([P, 2 * PACK * CHUNK], BF16, "B1", "xb2")
-        weave(xb[:, 0 : PACK * CHUNK], x_f32[0, 2])
-        weave(xb[:, PACK * CHUNK :], x_f32[1, 2])
-        quant_x([(0, 2), (1, 2)], xb[:])
-        quant_z(0, "wc10")
-        held = tile([P, 4 * PACK * CHUNK], BF16, "B1", "held")
-        xb = held[:, 0 : 2 * PACK * CHUNK]
-        zbs[1] = held[:, 2 * PACK * CHUNK :]
-        weave(xb[:, 0 : PACK * CHUNK], x_f32[0, 3])
-        weave(xb[:, PACK * CHUNK :], x_f32[1, 3])
+        late = {}
+        for c in (2, 3):
+            for b in range(2):
+                late[b, c] = tile([P, PACK * CHUNK], BF16, "B1", "xb%d%d" % (b, c), 2048 * ((1 - b, 2 + b)[c - 2]))
+                weave(late[b, c][:], x_f32[b, c])
+        for b in range(2):
+            quant_x([(b, 2)], late[b, 2][:], "G0", 1024 * b)
+        quant_z(0, "B1", zb0[:], 2048)
+        z_tile(0, 1, "B1")
         gated(nc.vector, 0, 1, 2)
+        quant_x([(0, 3)], late[0, 3][:], "wb0")
+        z_tile(1, 1, "R1")
         gated(nc.vector, 1, 1, 2)
-        quant_x([(0, 3), (1, 3)], xb)
-        quant_z(1, "wc11")
+        quant_x([(1, 3)], late[1, 3][:], "wb0", 1024)
+        quant_z_part(0, 1, "wc11")
         open_gate(0, 2, 0)
         close_gate(0, 2, gate_tile("P03", "gate02"))
         open_gate(1, 2, 2)
         close_gate(1, 2, gate_tile("P00", "gate12"))
-        for b in range(2):
-            open_gate(b, 3, 4 + 2 * b)
-            close_gate(b, 3, gate_tile("P0%d" % (1 + b), "gate%d3" % b))
-        zbs[2] = tile([P, 2 * PACK * CHUNK], BF16, "wb0", "zb2")[:]
-        zbs[3] = tile([P, 2 * PACK * CHUNK], BF16, "wb1", "zb3")[:]
+        scores(0, 4, nc.scalar.copy, tile([P, PACK * CHUNK], F32, "P13", "staged0")[:])
+        open_gate(0, 3, 6)
+        close_gate(0, 3, gate_tile("P01", "gate03"))
+        open_gate(1, 3, 0)
+        close_gate(1, 3, gate_tile("P02", "gate13"))
+        z_tile(0, 2, "R1", 2048)
         gated(nc.vector, 0, 2, 2)
+        quant_z_part(1, 1, "wc11", 1024)
+        z_tile(1, 2, "gate11")
         gated(nc.vector, 1, 2, 2)
+        quant_z_part(0, 2, "v0")
+        z_tile(0, 3, "B0")
         gated(nc.vector, 0, 3, 2)
-        quant_z(2, "v0")
+        quant_z_part(1, 2, "v0", 1024)
+        z_tile(1, 3, "B0", 2048)
         gated(nc.vector, 1, 3, 2)
         quant_z_part(0, 3, "v1")
         quant_z_part(1, 3, "z31")
-        for c in range(3):
-            scores(c, 2 * c, nc.scalar.copy, tile([P, PACK * CHUNK], F32, "P1%d" % c, "staged%d" % c)[:])
-        last_scores(3, (6, 7, 0, 1), "P13")
+        scores(1, 6, nc.scalar.copy, tile([P, PACK * CHUNK], F32, "P11", "staged1")[:])
+        scores(2, 4, nc.scalar.copy, tile([P, PACK * CHUNK], F32, "P12", "staged2")[:])
+        last_scores(3, (2, 3, 0, 1), "P10")

@@ -42,7 +42,7 @@ AREA_SIZES = (
     ("x00", 2048), ("x10", 1024), ("x02", 2048),
     ("x00s", 512), ("x10s", 256), ("x11s", 256), ("x02s", 256), ("x12s", 256), ("x03s", 256), ("x13s", 256),
     ("z0s", 512), ("z10s", 256), ("z11s", 256), ("z20s", 256), ("z21s", 256), ("z30s", 256), ("z31s", 256), ("z31", 1024),
-    ("b1f", 64), ("b1r", 64), ("b1p", 64), ("b2", 64),
+    ("warm", 64), ("b1f", 64), ("b1r", 64), ("b1p", 64), ("b2", 64),
 )
 
 
@@ -302,6 +302,8 @@ def tile_list_playlist_slot_refresh_kernel(
             nc.sync.dma_start(out=tab_sc[a:QUAD:2, :].bitcast(I32), in_=tab_scales[a].bitcast(I32))
         load_tab(0)
         nc.sync.dma_start(out=b1_first[:], in_=b1[0:P].rearrange("(p t) -> p t", t=1))
+        warm = tile([P, 1], F32, "warm", "warm")
+        nc.scalar.activation(out=warm[:], in_=b1_first[:], func=ACT.Sigmoid)
         nc.sync.dma_start(idx2[:], offs2)
         nc.sync.dma_start(idx3[:], offs3)
         nc.sync.dma_start(out=b1_planes[:], in_=b1[PASS : 2 * PASS].rearrange("(p i) -> p i", i=PACK))

@@ -39,8 +39,8 @@ AREA_SIZES = (
     ("ws00", 256), ("ws01", 256), ("ws02", 256), ("ws03", 256), ("ws10", 512), ("ws11", 512),
     ("w3c0", 2048), ("w3c1", 2048), ("w3s0", 512), ("w3s1", 512),
     ("gate11", 4096), ("x11", 1024),
-    ("x00", 2048), ("x10", 1024), ("x02", 2048),
-    ("x00s", 512), ("x10s", 256), ("x11s", 256), ("x02s", 256), ("x12s", 256), ("x03s", 256), ("x13s", 256),
+    ("x00", 2048), ("x10", 1024),
+    ("x00s", 512), ("x10s", 256), ("x11s", 256), ("x02s", 512), ("x03s", 512),
     ("z0s", 512), ("z10s", 256), ("z11s", 256), ("z20s", 256), ("z21s", 256), ("z30s", 256), ("z31s", 256), ("z31", 1024),
     ("warm", 64), ("b1f", 64), ("b1r", 64), ("b1p", 64), ("b2", 64),
 )
@@ -519,13 +519,13 @@ def tile_list_playlist_slot_refresh_kernel(
         rows = tile([P, 2, CHUNK], F32, "B1", "rows_b", -256)
         for t in range(2):
             far_rows(2, 2 + t, rows[:, t, :])
-        xb = tile([P, PACK * CHUNK], BF16, "G0", "xb11", 2048)
+        xb = tile([P, PACK * CHUNK], BF16, "G0", "xb11", 3584)
         weave(xb[:], x_f32[1, 1])
         quant_x([(1, 1)], xb[:], "x11")
-        rows = tile([P, PACK, CHUNK], F32, "G0", "rows_c", -1792)
+        rows = tile([P, PACK, CHUNK], F32, "G0", "rows_c", -256)
         for t in range(PACK):
             far_rows(3, t, rows[:, t, :])
-        far = tile([P, 2 * PACK * CHUNK], F32, "G0", "far", 2304)
+        far = tile([P, 2 * PACK * CHUNK], F32, "G0", "far", 4096)
         for c in (2, 3):
             far_planes(c, far[:, PACK * CHUNK * (c - 2) : PACK * CHUNK * (c - 1)])
         first_gate = tile([P, PACK * CHUNK + 128], F32, "B1", "gate00", 2048 - 256)
@@ -540,27 +540,24 @@ def tile_list_playlist_slot_refresh_kernel(
         gated(nc.gpsimd, 1, 0, 4)
         late = {}
         for c in (2, 3):
+            late[c] = tile([P, 2 * PACK * CHUNK], BF16, "B1", "xb%d" % c, 4096 * (c - 2))
             for b in range(2):
-                late[b, c] = tile([P, PACK * CHUNK], BF16, "B1", "xb%d%d" % (b, c), 2048 * ((1 - b, 2 + b)[c - 2]))
-                weave(late[b, c][:], x_f32[b, c])
-        for b in range(2):
-            quant_x([(b, 2)], late[b, 2][:], "G0", 1024 * b)
-        quant_z(0, "B1", zb0[:], 2048)
+                weave(late[c][:, PACK * CHUNK * b : PACK * CHUNK * (b + 1)], x_f32[b, c])
+        quant_x([(0, 2), (1, 2)], late[2][:], "G0")
+        quant_z(0, "G0", zb0[:], 2048)
         z_tile(0, 1, "B1")
         gated(nc.vector, 0, 1, 2)
-        quant_x([(0, 3)], late[0, 3][:], "wb0")
+        quant_x([(0, 3), (1, 3)], late[3][:], "wb0")
         z_tile(1, 1, "R1")
         gated(nc.vector, 1, 1, 2)
-        quant_x([(1, 3)], late[1, 3][:], "wb0", 1024)
         quant_z_part(0, 1, "wc11")
         open_gate(0, 2, 0)
         close_gate(0, 2, gate_tile("P03", "gate02"))
         open_gate(1, 2, 2)
         close_gate(1, 2, gate_tile("P00", "gate12"))
-        scores(0, 4, nc.scalar.copy, tile([P, PACK * CHUNK], F32, "P13", "staged0")[:])
-        open_gate(0, 3, 6)
+        open_gate(0, 3, 4)
         close_gate(0, 3, gate_tile("P01", "gate03"))
-        open_gate(1, 3, 0)
+        open_gate(1, 3, 6)
         close_gate(1, 3, gate_tile("P02", "gate13"))
         z_tile(0, 2, "R1", 2048)
         gated(nc.vector, 0, 2, 2)
@@ -575,6 +572,7 @@ def tile_list_playlist_slot_refresh_kernel(
         gated(nc.vector, 1, 3, 2)
         quant_z_part(0, 3, "v1")
         quant_z_part(1, 3, "z31")
-        scores(1, 6, nc.scalar.copy, tile([P, PACK * CHUNK], F32, "P11", "staged1")[:])
+        scores(0, 2, nc.scalar.copy, tile([P, PACK * CHUNK], F32, "P13", "staged0")[:])
+        scores(1, 0, nc.scalar.copy, tile([P, PACK * CHUNK], F32, "P11", "staged1")[:])
         scores(2, 4, nc.scalar.copy, tile([P, PACK * CHUNK], F32, "P12", "staged2")[:])
-        last_scores(3, (2, 3, 0, 1), "P10")
+        last_scores(3, (6, 7, 2, 3), "P10")

@@ -41,7 +41,7 @@ AREA_SIZES = (
     ("gate11", 4096), ("x11", 1024),
     ("x00", 2048), ("x10", 1024),
     ("x00s", 512), ("x10s", 256), ("x11s", 256), ("x02s", 512), ("x03s", 512),
-    ("z0s", 512), ("z10s", 256), ("z11s", 256), ("z20s", 256), ("z21s", 256), ("z30s", 256), ("z31s", 256), ("z31", 1024),
+    ("z0s", 512), ("z10s", 256), ("z11s", 256), ("z20s", 256), ("z21s", 256), ("zas", 256), ("zb0s", 128), ("zb1s", 128), ("zb", 1024),
     ("warm", 64), ("b1f", 64), ("b1r", 64), ("b1p", 64), ("b2", 64),
 )
 
@@ -115,9 +115,10 @@ def tile_list_playlist_slot_refresh_kernel(
         w1_codes = {}
         w1_sc = {}
 
-        def load_tab(a):
+        def load_tab(a, lo, hi):
             nc.sync.dma_start(
-                out=tab_w[:, T * a : T * (a + 1)], in_=tab_words[a].rearrange("p t i -> p (t i)").bitcast(I32)
+                out=tab_w[:, T * a + lo : T * a + hi],
+                in_=tab_words[a].rearrange("p t i -> p (t i)").bitcast(I32)[:, lo:hi],
             )
 
         def tab_window(a):
@@ -176,25 +177,25 @@ def tile_list_playlist_slot_refresh_kernel(
 
         hs = {}
 
-        def features(b, i, slot):
+        def features(b, i, slot, cuts=(0, BANK, S), first_bank=None):
             h = tile([P, S], F32, slot, "h%d%d" % (b, i))
             bias = b1_planes[:, i : i + 1] if b == 1 else b1_rows[:, i - 1 : i] if i > 0 else b1_first[:]
-            accs = [bank(2 * i + c, "acc_h%d" % c) for c in range(2)]
-            for c in range(2):
+            spans = list(zip(cuts, cuts[1:]))
+            start = 2 * i if first_bank is None else first_bank
+            accs = [bank(start + c, "acc_h%d" % c) for c in range(len(spans))]
+            for acc, (lo, hi) in zip(accs, spans):
                 for a in range(2):
                     nc.tensor.matmul_mx(
-                        out=accs[c][:],
+                        out=acc[:, 0 : hi - lo],
                         lhsT=w1_codes[a, b, i].bitcast(FP8X4),
                         lhsT_scale=w1_sc[a, b, i],
-                        rhs=v_codes[a][:, BANK * c : BANK * (c + 1)].bitcast(FP8X4),
-                        rhs_scale=v_sc[:, a, BANK * c : BANK * (c + 1)],
+                        rhs=v_codes[a][:, lo:hi].bitcast(FP8X4),
+                        rhs_scale=v_sc[:, a, lo:hi],
                         start=(a == 0),
                         stop=(a == 1),
                     )
-            for c in range(2):
-                nc.scalar.activation(
-                    out=h[:, BANK * c : BANK * (c + 1)], in_=accs[c][:], func=ACT.Identity, bias=bias
-                )
+            for acc, (lo, hi) in zip(accs, spans):
+                nc.scalar.activation(out=h[:, lo:hi], in_=acc[:, 0 : hi - lo], func=ACT.Identity, bias=bias)
             hs[b, i] = h
 
         def put(b, i, lo, hi):
@@ -300,30 +301,27 @@ def tile_list_playlist_slot_refresh_kernel(
         nc.sync.dma_start(idx[:], offs)
         for a in range(2):
             nc.sync.dma_start(out=tab_sc[a:QUAD:2, :].bitcast(I32), in_=tab_scales[a].bitcast(I32))
-        load_tab(0)
+        load_tab(0, 0, T)
         nc.sync.dma_start(out=b1_first[:], in_=b1[0:P].rearrange("(p t) -> p t", t=1))
         warm = tile([P, 1], F32, "warm", "warm")
         nc.scalar.activation(out=warm[:], in_=b1_first[:], func=ACT.Sigmoid)
         nc.sync.dma_start(idx2[:], offs2)
-        nc.sync.dma_start(idx3[:], offs3)
-        nc.sync.dma_start(out=b1_planes[:], in_=b1[PASS : 2 * PASS].rearrange("(p i) -> p i", i=PACK))
         nc.vector.tensor_copy(v_sc_packed[:], tab_sc[:].indirect(idx[:]))
         nc.vector.tensor_copy(v_codes[0][:], tab_window(0).indirect(idx[:]))
         load_w1_rows(0, 1, 0)
         load_w1_rows(0, 1, 1)
         prep_w1_rows(0, 0, "wb0")
-        load_tab(1)
-        nc.sync.dma_start(out=b2_sb[:], in_=b2.rearrange("(a p i) -> p a i", a=2, i=PACK))
+        load_tab(1, 0, T // 2)
+        load_tab(1, T // 2, T)
+        nc.sync.dma_start(idx3[:], offs3)
         for q in range(4):
             nc.sync.dma_start(
                 out=v_sc[QUAD * q : QUAD * q + 4, :, :].bitcast(I32),
                 in_=v_sc_packed[8 * q : 8 * q + 8, :].bitcast(I32),
             )
-        for c in range(2):
-            nc.vector.tensor_copy(
-                v_codes[1][:, BANK * c : BANK * (c + 1)],
-                tab_window(1).indirect(idx[:, LIST_COLS * c : LIST_COLS * (c + 1)]),
-            )
+        first_cuts = (0, HALF, BANK, S)
+        for lo, hi in zip(first_cuts, first_cuts[1:]):
+            nc.vector.tensor_copy(v_codes[1][:, lo:hi], tab_window(1).indirect(idx[:, lo // 16 : hi // 16]))
         dealt_near = tile([P, PACK * BANK], F32, "A", "dealt_near")[:]
         dealt_far = {}
         for c in range(2):
@@ -332,7 +330,7 @@ def tile_list_playlist_slot_refresh_kernel(
             x_f32[0, 2 + c] = as_planes(dealt_far[2 + c][:])
         load_page(0, 0)
         nc.sync.dma_start(out=gains_rows[:, 0:BANK], in_=wgs[:, 0:BANK])
-        features(0, 0, "h0")
+        features(0, 0, "h0", first_cuts, 5)
         put(0, 0, 0, BANK)
         load_w1_rows(1, 3, 0)
         load_w1_rows(1, 3, 1)
@@ -354,6 +352,8 @@ def tile_list_playlist_slot_refresh_kernel(
         load_w2()
         order_w2_words(0, 0, "h1")
         load_page(0, 2)
+        nc.sync.dma_start(out=b1_planes[:], in_=b1[PASS : 2 * PASS].rearrange("(p i) -> p i", i=PACK))
+        nc.sync.dma_start(out=b2_sb[:], in_=b2.rearrange("(a p i) -> p a i", a=2, i=PACK))
         put(0, 2, 0, S)
         order_w2_words(0, 1, "h2")
         prep_w1_planes(0)
@@ -438,13 +438,16 @@ def tile_list_playlist_slot_refresh_kernel(
         def gate_tile(slot, name, at=0):
             return as_planes(tile([P, PACK * CHUNK], F32, slot, name, at)[:])
 
-        def gated(engine, b, c, run):
+        def product(engine, dst, b, c, lo, hi, run):
             engine.tensor_tensor(
-                zbs[b, c].rearrange("p (m e t) -> p m t e", e=run, t=PACK),
-                x_f32[b, c].rearrange("p t (m e) -> p m t e", e=run),
-                gates[b, c].rearrange("p t (m e) -> p m t e", e=run),
+                dst.rearrange("p (m e t) -> p m t e", e=run, t=PACK),
+                x_f32[b, c][:, :, lo:hi].rearrange("p t (m e) -> p m t e", e=run),
+                gates[b, c][:, :, lo:hi].rearrange("p t (m e) -> p m t e", e=run),
                 MULT,
             )
+
+        def gated(engine, b, c, run):
+            product(engine, zbs[b, c], b, c, 0, CHUNK, run)
 
         def z_tile(b, c, slot, at=0):
             zbs[b, c] = tile([P, PACK * CHUNK], BF16, slot, "zb%d%d" % (b, c), at)[:]
@@ -484,16 +487,26 @@ def tile_list_playlist_slot_refresh_kernel(
                     in_=part.rearrange("p (j m) -> p j m", j=2),
                 )
 
-        def last_scores(c, banks, slot):
-            staged = tile([P, N // P, CHUNK], F32, slot, "staged%d" % c)
-            accs = [bank(k, "acc_o%d%d" % (c, k)) for k in banks]
+        def piece_scores(col, banks, copies, staged):
+            accs = [bank(k, "acc_e%d%d" % (col, k)) for k in banks]
             for b in range(2):
                 for n in range(N // P):
-                    score_pass(accs[n][:, 0:CHUNK], n, b, c)
-            for n in range(N // P):
-                copy = nc.vector.tensor_copy if n % 2 == 1 else nc.scalar.copy
-                copy(out=staged[:, n, :], in_=accs[n][:, 0:CHUNK])
-                nc.sync.dma_start(out=out[P * n : P * (n + 1), CHUNK * c : CHUNK * (c + 1)], in_=staged[:, n, :])
+                    nc.tensor.matmul_mx(
+                        out=accs[n // 2][:, P * (n % 2) : P * (n % 2 + 1)],
+                        lhsT=w3_codes[b][:, P * n : P * (n + 1)].bitcast(FP8X4),
+                        lhsT_scale=w3_sc[b][:, P * n : P * (n + 1)],
+                        rhs=z_codes[b, col].bitcast(FP8X4),
+                        rhs_scale=z_sc[b, col],
+                        start=(b == 0 and n % 2 == 0),
+                        stop=(b == 1 and n % 2 == 1),
+                    )
+            for u in range(2):
+                part = staged[:, 2 * P * u : 2 * P * (u + 1)]
+                copies[u](out=part, in_=accs[u][:, 0 : 2 * P])
+                nc.sync.dma_start(
+                    out=out[2 * P * u : 2 * P * (u + 1), col : col + P].rearrange("(j p) m -> p j m", p=P),
+                    in_=part.rearrange("p (j m) -> p j m", j=2),
+                )
 
         def far_rows(c, t, dst):
             gather(dst, pages[0, t], CHUNK * c, CHUNK * (c + 1))
@@ -565,14 +578,25 @@ def tile_list_playlist_slot_refresh_kernel(
         z_tile(1, 2, "gate11")
         gated(nc.vector, 1, 2, 2)
         quant_z_part(0, 2, "v0")
-        z_tile(0, 3, "B0")
-        gated(nc.vector, 0, 3, 2)
+        piece = PACK * P
+        first = tile([P, 2 * piece], BF16, "B0", "zb3a")
+        product(nc.vector, first[:, 0:piece], 0, 3, 0, P, 2)
         quant_z_part(1, 2, "v0", 1024)
-        z_tile(1, 3, "B0", 2048)
-        gated(nc.vector, 1, 3, 2)
-        quant_z_part(0, 3, "v1")
-        quant_z_part(1, 3, "z31")
+        product(nc.vector, first[:, piece:], 1, 3, 0, P, 2)
+        second = [tile([P, piece], BF16, "B0", "zb3b%d" % b, 2048 + 1024 * b) for b in range(2)]
+        product(nc.vector, second[0][:], 0, 3, P, CHUNK, 2)
+        codes, scales = quantise("za", "v1", first[:])
+        for b in range(2):
+            z_codes[b, M - CHUNK] = codes[:, P * b : P * (b + 1)]
+            z_sc[b, M - CHUNK] = scales[:, P * b : P * (b + 1)]
+        product(nc.vector, second[1][:], 1, 3, P, CHUNK, 2)
+        for b in range(2):
+            codes, scales = quantise("zb%d" % b, "zb", second[b][:], 512 * b)
+            z_codes[b, M - P] = codes[:]
+            z_sc[b, M - P] = scales[:]
         scores(0, 2, nc.scalar.copy, tile([P, PACK * CHUNK], F32, "P13", "staged0")[:])
         scores(1, 0, nc.scalar.copy, tile([P, PACK * CHUNK], F32, "P11", "staged1")[:])
         scores(2, 4, nc.scalar.copy, tile([P, PACK * CHUNK], F32, "P12", "staged2")[:])
-        last_scores(3, (6, 7, 2, 3), "P10")
+        staged = tile([P, PACK * CHUNK], F32, "P10", "staged3")
+        piece_scores(M - CHUNK, (6, 7), (nc.scalar.copy, nc.scalar.copy), staged[:, 0:BANK])
+        piece_scores(M - P, (2, 3), (nc.scalar.copy, nc.vector.tensor_copy), staged[:, BANK:])

@@ -213,8 +213,8 @@ def tile_list_playlist_slot_refresh_kernel(
         def gather(dst, page, lo, hi):
             nc.vector.tensor_copy(dst, page[:].indirect(idx3[:, lo // 16 : hi // 16]))
 
-        def fetch_rows(t, slot):
-            rows = tile([P, BANK], F32, slot, "x_rows%d" % t)
+        def fetch_rows(t, slot, at=0):
+            rows = tile([P, BANK], F32, slot, "x_rows%d" % t, at)
             gather(rows[:], pages[0, t], 0, BANK)
             x_rows[t] = rows
 
@@ -275,8 +275,8 @@ def tile_list_playlist_slot_refresh_kernel(
                     in_=w2_scales[:, 4 * q : 4 * q + 4, :].bitcast(I32),
                 )
 
-        def order_w2_words(a, b, slot):
-            codes = tile([P, 2 * PASS], U8, slot, "w2_codes%d%d" % (a, b))
+        def order_w2_words(a, b, slot, at=0):
+            codes = tile([P, 2 * PASS], U8, slot, "w2_codes%d%d" % (a, b), at)
             nc.gpsimd.tensor_copy(
                 out=codes[:].bitcast(U16).rearrange("p (t m) -> p t m", t=PACK),
                 in_=w2_raw[:, a, 2 * PASS * b : 2 * PASS * (b + 1)].bitcast(U16).rearrange("p (m t) -> p t m", t=PACK),
@@ -362,20 +362,16 @@ def tile_list_playlist_slot_refresh_kernel(
         load_page(0, 3)
         put(0, 3, 0, S)
         order_w2_words(1, 0, "h0")
-        stage_w3(0, 0, HALF, "R0")
-        prep_w3(0, 0, HALF, "sb0")
+        order_w2_words(1, 1, "h0", 1024)
         stage_w3(0, HALF, N, "R1")
         prep_w3(0, HALF, N, "sb1")
         fetch_rows(2, "R1")
+        fetch_rows(3, "R1", 2048)
         features(1, 0, "R0")
         features(1, 1, "h3")
         load_gains(0)
         load_page(1, 0)
         put(1, 0, 0, S)
-        order_w2_words(1, 1, "R0")
-        stage_w3(1, HALF, N, "B1")
-        prep_w3(1, HALF, N, "sb0")
-        fetch_rows(3, "B1")
         load_gains(1)
         load_page(1, 1)
         load_w2_scales()
@@ -388,6 +384,8 @@ def tile_list_playlist_slot_refresh_kernel(
         load_w3(1, 0, HALF, x_near[:, HALF : HALF + 2 * BANK])
         load_gains(3)
         load_page(1, 3)
+        stage_w3(0, 0, HALF, "gate11")
+        stage_w3(1, HALF, N, "B1")
         put(1, 1, 0, S)
         features(1, 2, "R3")
         put(1, 2, 0, S)
@@ -521,6 +519,8 @@ def tile_list_playlist_slot_refresh_kernel(
             for b in range(2):
                 open_gate(b, c, 4 * c + 2 * b)
         put(1, 3, 0, S)
+        prep_w3(0, 0, HALF, "sb0")
+        prep_w3(1, HALF, N, "wb1")
         for c in range(2):
             gather(x_f32[1, c][:, PACK - 1, :], pages[1, PACK - 1], CHUNK * c, CHUNK * (c + 1))
         rows = tile([P, 2, CHUNK], F32, "G1", "rows_a")

@@ -549,8 +549,10 @@ def tile_list_playlist_slot_refresh_kernel(
         zb0 = tile([P, 2 * PACK * CHUNK], BF16, "wb0", "zb0")
         for b in range(2):
             zbs[b, 0] = zb0[:, PACK * CHUNK * b : PACK * CHUNK * (b + 1)]
-        gated(nc.gpsimd, 0, 0, 4)
-        gated(nc.gpsimd, 1, 0, 4)
+        gated(nc.gpsimd, 0, 0, 1)
+        gated(nc.gpsimd, 1, 0, 1)
+        z_tile(0, 1, "h3")
+        gated(nc.gpsimd, 0, 1, 1)
         late = {}
         for c in (2, 3):
             late[c] = tile([P, 2 * PACK * CHUNK], BF16, "B1", "xb%d" % c, 4096 * (c - 2))
@@ -558,12 +560,10 @@ def tile_list_playlist_slot_refresh_kernel(
                 weave(late[c][:, PACK * CHUNK * b : PACK * CHUNK * (b + 1)], x_f32[b, c])
         quant_x([(0, 2), (1, 2)], late[2][:], "G0")
         quant_z(0, "G0", zb0[:], 2048)
-        z_tile(0, 1, "B1")
-        gated(nc.vector, 0, 1, 2)
-        quant_x([(0, 3), (1, 3)], late[3][:], "wb0")
-        z_tile(1, 1, "R1")
+        z_tile(1, 1, "B1")
         gated(nc.vector, 1, 1, 2)
-        quant_z_part(0, 1, "wc11")
+        quant_z_part(0, 1, "B1", 2048)
+        quant_x([(0, 3), (1, 3)], late[3][:], "gate11", 2048)
         open_gate(0, 2, 0)
         close_gate(0, 2, gate_tile("P03", "gate02"))
         open_gate(1, 2, 2)

@@ -549,10 +549,10 @@ def tile_list_playlist_slot_refresh_kernel(
         zb0 = tile([P, 2 * PACK * CHUNK], BF16, "wb0", "zb0")
         for b in range(2):
             zbs[b, 0] = zb0[:, PACK * CHUNK * b : PACK * CHUNK * (b + 1)]
-        gated(nc.gpsimd, 0, 0, 1)
-        gated(nc.gpsimd, 1, 0, 1)
+        gated(nc.gpsimd, 0, 0, 8)
+        gated(nc.gpsimd, 1, 0, 8)
         z_tile(0, 1, "h3")
-        gated(nc.gpsimd, 0, 1, 1)
+        gated(nc.gpsimd, 0, 1, 8)
         late = {}
         for c in (2, 3):
             late[c] = tile([P, 2 * PACK * CHUNK], BF16, "B1", "xb%d" % c, 4096 * (c - 2))

@@ -37,12 +37,11 @@ AREA_SIZES = (
     ("h3", 4096), ("h0", 4096), ("h1", 4096), ("h2", 4096),
     ("wc00", 1024), ("wc01", 1024), ("wc02", 1024), ("wc03", 1024), ("wc10", 2048), ("wc11", 2048),
     ("ws00", 256), ("ws01", 256), ("ws02", 256), ("ws03", 256), ("ws10", 512), ("ws11", 512),
-    ("w3c0", 2048), ("w3c1", 2048), ("w3s0", 512), ("w3s1", 512),
-    ("gate11", 4096), ("x11", 1024),
-    ("x00", 2048), ("x10", 1024),
-    ("x00s", 512), ("x10s", 256), ("x11s", 256), ("x02s", 512), ("x03s", 512),
-    ("z0s", 512), ("z10s", 256), ("z11s", 256), ("z20s", 256), ("z21s", 256), ("zas", 256), ("zb0s", 128), ("zb1s", 128), ("zb", 1024),
-    ("warm", 64), ("b1f", 64), ("b1r", 64), ("b1p", 64), ("b2", 64),
+    ("w3c", 4096), ("w3s", 1024), ("W3B", 11264), ("b1p", 1024),
+    ("x00", 1024), ("x10", 1024), ("x11", 1024),
+    ("x00s", 256), ("x01s", 256), ("x10s", 256), ("x11s", 256), ("x02s", 256), ("x12s", 256), ("x03s", 512),
+    ("z0s", 512), ("z10s", 256), ("z11s", 256), ("z20s", 256), ("z21s", 256), ("zas", 256), ("zb0s", 128), ("zb1s", 128),
+    ("warm", 64), ("b1f", 64), ("b1r", 64), ("b2", 64),
 )
 
 
@@ -241,9 +240,7 @@ def tile_list_playlist_slot_refresh_kernel(
                 x_codes[key] = codes[:, CHUNK * j : CHUNK * (j + 1)]
                 x_sc[key] = scales[:, CHUNK * j : CHUNK * (j + 1)]
 
-        w3_codes = [tile([P, N], U32, "w3c%d" % b, "w3_codes%d" % b) for b in range(2)]
-        w3_sc = [tile([P, N], U8, "w3s%d" % b, "w3_sc%d" % b) for b in range(2)]
-
+        w3_woven = tile([P, 2 * N * PACK], BF16, "W3B", "w3_woven")
         w3_raw = {}
 
         def load_w3(b, lo, hi, raw):
@@ -252,14 +249,12 @@ def tile_list_playlist_slot_refresh_kernel(
             nc.sync.dma_start(out=part, in_=rows.rearrange("(p j) n -> p j n", j=PACK))
             w3_raw[b, lo] = part
 
-        def stage_w3(b, lo, hi, slot):
-            raw = tile([P, PACK * (hi - lo)], F32, slot, "w3_raw%d%d" % (b, lo))
+        def stage_w3(b, lo, hi, slot, at=0):
+            raw = tile([P, PACK * (hi - lo)], F32, slot, "w3_raw%d%d" % (b, lo), at)
             load_w3(b, lo, hi, raw[:])
 
-        def prep_w3(b, lo, hi, slot):
-            grouped = tile([P, (hi - lo) * PACK], BF16, slot, "w3_b%d%d" % (b, lo))
-            weave(grouped[:], w3_raw[b, lo])
-            nc.vector.quantize_mx(out=w3_codes[b][:, lo:hi].bitcast(FP8X4), scales=w3_sc[b][:, lo:hi], in_=grouped[:])
+        def weave_w3(b, lo, hi):
+            weave(w3_woven[:, PACK * (N * b + lo) : PACK * (N * b + hi)], w3_raw[b, lo])
 
         w2_raw = tile([P, 2, 2 * H], U8, "w2_raw", "w2_raw")
         w2_codes = {}
@@ -275,9 +270,9 @@ def tile_list_playlist_slot_refresh_kernel(
                     in_=w2_scales[:, 4 * q : 4 * q + 4, :].bitcast(I32),
                 )
 
-        def order_w2_words(a, b, slot, at=0):
-            codes = tile([P, 2 * PASS], U8, slot, "w2_codes%d%d" % (a, b), at)
-            nc.gpsimd.tensor_copy(
+        def order_w2_words(a, b, slot, copy):
+            codes = tile([P, 2 * PASS], U8, slot, "w2_codes%d%d" % (a, b))
+            copy(
                 out=codes[:].bitcast(U16).rearrange("p (t m) -> p t m", t=PACK),
                 in_=w2_raw[:, a, 2 * PASS * b : 2 * PASS * (b + 1)].bitcast(U16).rearrange("p (m t) -> p t m", t=PACK),
             )
@@ -350,21 +345,20 @@ def tile_list_playlist_slot_refresh_kernel(
         fetch_rows(0, "R3")
         features(0, 3, "h0")
         load_w2()
-        order_w2_words(0, 0, "h1")
+        order_w2_words(0, 0, "h1", nc.gpsimd.tensor_copy)
         load_page(0, 2)
         nc.sync.dma_start(out=b1_planes[:], in_=b1[PASS : 2 * PASS].rearrange("(p i) -> p i", i=PACK))
         nc.sync.dma_start(out=b2_sb[:], in_=b2.rearrange("(a p i) -> p a i", a=2, i=PACK))
         put(0, 2, 0, S)
-        order_w2_words(0, 1, "h2")
+        order_w2_words(0, 1, "h2", nc.gpsimd.tensor_copy)
         prep_w1_planes(0)
         fetch_rows(1, "B0")
         prep_w1_planes(1)
         load_page(0, 3)
         put(0, 3, 0, S)
-        order_w2_words(1, 0, "h0")
-        order_w2_words(1, 1, "h0", 1024)
+        order_w2_words(1, 0, "h0", nc.gpsimd.tensor_copy)
         stage_w3(0, HALF, N, "R1")
-        prep_w3(0, HALF, N, "sb1")
+        weave_w3(0, HALF, N)
         fetch_rows(2, "R1")
         fetch_rows(3, "R1", 2048)
         features(1, 0, "R0")
@@ -382,22 +376,25 @@ def tile_list_playlist_slot_refresh_kernel(
         deal(dealt_near, 2, x_rows[2][:])
         deal(dealt_near, 3, x_rows[3][:])
         load_w3(1, 0, HALF, x_near[:, HALF : HALF + 2 * BANK])
+        stage_w3(0, 0, HALF, "G0", 8192)
         load_gains(3)
         load_page(1, 3)
-        stage_w3(0, 0, HALF, "gate11")
         stage_w3(1, HALF, N, "B1")
         put(1, 1, 0, S)
         features(1, 2, "R3")
         put(1, 2, 0, S)
         order_w2_scales("R3")
-        prep_w3(1, 0, HALF, "sb1")
-        features(1, 3, "B0")
+        weave_w3(1, 0, HALF)
+        weave_w3(0, 0, HALF)
         fetch(0)
         fetch(1)
         fetch(2)
-        xb = tile([P, BANK * PACK], BF16, "wb0", "xb_near")
-        weave(xb[:], as_planes(dealt_near))
-        quant_x([(0, 0), (0, 1)], xb[:], "x00")
+        xb_near = tile([P, BANK * PACK], BF16, "wb0", "xb_near")
+        weave(xb_near[:], as_planes(dealt_near))
+        quant_x([(0, 0)], xb_near[:, 0 : PACK * CHUNK], "x00")
+        weave_w3(1, HALF, N)
+        features(1, 3, "B1")
+        order_w2_words(1, 1, "b1p", nc.scalar.copy)
 
         gate_banks = {}
         gates = {}
@@ -464,22 +461,22 @@ def tile_list_playlist_slot_refresh_kernel(
         def score_pass(acc, n, b, c):
             nc.tensor.matmul_mx(
                 out=acc,
-                lhsT=w3_codes[b][:, P * n : P * (n + 1)].bitcast(FP8X4),
-                lhsT_scale=w3_sc[b][:, P * n : P * (n + 1)],
+                lhsT=w3_codes[:, N * b + P * n : N * b + P * (n + 1)].bitcast(FP8X4),
+                lhsT_scale=w3_sc[:, N * b + P * n : N * b + P * (n + 1)],
                 rhs=z_codes[b, c].bitcast(FP8X4),
                 rhs_scale=z_sc[b, c],
                 start=(b == 0),
                 stop=(b == 1),
             )
 
-        def scores(c, first, copy, staged):
+        def scores(c, first, copies, staged):
             for u in range(2):
                 acc = bank(first + u, "acc_o%d%d" % (c, u))
                 for j in range(2):
                     for b in range(2):
                         score_pass(acc[:, CHUNK * j : CHUNK * (j + 1)], 2 * u + j, b, c)
                 part = staged[:, BANK * u : BANK * (u + 1)]
-                copy(out=part, in_=acc[:])
+                copies[u](out=part, in_=acc[:])
                 nc.sync.dma_start(
                     out=out[2 * P * u : 2 * P * (u + 1), CHUNK * c : CHUNK * (c + 1)].rearrange("(j p) m -> p j m", p=P),
                     in_=part.rearrange("p (j m) -> p j m", j=2),
@@ -491,8 +488,8 @@ def tile_list_playlist_slot_refresh_kernel(
                 for n in range(N // P):
                     nc.tensor.matmul_mx(
                         out=accs[n // 2][:, P * (n % 2) : P * (n % 2 + 1)],
-                        lhsT=w3_codes[b][:, P * n : P * (n + 1)].bitcast(FP8X4),
-                        lhsT_scale=w3_sc[b][:, P * n : P * (n + 1)],
+                        lhsT=w3_codes[:, N * b + P * n : N * b + P * (n + 1)].bitcast(FP8X4),
+                        lhsT_scale=w3_sc[:, N * b + P * n : N * b + P * (n + 1)],
                         rhs=z_codes[b, col].bitcast(FP8X4),
                         rhs_scale=z_sc[b, col],
                         start=(b == 0 and n % 2 == 0),
@@ -515,88 +512,86 @@ def tile_list_playlist_slot_refresh_kernel(
             for i in range(PACK):
                 gather(x_f32[1, c][:, i, :], pages[1, i], CHUNK * c, CHUNK * (c + 1))
 
-        for c in range(2):
-            for b in range(2):
-                open_gate(b, c, 4 * c + 2 * b)
+        for b in range(2):
+            open_gate(b, 0, 2 * b)
         put(1, 3, 0, S)
-        prep_w3(0, 0, HALF, "sb0")
-        prep_w3(1, HALF, N, "wb1")
+        quant_x([(0, 1)], xb_near[:, PACK * CHUNK :], "w2_raw")
+        for b in range(2):
+            open_gate(b, 1, 4 + 2 * b)
         for c in range(2):
             gather(x_f32[1, c][:, PACK - 1, :], pages[1, PACK - 1], CHUNK * c, CHUNK * (c + 1))
-        rows = tile([P, 2, CHUNK], F32, "G1", "rows_a")
-        for t in range(2):
-            far_rows(2, t, rows[:, t, :])
-        xb = tile([P, PACK * CHUNK], BF16, "B0", "xb10", 6144)
+        far_rows(2, 0, tile([P, CHUNK], F32, "G1", "rows_first")[:])
+        xb = tile([P, PACK * CHUNK], BF16, "w3c", "xb10")
         weave(xb[:], x_f32[1, 0])
         quant_x([(1, 0)], xb[:], "x10")
-        rows = tile([P, 2, CHUNK], F32, "B1", "rows_b", -256)
-        for t in range(2):
-            far_rows(2, 2 + t, rows[:, t, :])
-        xb = tile([P, PACK * CHUNK], BF16, "G0", "xb11", 3584)
+        w3_codes = tile([P, 2 * N], U32, "w3c", "w3_codes")
+        w3_sc = tile([P, 2 * N], U8, "w3s", "w3_sc")
+        nc.vector.quantize_mx(out=w3_codes[:].bitcast(FP8X4), scales=w3_sc[:], in_=w3_woven[:])
+        xb = tile([P, PACK * CHUNK], BF16, "sb0", "xb11")
         weave(xb[:], x_f32[1, 1])
         quant_x([(1, 1)], xb[:], "x11")
-        rows = tile([P, PACK, CHUNK], F32, "G0", "rows_c", -256)
-        for t in range(PACK):
-            far_rows(3, t, rows[:, t, :])
-        far = tile([P, 2 * PACK * CHUNK], F32, "G0", "far", 4096)
-        for c in (2, 3):
-            far_planes(c, far[:, PACK * CHUNK * (c - 2) : PACK * CHUNK * (c - 1)])
-        first_gate = tile([P, PACK * CHUNK + 128], F32, "B1", "gate00", 2048 - 256)
-        close_gate(0, 0, as_planes(first_gate[:, 0 : PACK * CHUNK]))
-        close_gate(1, 0, gate_tile("wb1", "gate10"))
+        rows = tile([P, 2 * PACK - 1, CHUNK], F32, "W3B", "rows_late")
+        for k in range(1, 2 * PACK):
+            far_rows(2 + k // PACK, k % PACK, rows[:, k - 1, :])
+        far_planes(2, tile([P, PACK * CHUNK], F32, "W3B", "x12", 7168)[:])
+        close_gate(0, 0, gate_tile("GR", "gate00"))
+        close_gate(1, 0, gate_tile("R0", "gate10"))
         close_gate(0, 1, gate_tile("R1", "gate01"))
-        close_gate(1, 1, gate_tile("gate11", "gate11"))
-        zb0 = tile([P, 2 * PACK * CHUNK], BF16, "wb0", "zb0")
+        close_gate(1, 1, gate_tile("B0", "gate11"))
+        zb0 = tile([P, 2 * PACK * CHUNK], BF16, "G0", "zb0", 3072)
         for b in range(2):
             zbs[b, 0] = zb0[:, PACK * CHUNK * b : PACK * CHUNK * (b + 1)]
-        gated(nc.gpsimd, 0, 0, 8)
-        gated(nc.gpsimd, 1, 0, 8)
-        z_tile(0, 1, "h3")
+            gated(nc.gpsimd, b, 0, 8)
+        xb02 = tile([P, PACK * CHUNK], BF16, "G0", "xb02", 7168)
+        weave(xb02[:], x_f32[0, 2])
+        xb3 = tile([P, 2 * PACK * CHUNK], BF16, "B0", "xb3", 4096)
+        weave(xb3[:, 0 : PACK * CHUNK], x_f32[0, 3])
+        xb12 = tile([P, PACK * CHUNK], BF16, "W3B", "xb12")
+        weave(xb12[:], x_f32[1, 2])
+        quant_z(0, "W3B", zb0[:], 2048)
+        quant_x([(0, 2)], xb02[:], "W3B", 4096)
+        z_tile(0, 1, "G0", 6144)
         gated(nc.gpsimd, 0, 1, 8)
-        late = {}
-        for c in (2, 3):
-            late[c] = tile([P, 2 * PACK * CHUNK], BF16, "B1", "xb%d" % c, 4096 * (c - 2))
-            for b in range(2):
-                weave(late[c][:, PACK * CHUNK * b : PACK * CHUNK * (b + 1)], x_f32[b, c])
-        quant_x([(0, 2), (1, 2)], late[2][:], "G0")
-        quant_z(0, "G0", zb0[:], 2048)
-        z_tile(1, 1, "B1")
+        far_planes(3, tile([P, PACK * CHUNK], F32, "G0", "x13")[:])
+        scores(0, 4, (nc.scalar.copy, nc.vector.tensor_copy), tile([P, PACK * CHUNK], F32, "P00", "staged0")[:])
+        for b in range(2):
+            open_gate(b, 2, 2 * b)
+        weave(xb3[:, PACK * CHUNK :], x_f32[1, 3])
+        quant_x([(1, 2)], xb12[:], "R1", 64)
+        z_tile(1, 1, "R1", 1088)
         gated(nc.vector, 1, 1, 2)
-        quant_z_part(0, 1, "B1", 2048)
-        quant_x([(0, 3), (1, 3)], late[3][:], "gate11", 2048)
-        open_gate(0, 2, 0)
-        close_gate(0, 2, gate_tile("P03", "gate02"))
-        open_gate(1, 2, 2)
-        close_gate(1, 2, gate_tile("P00", "gate12"))
-        open_gate(0, 3, 4)
-        close_gate(0, 3, gate_tile("P01", "gate03"))
-        open_gate(1, 3, 6)
-        close_gate(1, 3, gate_tile("P02", "gate13"))
-        z_tile(0, 2, "R1", 2048)
+        quant_z_part(0, 1, "R1", -960)
+        quant_x([(0, 3), (1, 3)], xb3[:], "R1", 3136)
+        close_gate(0, 2, gate_tile("P02", "gate02"))
+        close_gate(1, 2, gate_tile("P02", "gate12", 4096))
+        open_gate(0, 3, 6)
+        close_gate(0, 3, gate_tile("P03", "gate03"))
+        open_gate(1, 3, 4)
+        close_gate(1, 3, gate_tile("P03", "gate13", 4096))
+        z_tile(0, 2, "B0")
         gated(nc.vector, 0, 2, 2)
-        quant_z_part(1, 1, "wc11", 1024)
-        z_tile(1, 2, "gate11")
+        quant_z_part(1, 1, "v0", 3072)
+        z_tile(1, 2, "B0", 2048)
         gated(nc.vector, 1, 2, 2)
-        quant_z_part(0, 2, "v0")
+        quant_z_part(0, 2, "v1")
         piece = PACK * P
-        first = tile([P, 2 * piece], BF16, "B0", "zb3a")
+        first = tile([P, 2 * piece], BF16, "wb1", "zb3a")
         product(nc.vector, first[:, 0:piece], 0, 3, 0, P, 2)
-        quant_z_part(1, 2, "v0", 1024)
+        quant_z_part(1, 2, "v1", 1024)
         product(nc.vector, first[:, piece:], 1, 3, 0, P, 2)
-        second = [tile([P, piece], BF16, "B0", "zb3b%d" % b, 2048 + 1024 * b) for b in range(2)]
+        second = [tile([P, piece], BF16, "wb1", "zb3b%d" % b, 2048 + 1024 * b) for b in range(2)]
         product(nc.vector, second[0][:], 0, 3, P, CHUNK, 2)
-        codes, scales = quantise("za", "v1", first[:])
+        codes, scales = quantise("za", "v1", first[:], 2048)
         for b in range(2):
             z_codes[b, M - CHUNK] = codes[:, P * b : P * (b + 1)]
             z_sc[b, M - CHUNK] = scales[:, P * b : P * (b + 1)]
         product(nc.vector, second[1][:], 1, 3, P, CHUNK, 2)
         for b in range(2):
-            codes, scales = quantise("zb%d" % b, "zb", second[b][:], 512 * b)
+            codes, scales = quantise("zb%d" % b, "v1", second[b][:], 3072 + 512 * b)
             z_codes[b, M - P] = codes[:]
             z_sc[b, M - P] = scales[:]
-        scores(0, 2, nc.scalar.copy, tile([P, PACK * CHUNK], F32, "P13", "staged0")[:])
-        scores(1, 0, nc.scalar.copy, tile([P, PACK * CHUNK], F32, "P11", "staged1")[:])
-        scores(2, 4, nc.scalar.copy, tile([P, PACK * CHUNK], F32, "P12", "staged2")[:])
-        staged = tile([P, PACK * CHUNK], F32, "P10", "staged3")
+        scores(1, 0, (nc.scalar.copy, nc.scalar.copy), tile([P, PACK * CHUNK], F32, "P00", "staged1", 4096)[:])
+        scores(2, 2, (nc.scalar.copy, nc.scalar.copy), tile([P, PACK * CHUNK], F32, "P01", "staged2")[:])
+        staged = tile([P, PACK * CHUNK], F32, "P01", "staged3", 4096)
         piece_scores(M - CHUNK, (6, 7), (nc.scalar.copy, nc.scalar.copy), staged[:, 0:BANK])
-        piece_scores(M - P, (2, 3), (nc.scalar.copy, nc.vector.tensor_copy), staged[:, BANK:])
+        piece_scores(M - P, (4, 5), (nc.scalar.copy, nc.vector.tensor_copy), staged[:, BANK:])

@@ -37,9 +37,9 @@ AREA_SIZES = (
     ("h3", 4096), ("h0", 4096), ("h1", 4096), ("h2", 4096),
     ("wc00", 1024), ("wc01", 1024), ("wc02", 1024), ("wc03", 1024), ("wc10", 2048), ("wc11", 2048),
     ("ws00", 256), ("ws01", 256), ("ws02", 256), ("ws03", 256), ("ws10", 512), ("ws11", 512),
-    ("w3c", 4096), ("w3s", 1024), ("W3B", 11264), ("b1p", 1024),
+    ("w3c", 4096), ("w3s", 1024), ("S0", 5184), ("W3B", 12224), ("b1p", 1024),
     ("x00", 1024), ("x10", 1024), ("x11", 1024),
-    ("x00s", 256), ("x01s", 256), ("x10s", 256), ("x11s", 256), ("x02s", 256), ("x12s", 256), ("x03s", 512),
+    ("x00s", 256), ("x01s", 256), ("x10s", 256), ("x11s", 256), ("x02s", 256), ("x12s", 256), ("x03s", 256), ("x13s", 256),
     ("z0s", 512), ("z10s", 256), ("z11s", 256), ("z20s", 256), ("z21s", 256), ("zas", 256), ("zb0s", 128), ("zb1s", 128),
     ("warm", 64), ("b1f", 64), ("b1r", 64), ("b2", 64),
 )
@@ -147,21 +147,25 @@ def tile_list_playlist_slot_refresh_kernel(
                 out=codes[:].bitcast(FP8X4), scales=scales[:], in_=grouped[:].rearrange("p a k -> p (a k)")
             )
 
-        def prep_w1_planes(a):
+        def prep_w1_planes(a, grouped):
             raw = tile([P, PACK, PASS], F32, "B%d" % a, "w1_raw1%d" % a)
             rows = w1[PASS * a : PASS * (a + 1), PASS : 2 * PASS]
             nc.sync.dma_start(out=raw[:], in_=rows.rearrange("(p j) c -> p j c", j=PACK))
-            grouped = tile([P, PASS * PACK], BF16, "wb%d" % a, "w1_b1%d" % a)
-            codes = tile([P, PASS], U32, "wc1%d" % a, "w1_codes1%d" % a)
-            scales = tile([P, PASS], U8, "ws1%d" % a, "w1_sc1%d" % a)
             nc.scalar.copy(
-                out=grouped[:].rearrange("p (t m j) -> p m j t", t=PACK, j=PACK),
+                out=grouped[:, a, :].rearrange("p (t m j) -> p m j t", t=PACK, j=PACK),
                 in_=raw[:].rearrange("p j (m t) -> p m j t", t=PACK),
             )
-            nc.vector.quantize_mx(out=codes[:].bitcast(FP8X4), scales=scales[:], in_=grouped[:])
-            for i in range(PACK):
-                w1_codes[a, 1, i] = codes[:, P * i : P * (i + 1)]
-                w1_sc[a, 1, i] = scales[:, P * i : P * (i + 1)]
+
+        def quant_w1_planes(grouped):
+            codes = tile([P, 2 * PASS], U32, "wc10", "w1_codes1")
+            scales = tile([P, 2 * PASS], U8, "ws10", "w1_sc1")
+            nc.vector.quantize_mx(
+                out=codes[:].bitcast(FP8X4), scales=scales[:], in_=grouped[:].rearrange("p a k -> p (a k)")
+            )
+            for a in range(2):
+                for i in range(PACK):
+                    w1_codes[a, 1, i] = codes[:, PASS * a + P * i : PASS * a + P * (i + 1)]
+                    w1_sc[a, 1, i] = scales[:, PASS * a + P * i : PASS * a + P * (i + 1)]
 
         pages = {}
 
@@ -298,8 +302,9 @@ def tile_list_playlist_slot_refresh_kernel(
             nc.sync.dma_start(out=tab_sc[a:QUAD:2, :].bitcast(I32), in_=tab_scales[a].bitcast(I32))
         load_tab(0, 0, T)
         nc.sync.dma_start(out=b1_first[:], in_=b1[0:P].rearrange("(p t) -> p t", t=1))
-        warm = tile([P, 1], F32, "warm", "warm")
-        nc.scalar.activation(out=warm[:], in_=b1_first[:], func=ACT.Sigmoid)
+        warm = tile([P, 2], F32, "warm", "warm")
+        nc.gpsimd.memset(warm[:, 0:1], 0.0)
+        nc.scalar.activation(out=warm[:, 1:2], in_=warm[:, 0:1], func=ACT.Sigmoid)
         nc.sync.dma_start(idx2[:], offs2)
         nc.vector.tensor_copy(v_sc_packed[:], tab_sc[:].indirect(idx[:]))
         nc.vector.tensor_copy(v_codes[0][:], tab_window(0).indirect(idx[:]))
@@ -351,9 +356,11 @@ def tile_list_playlist_slot_refresh_kernel(
         nc.sync.dma_start(out=b2_sb[:], in_=b2.rearrange("(a p i) -> p a i", a=2, i=PACK))
         put(0, 2, 0, S)
         order_w2_words(0, 1, "h2", nc.gpsimd.tensor_copy)
-        prep_w1_planes(0)
+        w1_planes = tile([P, 2, PASS * PACK], BF16, "wb0", "w1_b1")
+        prep_w1_planes(0, w1_planes)
         fetch_rows(1, "B0")
-        prep_w1_planes(1)
+        prep_w1_planes(1, w1_planes)
+        quant_w1_planes(w1_planes)
         load_page(0, 3)
         put(0, 3, 0, S)
         order_w2_words(1, 0, "h0", nc.gpsimd.tensor_copy)
@@ -530,10 +537,11 @@ def tile_list_playlist_slot_refresh_kernel(
         xb = tile([P, PACK * CHUNK], BF16, "sb0", "xb11")
         weave(xb[:], x_f32[1, 1])
         quant_x([(1, 1)], xb[:], "x11")
-        rows = tile([P, 2 * PACK - 1, CHUNK], F32, "W3B", "rows_late")
-        for k in range(1, 2 * PACK):
-            far_rows(2 + k // PACK, k % PACK, rows[:, k - 1, :])
-        far_planes(2, tile([P, PACK * CHUNK], F32, "W3B", "x12", 7168)[:])
+        for c, ts, at in ((2, (2, 1, 3), 3072), (3, (0, 2), 1024), (3, (1, 3), -1984)):
+            rows = tile([P, len(ts), CHUNK], F32, "W3B", "rows_late%d%d" % (c, ts[0]), at)
+            for k, t in enumerate(ts):
+                far_rows(c, t, rows[:, k, :])
+        far_planes(2, tile([P, PACK * CHUNK], F32, "W3B", "x12", 8128)[:])
         close_gate(0, 0, gate_tile("GR", "gate00"))
         close_gate(1, 0, gate_tile("R0", "gate10"))
         close_gate(0, 1, gate_tile("R1", "gate01"))
@@ -544,34 +552,36 @@ def tile_list_playlist_slot_refresh_kernel(
             gated(nc.gpsimd, b, 0, 8)
         xb02 = tile([P, PACK * CHUNK], BF16, "G0", "xb02", 7168)
         weave(xb02[:], x_f32[0, 2])
-        xb3 = tile([P, 2 * PACK * CHUNK], BF16, "B0", "xb3", 4096)
-        weave(xb3[:, 0 : PACK * CHUNK], x_f32[0, 3])
-        xb12 = tile([P, PACK * CHUNK], BF16, "W3B", "xb12")
+        xb12 = tile([P, PACK * CHUNK], BF16, "W3B", "xb12", 4096)
         weave(xb12[:], x_f32[1, 2])
-        quant_z(0, "W3B", zb0[:], 2048)
-        quant_x([(0, 2)], xb02[:], "W3B", 4096)
-        z_tile(0, 1, "G0", 6144)
+        xb03 = tile([P, PACK * CHUNK], BF16, "sb1", "xb03")
+        weave(xb03[:], x_f32[0, 3])
+        quant_z(0, "W3B", zb0[:], 1984)
+        quant_x([(0, 2)], xb02[:], "W3B", 960)
+        z_tile(0, 1, "G0", 4096)
         gated(nc.gpsimd, 0, 1, 8)
         far_planes(3, tile([P, PACK * CHUNK], F32, "G0", "x13")[:])
-        scores(0, 4, (nc.scalar.copy, nc.vector.tensor_copy), tile([P, PACK * CHUNK], F32, "P00", "staged0")[:])
+        scores(0, 4, (nc.scalar.copy, nc.scalar.copy), tile([P, PACK * CHUNK], F32, "S0", "staged0")[:])
         for b in range(2):
             open_gate(b, 2, 2 * b)
-        weave(xb3[:, PACK * CHUNK :], x_f32[1, 3])
+        xb13 = tile([P, PACK * CHUNK], BF16, "W3B", "xb13", -1088)
+        weave(xb13[:], x_f32[1, 3])
         quant_x([(1, 2)], xb12[:], "R1", 64)
         z_tile(1, 1, "R1", 1088)
         gated(nc.vector, 1, 1, 2)
+        quant_x([(0, 3)], xb03[:], "R1", 3136)
         quant_z_part(0, 1, "R1", -960)
-        quant_x([(0, 3), (1, 3)], xb3[:], "R1", 3136)
+        quant_x([(1, 3)], xb13[:], "B0", 4032)
         close_gate(0, 2, gate_tile("P02", "gate02"))
         close_gate(1, 2, gate_tile("P02", "gate12", 4096))
         open_gate(0, 3, 6)
         close_gate(0, 3, gate_tile("P03", "gate03"))
         open_gate(1, 3, 4)
         close_gate(1, 3, gate_tile("P03", "gate13", 4096))
-        z_tile(0, 2, "B0")
+        z_tile(0, 2, "B0", -64)
         gated(nc.vector, 0, 2, 2)
         quant_z_part(1, 1, "v0", 3072)
-        z_tile(1, 2, "B0", 2048)
+        z_tile(1, 2, "B0", 1984)
         gated(nc.vector, 1, 2, 2)
         quant_z_part(0, 2, "v1")
         piece = PACK * P

@@ -37,7 +37,7 @@ AREA_SIZES = (
     ("h3", 4096), ("h0", 4096), ("h1", 4096), ("h2", 4096),
     ("wc00", 1024), ("wc01", 1024), ("wc02", 1024), ("wc03", 1024), ("wc10", 2048), ("wc11", 2048),
     ("ws00", 256), ("ws01", 256), ("ws02", 256), ("ws03", 256), ("ws10", 512), ("ws11", 512),
-    ("w3c", 4096), ("w3s", 1024), ("S0", 5184), ("W3B", 12224), ("b1p", 1024),
+    ("w3c", 4096), ("w3s", 1024), ("S0", 4352), ("W3B", 12224), ("b1p", 1024),
     ("x00", 1024), ("x10", 1024), ("x11", 1024),
     ("x00s", 256), ("x01s", 256), ("x10s", 256), ("x11s", 256), ("x02s", 256), ("x12s", 256), ("x03s", 256), ("x13s", 256),
     ("z0s", 512), ("z10s", 256), ("z11s", 256), ("z20s", 256), ("z21s", 256), ("zas", 256), ("zb0s", 128), ("zb1s", 128),
@@ -510,9 +510,10 @@ def tile_list_playlist_slot_refresh_kernel(
                     in_=part.rearrange("p (j m) -> p j m", j=2),
                 )
 
-        def far_rows(c, t, dst):
-            gather(dst, pages[0, t], CHUNK * c, CHUNK * (c + 1))
-            deal(dealt_far[c], t, dst)
+        def far_rows(first, last, t, dst):
+            gather(dst, pages[0, t], CHUNK * first, CHUNK * (last + 1))
+            for c in range(first, last + 1):
+                deal(dealt_far[c], t, dst[:, CHUNK * (c - first) : CHUNK * (c - first + 1)])
 
         def far_planes(c, dst):
             x_f32[1, c] = as_planes(dst)
@@ -527,7 +528,7 @@ def tile_list_playlist_slot_refresh_kernel(
             open_gate(b, 1, 4 + 2 * b)
         for c in range(2):
             gather(x_f32[1, c][:, PACK - 1, :], pages[1, PACK - 1], CHUNK * c, CHUNK * (c + 1))
-        far_rows(2, 0, tile([P, CHUNK], F32, "G1", "rows_first")[:])
+        far_rows(2, 3, 0, tile([P, BANK], F32, "G1", "rows_first")[:])
         xb = tile([P, PACK * CHUNK], BF16, "w3c", "xb10")
         weave(xb[:], x_f32[1, 0])
         quant_x([(1, 0)], xb[:], "x10")
@@ -537,10 +538,12 @@ def tile_list_playlist_slot_refresh_kernel(
         xb = tile([P, PACK * CHUNK], BF16, "sb0", "xb11")
         weave(xb[:], x_f32[1, 1])
         quant_x([(1, 1)], xb[:], "x11")
-        for c, ts, at in ((2, (2, 1, 3), 3072), (3, (0, 2), 1024), (3, (1, 3), -1984)):
-            rows = tile([P, len(ts), CHUNK], F32, "W3B", "rows_late%d%d" % (c, ts[0]), at)
-            for k, t in enumerate(ts):
-                far_rows(c, t, rows[:, k, :])
+        rows = tile([P, PACK * CHUNK], F32, "W3B", "rows_a", 3328)
+        far_rows(2, 3, 2, rows[:, 0:BANK])
+        far_rows(2, 2, 1, rows[:, BANK : BANK + CHUNK])
+        far_rows(2, 2, 3, rows[:, BANK + CHUNK :])
+        far_rows(3, 3, 1, tile([P, CHUNK], F32, "W3B", "rows_b", 2304)[:])
+        far_rows(3, 3, 3, tile([P, CHUNK], F32, "W3B", "rows_c", -512)[:])
         far_planes(2, tile([P, PACK * CHUNK], F32, "W3B", "x12", 8128)[:])
         close_gate(0, 0, gate_tile("GR", "gate00"))
         close_gate(1, 0, gate_tile("R0", "gate10"))
@@ -552,19 +555,19 @@ def tile_list_playlist_slot_refresh_kernel(
             gated(nc.gpsimd, b, 0, 8)
         xb02 = tile([P, PACK * CHUNK], BF16, "G0", "xb02", 7168)
         weave(xb02[:], x_f32[0, 2])
-        xb12 = tile([P, PACK * CHUNK], BF16, "W3B", "xb12", 4096)
+        xb12 = tile([P, PACK * CHUNK], BF16, "W3B", "xb12", 4864)
         weave(xb12[:], x_f32[1, 2])
         xb03 = tile([P, PACK * CHUNK], BF16, "sb1", "xb03")
         weave(xb03[:], x_f32[0, 3])
-        quant_z(0, "W3B", zb0[:], 1984)
-        quant_x([(0, 2)], xb02[:], "W3B", 960)
+        quant_z(0, "W3B", zb0[:], 2816)
+        quant_x([(0, 2)], xb02[:], "W3B", 1792)
         z_tile(0, 1, "G0", 4096)
         gated(nc.gpsimd, 0, 1, 8)
         far_planes(3, tile([P, PACK * CHUNK], F32, "G0", "x13")[:])
         scores(0, 4, (nc.scalar.copy, nc.scalar.copy), tile([P, PACK * CHUNK], F32, "S0", "staged0")[:])
         for b in range(2):
             open_gate(b, 2, 2 * b)
-        xb13 = tile([P, PACK * CHUNK], BF16, "W3B", "xb13", -1088)
+        xb13 = tile([P, PACK * CHUNK], BF16, "W3B", "xb13", -256)
         weave(xb13[:], x_f32[1, 3])
         quant_x([(1, 2)], xb12[:], "R1", 64)
         z_tile(1, 1, "R1", 1088)

@@ -24,13 +24,14 @@ HALF = BANK // 2
 QUAD = 32
 LIST_COLS = BANK // 16
 CHUNK = HALF
+RIDER = 16
 
 
 AREA_SIZES = (
     ("P00", 8192), ("P01", 8192), ("P02", 8192), ("P03", 8192),
     ("P10", 8192), ("P11", 8192), ("P12", 8192), ("P13", 8192),
     ("A", 16384), ("GR", 4096), ("G1", 8192),
-    ("R0", 4096), ("R1", 8192), ("R3", 4096), ("B0", 8192), ("B1", 8192), ("G0", 12288), ("XN", 8192),
+    ("R0", 4096), ("R1", 8192), ("R3", 4096), ("B0", 8192), ("B1", 8192), ("G0", 12288), ("XN", 8448),
     ("tab_sc", 2048), ("v_sc", 2048), ("v_scp", 1024), ("v0", 4096), ("v1", 4096),
     ("w2_raw", 4096), ("w2_sc_raw", 1024), ("w2_sc_moved", 1024),
     ("wb0", 4096), ("wb1", 4096), ("sb0", 2048), ("sb1", 2048),
@@ -39,7 +40,7 @@ AREA_SIZES = (
     ("ws00", 256), ("ws01", 256), ("ws02", 256), ("ws03", 256), ("ws10", 512), ("ws11", 512),
     ("w3c", 4096), ("w3s", 1024), ("S0", 4352), ("W3B", 12224), ("b1p", 1024),
     ("x00", 1024), ("x10", 1024), ("x11", 1024),
-    ("x00s", 256), ("x01s", 256), ("x10s", 256), ("x11s", 256), ("x02s", 256), ("x12s", 256), ("x03s", 256), ("x13s", 256),
+    ("x00s", 256), ("x01s", 256), ("x10s", 256), ("x11s", 256), ("x02s", 256), ("x12s", 256), ("x03s", 512), ("x13s", 256),
     ("z0s", 512), ("z10s", 256), ("z11s", 256), ("z20s", 256), ("z21s", 256), ("zas", 256), ("zb0s", 128), ("zb1s", 128),
     ("warm", 64), ("b1f", 64), ("b1r", 64), ("b2", 64),
 )
@@ -207,11 +208,12 @@ def tile_list_playlist_slot_refresh_kernel(
                 pages[b, i][:].indirect(idx2[:, lo // 16 : hi // 16]), hs[b, i][:, lo:hi], gain[:, lo:hi], MULT
             )
 
-        x_near = tile([P, PACK * BANK], F32, "XN", "x_near")
+        x_near = tile([P, PACK * (RIDER + BANK)], F32, "XN", "x_near")
+        near_planes = as_planes(x_near[:])
         x_f32 = {}
         x_rows = {}
         for c in range(2):
-            x_f32[1, c] = as_planes(x_near[:])[:, :, CHUNK * c : CHUNK * (c + 1)]
+            x_f32[1, c] = near_planes[:, :, RIDER + CHUNK * c : RIDER + CHUNK * (c + 1)]
 
         def gather(dst, page, lo, hi):
             nc.vector.tensor_copy(dst, page[:].indirect(idx3[:, lo // 16 : hi // 16]))
@@ -225,7 +227,7 @@ def tile_list_playlist_slot_refresh_kernel(
             nc.sync.dma_start(out=dst[QUAD * t : QUAD * (t + 1), :], in_=rows)
 
         def fetch(i):
-            gather(x_near[:, BANK * i : BANK * (i + 1)], pages[1, i], 0, BANK)
+            gather(near_planes[:, i, RIDER:], pages[1, i], 0, BANK)
 
         x_codes = {}
         x_sc = {}
@@ -244,7 +246,7 @@ def tile_list_playlist_slot_refresh_kernel(
                 x_codes[key] = codes[:, CHUNK * j : CHUNK * (j + 1)]
                 x_sc[key] = scales[:, CHUNK * j : CHUNK * (j + 1)]
 
-        w3_woven = tile([P, 2 * N * PACK], BF16, "W3B", "w3_woven")
+        w3_woven = tile([P, (2 * N + CHUNK) * PACK], BF16, "W3B", "w3_woven")
         w3_raw = {}
 
         def load_w3(b, lo, hi, raw):
@@ -386,7 +388,7 @@ def tile_list_playlist_slot_refresh_kernel(
         stage_w3(0, 0, HALF, "G0", 8192)
         load_gains(3)
         load_page(1, 3)
-        stage_w3(1, HALF, N, "B1")
+        stage_w3(1, HALF, N - RIDER, "B1")
         put(1, 1, 0, S)
         features(1, 2, "R3")
         put(1, 2, 0, S)
@@ -399,7 +401,10 @@ def tile_list_playlist_slot_refresh_kernel(
         xb_near = tile([P, BANK * PACK], BF16, "wb0", "xb_near")
         weave(xb_near[:], as_planes(dealt_near))
         quant_x([(0, 0)], xb_near[:, 0 : PACK * CHUNK], "x00")
-        weave_w3(1, HALF, N)
+        weave_w3(1, HALF, N - RIDER)
+        nc.sync.dma_start(
+            out=near_planes[:, :, 0:RIDER], in_=w3[PASS:, N - RIDER :].rearrange("(p j) n -> p j n", j=PACK)
+        )
         features(1, 3, "B1")
         order_w2_words(1, 1, "b1p", nc.scalar.copy)
 
@@ -490,24 +495,26 @@ def tile_list_playlist_slot_refresh_kernel(
                 )
 
         def piece_scores(col, banks, copies, staged):
+            per_bank = N // P // len(banks)
             accs = [bank(k, "acc_e%d%d" % (col, k)) for k in banks]
             for b in range(2):
                 for n in range(N // P):
                     nc.tensor.matmul_mx(
-                        out=accs[n // 2][:, P * (n % 2) : P * (n % 2 + 1)],
+                        out=accs[n // per_bank][:, P * (n % per_bank) : P * (n % per_bank + 1)],
                         lhsT=w3_codes[:, N * b + P * n : N * b + P * (n + 1)].bitcast(FP8X4),
                         lhsT_scale=w3_sc[:, N * b + P * n : N * b + P * (n + 1)],
                         rhs=z_codes[b, col].bitcast(FP8X4),
                         rhs_scale=z_sc[b, col],
-                        start=(b == 0 and n % 2 == 0),
-                        stop=(b == 1 and n % 2 == 1),
+                        start=(b == 0 and n % per_bank == 0),
+                        stop=(b == 1 and n % per_bank == per_bank - 1),
                     )
-            for u in range(2):
-                part = staged[:, 2 * P * u : 2 * P * (u + 1)]
-                copies[u](out=part, in_=accs[u][:, 0 : 2 * P])
+            width = per_bank * P
+            for u in range(len(banks)):
+                part = staged[:, width * u : width * (u + 1)]
+                copies[u](out=part, in_=accs[u][:, 0:width])
                 nc.sync.dma_start(
-                    out=out[2 * P * u : 2 * P * (u + 1), col : col + P].rearrange("(j p) m -> p j m", p=P),
-                    in_=part.rearrange("p (j m) -> p j m", j=2),
+                    out=out[width * u : width * (u + 1), col : col + P].rearrange("(j p) m -> p j m", p=P),
+                    in_=part.rearrange("p (j m) -> p j m", j=per_bank),
                 )
 
         def far_rows(first, last, t, dst):
@@ -529,12 +536,11 @@ def tile_list_playlist_slot_refresh_kernel(
         for c in range(2):
             gather(x_f32[1, c][:, PACK - 1, :], pages[1, PACK - 1], CHUNK * c, CHUNK * (c + 1))
         far_rows(2, 3, 0, tile([P, BANK], F32, "G1", "rows_first")[:])
-        xb = tile([P, PACK * CHUNK], BF16, "w3c", "xb10")
-        weave(xb[:], x_f32[1, 0])
-        quant_x([(1, 0)], xb[:], "x10")
+        weave(w3_woven[:, PACK * (2 * N - RIDER) :], near_planes[:, :, 0 : RIDER + CHUNK])
+        quant_x([(1, 0)], w3_woven[:, PACK * 2 * N :], "x10")
         w3_codes = tile([P, 2 * N], U32, "w3c", "w3_codes")
         w3_sc = tile([P, 2 * N], U8, "w3s", "w3_sc")
-        nc.vector.quantize_mx(out=w3_codes[:].bitcast(FP8X4), scales=w3_sc[:], in_=w3_woven[:])
+        nc.vector.quantize_mx(out=w3_codes[:].bitcast(FP8X4), scales=w3_sc[:], in_=w3_woven[:, 0 : PACK * 2 * N])
         xb = tile([P, PACK * CHUNK], BF16, "sb0", "xb11")
         weave(xb[:], x_f32[1, 1])
         quant_x([(1, 1)], xb[:], "x11")
@@ -553,16 +559,16 @@ def tile_list_playlist_slot_refresh_kernel(
         for b in range(2):
             zbs[b, 0] = zb0[:, PACK * CHUNK * b : PACK * CHUNK * (b + 1)]
             gated(nc.gpsimd, b, 0, 8)
-        xb02 = tile([P, PACK * CHUNK], BF16, "G0", "xb02", 7168)
+        xb02 = tile([P, PACK * CHUNK], BF16, "G0", "xb02", 8192)
         weave(xb02[:], x_f32[0, 2])
         xb12 = tile([P, PACK * CHUNK], BF16, "W3B", "xb12", 4864)
         weave(xb12[:], x_f32[1, 2])
-        xb03 = tile([P, PACK * CHUNK], BF16, "sb1", "xb03")
-        weave(xb03[:], x_f32[0, 3])
         quant_z(0, "W3B", zb0[:], 2816)
         quant_x([(0, 2)], xb02[:], "W3B", 1792)
-        z_tile(0, 1, "G0", 4096)
+        pair = tile([P, 2 * PACK * CHUNK], BF16, "G0", "pair", 4096)
+        zbs[0, 1] = pair[:, 0 : PACK * CHUNK]
         gated(nc.gpsimd, 0, 1, 8)
+        weave(pair[:, PACK * CHUNK :], x_f32[0, 3])
         far_planes(3, tile([P, PACK * CHUNK], F32, "G0", "x13")[:])
         scores(0, 4, (nc.scalar.copy, nc.scalar.copy), tile([P, PACK * CHUNK], F32, "S0", "staged0")[:])
         for b in range(2):
@@ -572,8 +578,9 @@ def tile_list_playlist_slot_refresh_kernel(
         quant_x([(1, 2)], xb12[:], "R1", 64)
         z_tile(1, 1, "R1", 1088)
         gated(nc.vector, 1, 1, 2)
-        quant_x([(0, 3)], xb03[:], "R1", 3136)
-        quant_z_part(0, 1, "R1", -960)
+        codes, scales = quantise("x03", "R1", pair[:], 3136)
+        z_codes[0, 1], z_sc[0, 1] = codes[:, 0:CHUNK], scales[:, 0:CHUNK]
+        x_codes[0, 3], x_sc[0, 3] = codes[:, CHUNK:], scales[:, CHUNK:]
         quant_x([(1, 3)], xb13[:], "B0", 4032)
         close_gate(0, 2, gate_tile("P02", "gate02"))
         close_gate(1, 2, gate_tile("P02", "gate12", 4096))
@@ -607,4 +614,4 @@ def tile_list_playlist_slot_refresh_kernel(
         scores(2, 2, (nc.scalar.copy, nc.scalar.copy), tile([P, PACK * CHUNK], F32, "P01", "staged2")[:])
         staged = tile([P, PACK * CHUNK], F32, "P01", "staged3", 4096)
         piece_scores(M - CHUNK, (6, 7), (nc.scalar.copy, nc.scalar.copy), staged[:, 0:BANK])
-        piece_scores(M - P, (4, 5), (nc.scalar.copy, nc.vector.tensor_copy), staged[:, BANK:])
+        piece_scores(M - P, (4, 5, 0, 1), (nc.scalar.copy, nc.vector.tensor_copy) * 2, staged[:, BANK:])

@@ -24,6 +24,7 @@ HALF = BANK // 2
 QUAD = 32
 LIST_COLS = BANK // 16
 CHUNK = HALF
+EXTRA = 64
 RIDER = 16
 
 
@@ -38,7 +39,7 @@ AREA_SIZES = (
     ("h3", 4096), ("h0", 4096), ("h1", 4096), ("h2", 4096),
     ("wc00", 1024), ("wc01", 1024), ("wc02", 1024), ("wc03", 1024), ("wc10", 2048), ("wc11", 2048),
     ("ws00", 256), ("ws01", 256), ("ws02", 256), ("ws03", 256), ("ws10", 512), ("ws11", 512),
-    ("w3c", 4096), ("w3s", 1024), ("S0", 4352), ("W3B", 12224), ("b1p", 1024),
+    ("w3c", 4096), ("w3s", 1024), ("S0", 4352), ("W3B", 13056), ("b1p", 1024),
     ("x00", 1024), ("x10", 1024), ("x11", 1024),
     ("x00s", 256), ("x01s", 256), ("x10s", 256), ("x11s", 256), ("x02s", 256), ("x12s", 256), ("x03s", 512), ("x13s", 256),
     ("z0s", 512), ("z10s", 256), ("z11s", 256), ("z20s", 256), ("z21s", 256), ("zas", 256), ("zb0s", 128), ("zb1s", 128),
@@ -544,13 +545,15 @@ def tile_list_playlist_slot_refresh_kernel(
         xb = tile([P, PACK * CHUNK], BF16, "sb0", "xb11")
         weave(xb[:], x_f32[1, 1])
         quant_x([(1, 1)], xb[:], "x11")
-        rows = tile([P, PACK * CHUNK], F32, "W3B", "rows_a", 3328)
+        rows = tile([P, BANK + CHUNK], F32, "W3B", "rows_a", 3328)
         far_rows(2, 3, 2, rows[:, 0:BANK])
         far_rows(2, 2, 1, rows[:, BANK : BANK + CHUNK])
-        far_rows(2, 2, 3, rows[:, BANK + CHUNK :])
+        shared = tile([P, PACK * (EXTRA + CHUNK)], BF16, "W3B", "shared", 6400)
+        xb12 = shared[:, PACK * EXTRA :]
+        far_rows(2, 2, 3, xb12[:, 0 : 2 * CHUNK].bitcast(F32))
         far_rows(3, 3, 1, tile([P, CHUNK], F32, "W3B", "rows_b", 2304)[:])
         far_rows(3, 3, 3, tile([P, CHUNK], F32, "W3B", "rows_c", -512)[:])
-        far_planes(2, tile([P, PACK * CHUNK], F32, "W3B", "x12", 8128)[:])
+        far_planes(2, tile([P, PACK * CHUNK], F32, "W3B", "x12", 8960)[:])
         close_gate(0, 0, gate_tile("GR", "gate00"))
         close_gate(1, 0, gate_tile("R0", "gate10"))
         close_gate(0, 1, gate_tile("R1", "gate01"))
@@ -559,10 +562,11 @@ def tile_list_playlist_slot_refresh_kernel(
         for b in range(2):
             zbs[b, 0] = zb0[:, PACK * CHUNK * b : PACK * CHUNK * (b + 1)]
             gated(nc.gpsimd, b, 0, 8)
+        zbs[1, 1] = shared[:, 0 : PACK * CHUNK]
+        product(nc.gpsimd, shared[:, 0 : PACK * EXTRA], 1, 1, 0, EXTRA, 8)
         xb02 = tile([P, PACK * CHUNK], BF16, "G0", "xb02", 8192)
         weave(xb02[:], x_f32[0, 2])
-        xb12 = tile([P, PACK * CHUNK], BF16, "W3B", "xb12", 4864)
-        weave(xb12[:], x_f32[1, 2])
+        weave(xb12, x_f32[1, 2])
         quant_z(0, "W3B", zb0[:], 2816)
         quant_x([(0, 2)], xb02[:], "W3B", 1792)
         pair = tile([P, 2 * PACK * CHUNK], BF16, "G0", "pair", 4096)
@@ -575,13 +579,13 @@ def tile_list_playlist_slot_refresh_kernel(
             open_gate(b, 2, 2 * b)
         xb13 = tile([P, PACK * CHUNK], BF16, "W3B", "xb13", -256)
         weave(xb13[:], x_f32[1, 3])
-        quant_x([(1, 2)], xb12[:], "R1", 64)
-        z_tile(1, 1, "R1", 1088)
-        gated(nc.vector, 1, 1, 2)
-        codes, scales = quantise("x03", "R1", pair[:], 3136)
+        quant_x([(1, 2)], xb12, "A")
+        codes, scales = quantise("x03", "A", pair[:], 1024)
         z_codes[0, 1], z_sc[0, 1] = codes[:, 0:CHUNK], scales[:, 0:CHUNK]
         x_codes[0, 3], x_sc[0, 3] = codes[:, CHUNK:], scales[:, CHUNK:]
-        quant_x([(1, 3)], xb13[:], "B0", 4032)
+        product(nc.vector, shared[:, PACK * EXTRA : PACK * CHUNK], 1, 1, EXTRA, CHUNK, 2)
+        quant_x([(1, 3)], xb13[:], "A", 3072)
+        quant_z_part(1, 1, "v0", 3072)
         close_gate(0, 2, gate_tile("P02", "gate02"))
         close_gate(1, 2, gate_tile("P02", "gate12", 4096))
         open_gate(0, 3, 6)
@@ -590,7 +594,6 @@ def tile_list_playlist_slot_refresh_kernel(
         close_gate(1, 3, gate_tile("P03", "gate13", 4096))
         z_tile(0, 2, "B0", -64)
         gated(nc.vector, 0, 2, 2)
-        quant_z_part(1, 1, "v0", 3072)
         z_tile(1, 2, "B0", 1984)
         gated(nc.vector, 1, 2, 2)
         quant_z_part(0, 2, "v1")

from contextlib import ExitStack

import concourse.mybir as mybir

K, T, S, T2, H, M, N = 1024, 2048, 1024, 2048, 1024, 1024, 512
FLOPS = 2 * K * H * S + 2 * H * H * M + 2 * H * N * M

F32 = mybir.dt.float32
BF16 = mybir.dt.bfloat16
I32 = mybir.dt.int32
U32 = mybir.dt.uint32
U16 = mybir.dt.uint16
U8 = mybir.dt.uint8
FP8X4 = mybir.dt.float8_e4m3fn_x4
FP4X4 = mybir.dt.float4_e2m1fn_x4
MULT = mybir.AluOpType.mult
ACT = mybir.ActivationFunctionType

P = 128
PACK = 4
PASS = P * PACK
BANK = 512
HALF = BANK // 2
QUAD = 32
LIST_COLS = BANK // 16
CHUNK = HALF
EXTRA = 64
RIDER = 16


AREA_SIZES = (
    ("P00", 8192), ("P01", 8192), ("P02", 8192), ("P03", 8192),
    ("P10", 8192), ("P11", 8192), ("P12", 8192), ("P13", 8192),
    ("A", 16384), ("GR", 4096), ("G1", 8192),
    ("R0", 4096), ("R1", 8192), ("R3", 4096), ("B0", 8192), ("B1", 8192), ("G0", 12288), ("XN", 8448),
    ("tab_sc", 2048), ("v_sc", 2048), ("v_scp", 1024), ("v0", 4096), ("v1", 4096),
    ("w2_raw", 4096), ("w2_sc_raw", 1024), ("w2_sc_moved", 1024),
    ("wb0", 4096), ("wb1", 4096), ("sb0", 2048), ("sb1", 2048),
    ("h3", 4096), ("h0", 4096), ("h1", 4096), ("h2", 4096),
    ("wc00", 1024), ("wc01", 1024), ("wc02", 1024), ("wc03", 1024), ("wc10", 2048), ("wc11", 2048),
    ("ws00", 256), ("ws01", 256), ("ws02", 256), ("ws03", 256), ("ws10", 512), ("ws11", 512),
    ("w3c", 4096), ("w3s", 1024), ("S0", 4352), ("W3B", 13056), ("b1p", 1024),
    ("x00", 1024), ("x10", 1024), ("x11", 1024),
    ("x00s", 256), ("x01s", 256), ("x10s", 256), ("x11s", 256), ("x02s", 256), ("x12s", 256), ("x03s", 512), ("x13s", 256),
    ("z0s", 512), ("z10s", 256), ("z11s", 256), ("z20s", 256), ("z21s", 256), ("zas", 256), ("zb0s", 128), ("zb1s", 128),
    ("warm", 64), ("b1f", 64), ("b1r", 64), ("b2", 64),
)


def area_offsets():
    starts = {}
    at = 0
    for area, size in AREA_SIZES:
        starts[area] = at
        at = at + size
    return starts


AREA = area_offsets()


def tile_list_playlist_slot_refresh_kernel(
    tc, tab_words, tab_scales, offs, offs2, offs3, w1, b1, wgs, page0, w2_words, w2_scales, b2, w3, out
):
    nc = tc.nc
    with ExitStack() as ctx:
        lists = ctx.enter_context(tc.tile_pool(name="lists", bufs=1))
        sb = ctx.enter_context(tc.tile_pool(name="sb", bufs=1))
        psum = ctx.enter_context(tc.psum_pool(name="psum", bufs=1))

        def tile(shape, dtype, area, name, at=0):
            start = AREA[area] + at
            return sb.tile(shape, dtype, name=name, offset=start, align_bytes=256 if start % 256 == 0 else 64)

        def bank(k, name):
            return psum.tile([P, BANK], F32, tag="bank%d" % k, name=name)

        def as_planes(ap):
            return ap.rearrange("p (t m) -> p t m", t=PACK)

        idx = lists.tile([P, S // 16], U16, name="idx")
        idx2 = lists.tile([P, S // 16], U16, name="idx2")
        idx3 = lists.tile([P, M // 16], U16, name="idx3")

        def weave(dst, src):
            nc.scalar.copy(
                out=dst.rearrange("p (c i t) -> p c t i", i=PACK, t=PACK),
                in_=src.rearrange("p t (c i) -> p c t i", i=PACK),
            )

        tab_sc = tile([P, T], U8, "tab_sc", "tab_sc")
        nc.vector.memset(tab_sc[QUAD : 2 * QUAD, :].bitcast(I32), 0)
        nc.vector.memset(tab_sc[2 * QUAD : P, :].bitcast(I32), 0)
        v_sc = tile([P, 2, S], U8, "v_sc", "v_sc")
        nc.gpsimd.memset(v_sc[:].bitcast(I32), 0)
        w2_sc_raw = tile([P, H], U8, "w2_sc_raw", "w2_sc_raw")
        nc.gpsimd.memset(w2_sc_raw[:].bitcast(I32), 0)
        w2_sc_moved = tile([P, H], U8, "w2_sc_moved", "w2_sc_moved")
        nc.gpsimd.memset(w2_sc_moved[:].bitcast(I32), 0)
        b1_first = tile([P, 1], F32, "b1f", "b1_first")
        b1_rows = tile([P, PACK - 1], F32, "b1r", "b1_rows")
        b1_planes = tile([P, PACK], F32, "b1p", "b1_planes")
        b2_sb = tile([P, 2, PACK], F32, "b2", "b2_sb")

        gains_rows = tile([P, S], F32, "GR", "gains_rows")
        gains = [tile([P, 2, S], F32, "G%d" % u, "gains%d" % u) for u in range(2)]
        wgs_rows = wgs.rearrange("(r i) j -> r i j", i=PACK)

        def load_gains(i):
            for q in (0, 2, 1, 3):
                nc.sync.dma_start(out=gains[i // 2][QUAD * q : QUAD * (q + 1), i % 2, :], in_=wgs_rows[:, i, :])

        tab_w = tile([P, 2 * T], I32, "A", "tab_w")
        v_codes = [tile([P, S], U32, "v%d" % a, "v_codes%d" % a) for a in range(2)]
        v_sc_packed = tile([P, S], U8, "v_scp", "v_sc_packed")
        w1_codes = {}
        w1_sc = {}

        def load_tab(a, lo, hi):
            nc.sync.dma_start(
                out=tab_w[:, T * a + lo : T * a + hi],
                in_=tab_words[a].rearrange("p t i -> p (t i)").bitcast(I32)[:, lo:hi],
            )

        def tab_window(a):
            return tab_w[:, T * a : T * (a + 1)].bitcast(U32)

        w1_raw = {}

        def load_w1_rows(t0, t1, a):
            if a == 0:
                w1_raw[t0] = tile([P, 2, PACK * P * (t1 - t0)], F32, "R%d" % t0, "w1_raw0%d" % t0)
            rows = w1[PASS * a : PASS * (a + 1), P * t0 : P * t1]
            nc.sync.dma_start(
                out=w1_raw[t0][:, a, :].rearrange("p (j c) -> p j c", j=PACK),
                in_=rows.rearrange("(p j) c -> p j c", j=PACK),
            )

        def prep_w1_rows(t, t0, slot):
            grouped = tile([P, 2, PASS], BF16, slot, "w1_b0%d" % t)
            codes = tile([P, 2 * P], U32, "wc0%d" % t, "w1_codes0%d" % t)
            scales = tile([P, 2 * P], U8, "ws0%d" % t, "w1_sc0%d" % t)
            for a in range(2):
                block = w1_raw[t0][:, a, :].rearrange("p (j c) -> p j c", j=PACK)[:, :, P * (t - t0) : P * (t - t0 + 1)]
                weave(grouped[:, a, :], block)
                w1_codes[a, 0, t] = codes[:, P * a : P * (a + 1)]
                w1_sc[a, 0, t] = scales[:, P * a : P * (a + 1)]
            nc.vector.quantize_mx(
                out=codes[:].bitcast(FP8X4), scales=scales[:], in_=grouped[:].rearrange("p a k -> p (a k)")
            )

        def prep_w1_planes(a, grouped):
            raw = tile([P, PACK, PASS], F32, "B%d" % a, "w1_raw1%d" % a)
            rows = w1[PASS * a : PASS * (a + 1), PASS : 2 * PASS]
            nc.sync.dma_start(out=raw[:], in_=rows.rearrange("(p j) c -> p j c", j=PACK))
            nc.scalar.copy(
                out=grouped[:, a, :].rearrange("p (t m j) -> p m j t", t=PACK, j=PACK),
                in_=raw[:].rearrange("p j (m t) -> p m j t", t=PACK),
            )

        def quant_w1_planes(grouped):
            codes = tile([P, 2 * PASS], U32, "wc10", "w1_codes1")
            scales = tile([P, 2 * PASS], U8, "ws10", "w1_sc1")
            nc.vector.quantize_mx(
                out=codes[:].bitcast(FP8X4), scales=scales[:], in_=grouped[:].rearrange("p a k -> p (a k)")
            )
            for a in range(2):
                for i in range(PACK):
                    w1_codes[a, 1, i] = codes[:, PASS * a + P * i : PASS * a + P * (i + 1)]
                    w1_sc[a, 1, i] = scales[:, PASS * a + P * i : PASS * a + P * (i + 1)]

        pages = {}

        def load_page(b, i):
            page = tile([P, T2], F32, "P%d%d" % (b, i), "page%d%d" % (b, i))
            if b == 0:
                rows = page0[P * i : P * (i + 1), :]
            else:
                rows = page0[PASS : 2 * PASS, :].rearrange("(p i) t -> p i t", i=PACK)[:, i, :]
            nc.sync.dma_start(out=page[:], in_=rows)
            pages[b, i] = page

        hs = {}

        def features(b, i, slot, cuts=(0, BANK, S), first_bank=None):
            h = tile([P, S], F32, slot, "h%d%d" % (b, i))
            bias = b1_planes[:, i : i + 1] if b == 1 else b1_rows[:, i - 1 : i] if i > 0 else b1_first[:]
            spans = list(zip(cuts, cuts[1:]))
            start = 2 * i if first_bank is None else first_bank
            accs = [bank(start + c, "acc_h%d" % c) for c in range(len(spans))]
            for acc, (lo, hi) in zip(accs, spans):
                for a in range(2):
                    nc.tensor.matmul_mx(
                        out=acc[:, 0 : hi - lo],
                        lhsT=w1_codes[a, b, i].bitcast(FP8X4),
                        lhsT_scale=w1_sc[a, b, i],
                        rhs=v_codes[a][:, lo:hi].bitcast(FP8X4),
                        rhs_scale=v_sc[:, a, lo:hi],
                        start=(a == 0),
                        stop=(a == 1),
                    )
            for acc, (lo, hi) in zip(accs, spans):
                nc.scalar.activation(out=h[:, lo:hi], in_=acc[:, 0 : hi - lo], func=ACT.Identity, bias=bias)
            hs[b, i] = h

        def put(b, i, lo, hi):
            gain = gains_rows[:] if b == 0 else gains[i // 2][:, i % 2, :]
            nc.vector.tensor_tensor(
                pages[b, i][:].indirect(idx2[:, lo // 16 : hi // 16]), hs[b, i][:, lo:hi], gain[:, lo:hi], MULT
            )

        x_near = tile([P, PACK * (RIDER + BANK)], F32, "XN", "x_near")
        near_planes = as_planes(x_near[:])
        x_f32 = {}
        x_rows = {}
        for c in range(2):
            x_f32[1, c] = near_planes[:, :, RIDER + CHUNK * c : RIDER + CHUNK * (c + 1)]

        def gather(dst, page, lo, hi):
            nc.vector.tensor_copy(dst, page[:].indirect(idx3[:, lo // 16 : hi // 16]))

        def fetch_rows(t, slot, at=0):
            rows = tile([P, BANK], F32, slot, "x_rows%d" % t, at)
            gather(rows[:], pages[0, t], 0, BANK)
            x_rows[t] = rows

        def deal(dst, t, rows):
            nc.sync.dma_start(out=dst[QUAD * t : QUAD * (t + 1), :], in_=rows)

        def fetch(i):
            gather(near_planes[:, i, RIDER:], pages[1, i], 0, BANK)

        x_codes = {}
        x_sc = {}

        def quantise(name, slot, woven, at=0):
            width = woven.shape[1] // PACK
            codes = tile([P, width], U32, slot, name + "_codes", at)
            scales = tile([P, width], U8, name + "s", name + "_sc")
            nc.vector.quantize_mx(out=codes[:].bitcast(FP8X4), scales=scales[:], in_=woven)
            return codes, scales

        def quant_x(keys, woven, slot, at=0):
            name = "x%d%d" % keys[0]
            codes, scales = quantise(name, slot, woven, at)
            for j, key in enumerate(keys):
                x_codes[key] = codes[:, CHUNK * j : CHUNK * (j + 1)]
                x_sc[key] = scales[:, CHUNK * j : CHUNK * (j + 1)]

        w3_woven = tile([P, (2 * N + CHUNK) * PACK], BF16, "W3B", "w3_woven")
        w3_raw = {}

        def load_w3(b, lo, hi, raw):
            part = raw.rearrange("p (j n) -> p j n", j=PACK)
            rows = w3[PASS * b : PASS * (b + 1), lo:hi]
            nc.sync.dma_start(out=part, in_=rows.rearrange("(p j) n -> p j n", j=PACK))
            w3_raw[b, lo] = part

        def stage_w3(b, lo, hi, slot, at=0):
            raw = tile([P, PACK * (hi - lo)], F32, slot, "w3_raw%d%d" % (b, lo), at)
            load_w3(b, lo, hi, raw[:])

        def weave_w3(b, lo, hi):
            weave(w3_woven[:, PACK * (N * b + lo) : PACK * (N * b + hi)], w3_raw[b, lo])

        w2_raw = tile([P, 2, 2 * H], U8, "w2_raw", "w2_raw")
        w2_codes = {}
        w2_sc = {}

        def load_w2():
            nc.sync.dma_start(out=w2_raw[:].bitcast(I32), in_=w2_words.rearrange("a p c -> p a c").bitcast(I32))

        def load_w2_scales():
            for q in range(4):
                nc.sync.dma_start(
                    out=w2_sc_raw[QUAD * q : QUAD * q + 8, :].bitcast(I32),
                    in_=w2_scales[:, 4 * q : 4 * q + 4, :].bitcast(I32),
                )

        def order_w2_words(a, b, slot, copy):
            codes = tile([P, 2 * PASS], U8, slot, "w2_codes%d%d" % (a, b))
            copy(
                out=codes[:].bitcast(U16).rearrange("p (t m) -> p t m", t=PACK),
                in_=w2_raw[:, a, 2 * PASS * b : 2 * PASS * (b + 1)].bitcast(U16).rearrange("p (m t) -> p t m", t=PACK),
            )
            w2_codes[a, b] = codes

        def order_w2_scales(slot):
            both = tile([P, H], U8, slot, "w2_sc_both")
            nc.gpsimd.tensor_copy(
                out=both[:].rearrange("p (b t m) -> p b t m", b=2, t=PACK),
                in_=w2_sc_raw[:].rearrange("p (b m t) -> p b t m", b=2, t=PACK),
            )
            for b in range(2):
                w2_sc[0, b] = both[:, PASS * b : PASS * (b + 1)]
                w2_sc[1, b] = w2_sc_moved[:, PASS * b : PASS * (b + 1)]
            for q in range(4):
                nc.sync.dma_start(
                    out=w2_sc_moved[QUAD * q : QUAD * q + 4, :].bitcast(I32),
                    in_=both[QUAD * q + 4 : QUAD * q + 8, :].bitcast(I32),
                )

        nc.sync.dma_start(idx[:], offs)
        for a in range(2):
            nc.sync.dma_start(out=tab_sc[a:QUAD:2, :].bitcast(I32), in_=tab_scales[a].bitcast(I32))
        load_tab(0, 0, T)
        nc.sync.dma_start(out=b1_first[:], in_=b1[0:P].rearrange("(p t) -> p t", t=1))
        warm = tile([P, 2], F32, "warm", "warm")
        nc.gpsimd.memset(warm[:, 0:1], 0.0)
        nc.scalar.activation(out=warm[:, 1:2], in_=warm[:, 0:1], func=ACT.Sigmoid)
        nc.sync.dma_start(idx2[:], offs2)
        nc.vector.tensor_copy(v_sc_packed[:], tab_sc[:].indirect(idx[:]))
        nc.vector.tensor_copy(v_codes[0][:], tab_window(0).indirect(idx[:]))
        load_w1_rows(0, 1, 0)
        load_w1_rows(0, 1, 1)
        prep_w1_rows(0, 0, "wb0")
        load_tab(1, 0, T // 2)
        load_tab(1, T // 2, T)
        nc.sync.dma_start(idx3[:], offs3)
        for q in range(4):
            nc.sync.dma_start(
                out=v_sc[QUAD * q : QUAD * q + 4, :, :].bitcast(I32),
                in_=v_sc_packed[8 * q : 8 * q + 8, :].bitcast(I32),
            )
        first_cuts = (0, HALF, BANK, S)
        for lo, hi in zip(first_cuts, first_cuts[1:]):
            nc.vector.tensor_copy(v_codes[1][:, lo:hi], tab_window(1).indirect(idx[:, lo // 16 : hi // 16]))
        dealt_near = tile([P, PACK * BANK], F32, "A", "dealt_near")[:]
        dealt_far = {}
        for c in range(2):
            x_f32[0, c] = as_planes(dealt_near)[:, :, CHUNK * c : CHUNK * (c + 1)]
            dealt_far[2 + c] = tile([P, PACK * CHUNK], F32, "A", "dealt%d" % (2 + c), 8192 + 4096 * c)
            x_f32[0, 2 + c] = as_planes(dealt_far[2 + c][:])
        load_page(0, 0)
        nc.sync.dma_start(out=gains_rows[:, 0:BANK], in_=wgs[:, 0:BANK])
        features(0, 0, "h0", first_cuts, 5)
        put(0, 0, 0, BANK)
        load_w1_rows(1, 3, 0)
        load_w1_rows(1, 3, 1)
        prep_w1_rows(1, 1, "sb0")
        with nc.allow_non_contiguous_dma(reason="one bias value for each partition and block of 128 channels"):
            nc.sync.dma_start(out=b1_rows[:], in_=b1[P:PASS].rearrange("(t p) -> p t", p=P))
        features(0, 1, "h1")
        nc.sync.dma_start(out=gains_rows[:, BANK:S], in_=wgs[:, BANK:S])
        put(0, 0, BANK, S)
        prep_w1_rows(2, 1, "sb1")
        features(0, 2, "h2")
        load_page(0, 1)
        put(0, 1, 0, S)
        load_w1_rows(3, 4, 0)
        load_w1_rows(3, 4, 1)
        prep_w1_rows(3, 3, "wb1")
        fetch_rows(0, "R3")
        features(0, 3, "h0")
        load_w2()
        order_w2_words(0, 0, "h1", nc.gpsimd.tensor_copy)
        load_page(0, 2)
        nc.sync.dma_start(out=b1_planes[:], in_=b1[PASS : 2 * PASS].rearrange("(p i) -> p i", i=PACK))
        nc.sync.dma_start(out=b2_sb[:], in_=b2.rearrange("(a p i) -> p a i", a=2, i=PACK))
        put(0, 2, 0, S)
        order_w2_words(0, 1, "h2", nc.gpsimd.tensor_copy)
        w1_planes = tile([P, 2, PASS * PACK], BF16, "wb0", "w1_b1")
        prep_w1_planes(0, w1_planes)
        fetch_rows(1, "B0")
        prep_w1_planes(1, w1_planes)
        quant_w1_planes(w1_planes)
        load_page(0, 3)
        put(0, 3, 0, S)
        order_w2_words(1, 0, "h0", nc.gpsimd.tensor_copy)
        stage_w3(0, HALF, N, "R1")
        weave_w3(0, HALF, N)
        fetch_rows(2, "R1")
        fetch_rows(3, "R1", 2048)
        features(1, 0, "R0")
        features(1, 1, "h3")
        load_gains(0)
        load_page(1, 0)
        put(1, 0, 0, S)
        load_gains(1)
        load_page(1, 1)
        load_w2_scales()
        deal(dealt_near, 0, x_rows[0][:])
        deal(dealt_near, 1, x_rows[1][:])
        load_gains(2)
        load_page(1, 2)
        deal(dealt_near, 2, x_rows[2][:])
        deal(dealt_near, 3, x_rows[3][:])
        load_w3(1, 0, HALF, x_near[:, HALF : HALF + 2 * BANK])
        stage_w3(0, 0, HALF, "G0", 8192)
        load_gains(3)
        load_page(1, 3)
        stage_w3(1, HALF, N - RIDER, "B1")
        put(1, 1, 0, S)
        features(1, 2, "R3")
        put(1, 2, 0, S)
        order_w2_scales("R3")
        weave_w3(1, 0, HALF)
        weave_w3(0, 0, HALF)
        fetch(0)
        fetch(1)
        fetch(2)
        xb_near = tile([P, BANK * PACK], BF16, "wb0", "xb_near")
        weave(xb_near[:], as_planes(dealt_near))
        quant_x([(0, 0)], xb_near[:, 0 : PACK * CHUNK], "x00")
        weave_w3(1, HALF, N - RIDER)
        nc.sync.dma_start(
            out=near_planes[:, :, 0:RIDER], in_=w3[PASS:, N - RIDER :].rearrange("(p j) n -> p j n", j=PACK)
        )
        features(1, 3, "B1")
        order_w2_words(1, 1, "b1p", nc.scalar.copy)

        gate_banks = {}
        gates = {}
        zbs = {}
        z_codes = {}
        z_sc = {}

        def gate_passes(a, b, c):
            for i in range(PACK):
                acc = gate_banks[b, c][i // 2]
                nc.tensor.matmul_mx(
                    out=acc[:, CHUNK * (i % 2) : CHUNK * (i % 2 + 1)],
                    lhsT=w2_codes[a, b][:, 2 * P * i : 2 * P * (i + 1)].bitcast(FP4X4),
                    lhsT_scale=w2_sc[a, b][:, P * i : P * (i + 1)],
                    rhs=x_codes[a, c].bitcast(FP8X4),
                    rhs_scale=x_sc[a, c],
                    start=(a == 0 and i % 2 == 0),
                    stop=(a == 1 and i % 2 == 1),
                )

        def open_gate(b, c, first):
            gate_banks[b, c] = [bank(first + u, "acc_g%d%d%d" % (b, c, u)) for u in range(2)]
            gate_passes(0, b, c)

        def close_gate(b, c, g):
            gate_passes(1, b, c)
            gates[b, c] = g
            for i in range(PACK):
                nc.scalar.activation(
                    out=g[:, i, :],
                    in_=gate_banks[b, c][i // 2][:, CHUNK * (i % 2) : CHUNK * (i % 2 + 1)],
                    func=ACT.Sigmoid,
                    bias=b2_sb[:, b, i : i + 1],
                )

        def gate_tile(slot, name, at=0):
            return as_planes(tile([P, PACK * CHUNK], F32, slot, name, at)[:])

        def product(engine, dst, b, c, lo, hi, run):
            engine.tensor_tensor(
                dst.rearrange("p (m e t) -> p m t e", e=run, t=PACK),
                x_f32[b, c][:, :, lo:hi].rearrange("p t (m e) -> p m t e", e=run),
                gates[b, c][:, :, lo:hi].rearrange("p t (m e) -> p m t e", e=run),
                MULT,
            )

        def gated(engine, b, c, run):
            product(engine, zbs[b, c], b, c, 0, CHUNK, run)

        def z_tile(b, c, slot, at=0):
            zbs[b, c] = tile([P, PACK * CHUNK], BF16, slot, "zb%d%d" % (b, c), at)[:]

        def quant_z(c, slot, both, at=0):
            codes, scales = quantise("z%d" % c, slot, both, at)
            for b in range(2):
                z_codes[b, c] = codes[:, CHUNK * b : CHUNK * (b + 1)]
                z_sc[b, c] = scales[:, CHUNK * b : CHUNK * (b + 1)]

        def quant_z_part(b, c, slot, at=0):
            codes, scales = quantise("z%d%d" % (c, b), slot, zbs[b, c], at)
            z_codes[b, c] = codes[:]
            z_sc[b, c] = scales[:]

        def score_pass(acc, n, b, c):
            nc.tensor.matmul_mx(
                out=acc,
                lhsT=w3_codes[:, N * b + P * n : N * b + P * (n + 1)].bitcast(FP8X4),
                lhsT_scale=w3_sc[:, N * b + P * n : N * b + P * (n + 1)],
                rhs=z_codes[b, c].bitcast(FP8X4),
                rhs_scale=z_sc[b, c],
                start=(b == 0),
                stop=(b == 1),
            )

        def scores(c, first, copies, staged):
            for u in range(2):
                acc = bank(first + u, "acc_o%d%d" % (c, u))
                for j in range(2):
                    for b in range(2):
                        score_pass(acc[:, CHUNK * j : CHUNK * (j + 1)], 2 * u + j, b, c)
                part = staged[:, BANK * u : BANK * (u + 1)]
                copies[u](out=part, in_=acc[:])
                nc.sync.dma_start(
                    out=out[2 * P * u : 2 * P * (u + 1), CHUNK * c : CHUNK * (c + 1)].rearrange("(j p) m -> p j m", p=P),
                    in_=part.rearrange("p (j m) -> p j m", j=2),
                )

        def piece_scores(col, banks, copies, staged):
            per_bank = N // P // len(banks)
            accs = [bank(k, "acc_e%d%d" % (col, k)) for k in banks]
            for b in range(2):
                for n in range(N // P):
                    nc.tensor.matmul_mx(
                        out=accs[n // per_bank][:, P * (n % per_bank) : P * (n % per_bank + 1)],
                        lhsT=w3_codes[:, N * b + P * n : N * b + P * (n + 1)].bitcast(FP8X4),
                        lhsT_scale=w3_sc[:, N * b + P * n : N * b + P * (n + 1)],
                        rhs=z_codes[b, col].bitcast(FP8X4),
                        rhs_scale=z_sc[b, col],
                        start=(b == 0 and n % per_bank == 0),
                        stop=(b == 1 and n % per_bank == per_bank - 1),
                    )
            width = per_bank * P
            for u in range(len(banks)):
                part = staged[:, width * u : width * (u + 1)]
                copies[u](out=part, in_=accs[u][:, 0:width])
                nc.sync.dma_start(
                    out=out[width * u : width * (u + 1), col : col + P].rearrange("(j p) m -> p j m", p=P),
                    in_=part.rearrange("p (j m) -> p j m", j=per_bank),
                )

        def far_rows(first, last, t, dst):
            gather(dst, pages[0, t], CHUNK * first, CHUNK * (last + 1))
            for c in range(first, last + 1):
                deal(dealt_far[c], t, dst[:, CHUNK * (c - first) : CHUNK * (c - first + 1)])

        def far_planes(c, dst):
            x_f32[1, c] = as_planes(dst)
            for i in range(PACK):
                gather(x_f32[1, c][:, i, :], pages[1, i], CHUNK * c, CHUNK * (c + 1))

        for b in range(2):
            open_gate(b, 0, 2 * b)
        put(1, 3, 0, S)
        quant_x([(0, 1)], xb_near[:, PACK * CHUNK :], "w2_raw")
        for b in range(2):
            open_gate(b, 1, 4 + 2 * b)
        for c in range(2):
            gather(x_f32[1, c][:, PACK - 1, :], pages[1, PACK - 1], CHUNK * c, CHUNK * (c + 1))
        far_rows(2, 3, 0, tile([P, BANK], F32, "G1", "rows_first")[:])
        weave(w3_woven[:, PACK * (2 * N - RIDER) :], near_planes[:, :, 0 : RIDER + CHUNK])
        quant_x([(1, 0)], w3_woven[:, PACK * 2 * N :], "x10")
        w3_codes = tile([P, 2 * N], U32, "w3c", "w3_codes")
        w3_sc = tile([P, 2 * N], U8, "w3s", "w3_sc")
        nc.vector.quantize_mx(out=w3_codes[:].bitcast(FP8X4), scales=w3_sc[:], in_=w3_woven[:, 0 : PACK * 2 * N])
        xb = tile([P, PACK * CHUNK], BF16, "sb0", "xb11")
        weave(xb[:], x_f32[1, 1])
        quant_x([(1, 1)], xb[:], "x11")
        rows = tile([P, BANK + CHUNK], F32, "W3B", "rows_a", 3328)
        far_rows(2, 3, 2, rows[:, 0:BANK])
        far_rows(2, 2, 1, rows[:, BANK : BANK + CHUNK])
        shared = tile([P, PACK * (EXTRA + CHUNK)], BF16, "W3B", "shared", 6400)
        xb12 = shared[:, PACK * EXTRA :]
        far_rows(2, 2, 3, xb12[:, 0 : 2 * CHUNK].bitcast(F32))
        far_rows(3, 3, 1, tile([P, CHUNK], F32, "W3B", "rows_b", 2304)[:])
        far_rows(3, 3, 3, tile([P, CHUNK], F32, "W3B", "rows_c", -512)[:])
        far_planes(2, tile([P, PACK * CHUNK], F32, "W3B", "x12", 8960)[:])
        close_gate(0, 0, gate_tile("GR", "gate00"))
        close_gate(1, 0, gate_tile("R0", "gate10"))
        close_gate(0, 1, gate_tile("R1", "gate01"))
        close_gate(1, 1, gate_tile("B0", "gate11"))
        zb0 = tile([P, 2 * PACK * CHUNK], BF16, "G0", "zb0", 3072)
        for b in range(2):
            zbs[b, 0] = zb0[:, PACK * CHUNK * b : PACK * CHUNK * (b + 1)]
            gated(nc.gpsimd, b, 0, 8)
        zbs[1, 1] = shared[:, 0 : PACK * CHUNK]
        product(nc.gpsimd, shared[:, 0 : PACK * EXTRA], 1, 1, 0, EXTRA, 8)
        xb02 = tile([P, PACK * CHUNK], BF16, "G0", "xb02", 8192)
        weave(xb02[:], x_f32[0, 2])
        weave(xb12, x_f32[1, 2])
        quant_z(0, "W3B", zb0[:], 2816)
        quant_x([(0, 2)], xb02[:], "W3B", 1792)
        pair = tile([P, 2 * PACK * CHUNK], BF16, "G0", "pair", 4096)
        zbs[0, 1] = pair[:, 0 : PACK * CHUNK]
        gated(nc.gpsimd, 0, 1, 8)
        weave(pair[:, PACK * CHUNK :], x_f32[0, 3])
        far_planes(3, tile([P, PACK * CHUNK], F32, "G0", "x13")[:])
        scores(0, 4, (nc.scalar.copy, nc.scalar.copy), tile([P, PACK * CHUNK], F32, "S0", "staged0")[:])
        for b in range(2):
            open_gate(b, 2, 2 * b)
        xb13 = tile([P, PACK * CHUNK], BF16, "W3B", "xb13", -256)
        weave(xb13[:], x_f32[1, 3])
        quant_x([(1, 2)], xb12, "A")
        codes, scales = quantise("x03", "A", pair[:], 1024)
        z_codes[0, 1], z_sc[0, 1] = codes[:, 0:CHUNK], scales[:, 0:CHUNK]
        x_codes[0, 3], x_sc[0, 3] = codes[:, CHUNK:], scales[:, CHUNK:]
        product(nc.vector, shared[:, PACK * EXTRA : PACK * CHUNK], 1, 1, EXTRA, CHUNK, 2)
        quant_x([(1, 3)], xb13[:], "A", 3072)
        quant_z_part(1, 1, "v0", 3072)
        close_gate(0, 2, gate_tile("P02", "gate02"))
        close_gate(1, 2, gate_tile("P02", "gate12", 4096))
        open_gate(0, 3, 6)
        close_gate(0, 3, gate_tile("P03", "gate03"))
        open_gate(1, 3, 4)
        close_gate(1, 3, gate_tile("P03", "gate13", 4096))
        z_tile(0, 2, "B0", -64)
        gated(nc.vector, 0, 2, 2)
        z_tile(1, 2, "B0", 1984)
        gated(nc.vector, 1, 2, 2)
        quant_z_part(0, 2, "v1")
        piece = PACK * P
        first = tile([P, 2 * piece], BF16, "wb1", "zb3a")
        product(nc.vector, first[:, 0:piece], 0, 3, 0, P, 2)
        quant_z_part(1, 2, "v1", 1024)
        product(nc.vector, first[:, piece:], 1, 3, 0, P, 2)
        second = [tile([P, piece], BF16, "wb1", "zb3b%d" % b, 2048 + 1024 * b) for b in range(2)]
        product(nc.vector, second[0][:], 0, 3, P, CHUNK, 2)
        codes, scales = quantise("za", "v1", first[:], 2048)
        for b in range(2):
            z_codes[b, M - CHUNK] = codes[:, P * b : P * (b + 1)]
            z_sc[b, M - CHUNK] = scales[:, P * b : P * (b + 1)]
        product(nc.vector, second[1][:], 1, 3, P, CHUNK, 2)
        for b in range(2):
            codes, scales = quantise("zb%d" % b, "v1", second[b][:], 3072 + 512 * b)
            z_codes[b, M - P] = codes[:]
            z_sc[b, M - P] = scales[:]
        scores(1, 0, (nc.scalar.copy, nc.scalar.copy), tile([P, PACK * CHUNK], F32, "P00", "staged1", 4096)[:])
        scores(2, 2, (nc.scalar.copy, nc.scalar.copy), tile([P, PACK * CHUNK], F32, "P01", "staged2")[:])
        staged = tile([P, PACK * CHUNK], F32, "P01", "staged3", 4096)
        piece_scores(M - CHUNK, (6, 7), (nc.scalar.copy, nc.scalar.copy), staged[:, 0:BANK])
        piece_scores(M - P, (4, 5, 0, 1), (nc.scalar.copy, nc.vector.tensor_copy) * 2, staged[:, BANK:])
